import numpy as np
import ml_dtypes


def mxq(x, axis, fmt="e4m3"):
    dtype, down = {"e4m3": (ml_dtypes.float8_e4m3fn, 7), "e5m2": (ml_dtypes.float8_e5m2, 14)}[fmt]
    v = np.moveaxis(np.asarray(x, np.float32).astype(ml_dtypes.bfloat16).astype(np.float64), axis, -1)
    blocks = v.reshape(v.shape[:-1] + (-1, 32))
    amax = np.abs(blocks).max(-1, keepdims=True)
    byte = np.maximum(np.where(amax > 0, np.frexp(amax)[1] - 1 + 127, 0) - down, 1)
    scale = np.exp2(byte - 127.0)
    codes = (blocks / scale).astype(np.float32).astype(dtype).astype(np.float64)
    return np.moveaxis((codes * scale).reshape(v.shape), -1, axis)


WIDE = False


def mx_kscale(k):
    if not WIDE:
        return np.ones(k)
    levels = np.array([10, -10, 5, -5, 0])
    if k % 512:
        return np.exp2(np.random.permutation(np.resize(levels, k // 32))).repeat(32)
    a = np.empty((k // 512, 16))
    for p in range(k // 512):
        a[p, :8] = np.random.permutation(np.resize(levels, 8))
        for g in range(8):
            far = levels[np.abs(levels - a[p, g]) >= 10]
            a[p, g + 8] = far[np.random.randint(len(far))]
    return np.exp2(a.ravel()).repeat(32)


def f64(x):
    return np.asarray(x).astype(np.float64)


def striped8(idx):
    return np.concatenate([x.reshape(-1, 16).T for x in idx]).astype(np.uint16)


def runs(offs, k):
    lists = np.stack([offs[16 * r : 16 * r + 16].T.reshape(-1) for r in range(8)]).astype(np.int64)
    return lists[np.arange(k) % 512 // 64]


def pack_weight(w):
    k, n = w.shape
    w = f64(np.asarray(w, np.float32).astype(ml_dtypes.bfloat16)).reshape(k // 32, 32, n)
    amax = np.abs(w).max(1)
    byte = np.clip(np.where(amax > 0, np.frexp(amax)[1] - 1 + 127 - 7, 1), 1, 254)
    scaled = (w * np.exp2(127.0 - byte)[:, None, :]).reshape(k, n).astype(np.float32)
    words = np.ascontiguousarray(scaled.reshape(k // 512, 128, 4, n).transpose(0, 1, 3, 2)).astype(ml_dtypes.float8_e4m3fn).view(np.uint8)
    return words, np.ascontiguousarray(byte.astype(np.uint8).reshape(k // 512, 16, n))


def unpack_weight(words, scales):
    g, p, n, _ = words.shape
    vals = np.ascontiguousarray(words).view(ml_dtypes.float8_e4m3fn).astype(np.float64) * np.repeat(np.exp2(scales.astype(np.float64) - 127.0), 8, axis=1)[..., None]
    return vals.transpose(0, 1, 3, 2).reshape(g * 512, n)


def relu(v):
    return np.maximum(v, 0.0)


K, T, S, N, H, U = 512, 2048, 512, 512, 512, 512


def setup_inputs():
    n = np.random.standard_normal
    s = mx_kscale(K)[:, None]
    u = mx_kscale(H)
    packed_xT = pack_weight(n((K, T)) * s)
    return {
        "x_words": packed_xT[0],
        "x_scales": packed_xT[1],
        "w1": (n((K, H)) / np.sqrt(K) / s * u).astype(np.float32),
        "b1": (0.5 * n((H, 1)) * u[:, None]).astype(np.float32),
        "w2": (n((H, N)) / np.sqrt(H) / u[:, None]).astype(np.float32),
        "scl": np.random.uniform(0.5, 1.5, (N, U)).astype(np.float32),
        "shf": n((N, U)).astype(np.float32),
        "offs": striped8(np.random.randint(0, T, (8, S))),
        "rg": striped8(np.random.randint(0, U, (8, S))),
    }


def reference(x_words, x_scales, w1, b1, w2, scl, shf, offs, rg):
    xq = unpack_weight(x_words, x_scales)[np.arange(K)[:, None], runs(offs, K)]
    h = relu((mxq(f64(w1), 0, "e4m3").T @ xq) + f64(b1))
    y = mxq(f64(w2), 0, "e4m3").T @ mxq(h, 0, "e4m3")
    return y * (f64(scl)[np.arange(N)[:, None], runs(rg, N)]) + f64(shf)[np.arange(N)[:, None], runs(rg, N)]

@@ -1,0 +1,180 @@
+from contextlib import ExitStack
+
+import concourse.mybir as mybir
+
+K, T, S, N, H, U = 512, 2048, 512, 512, 512, 512
+FLOPS = 2 * K * H * S + 2 * H * N * S
+
+F32 = mybir.dt.float32
+BF16 = mybir.dt.bfloat16
+I32 = mybir.dt.int32
+U32 = mybir.dt.uint32
+U16 = mybir.dt.uint16
+U8 = mybir.dt.uint8
+FP8X4 = mybir.dt.float8_e4m3fn_x4
+MULT = mybir.AluOpType.mult
+ADD = mybir.AluOpType.add
+RELU = mybir.ActivationFunctionType.Relu
+
+P = 128
+PACK = 4
+GROUP = 16
+CHUNKS = ((0, 256), (256, 512))
+W1_VECTOR_COLS = 88
+W2_VECTOR_COLS = 88
+TABLE_BYTES = U * 4
+
+
+def cast_weight(nc, raw, grouped, split):
+    dst = grouped[:].rearrange("p (t m j) -> p m t j", t=PACK, j=PACK)
+    src = raw[:].rearrange("p j (m t) -> p m t j", t=PACK)
+    nc.vector.tensor_copy(out=dst[:, 0:split], in_=src[:, 0:split])
+    nc.scalar.copy(out=dst[:, split:P], in_=src[:, split:P])
+
+
+def tile_picked_decode2_relu_p_kernel(tc, x_words, x_scales, w1, b1, w2, scl, shf, offs, rg, out):
+    nc = tc.nc
+    with ExitStack() as ctx:
+        lists = ctx.enter_context(tc.tile_pool(name="lists", bufs=1))
+        shared = ctx.enter_context(tc.tile_pool(name="shared", bufs=1))
+        keep = ctx.enter_context(tc.tile_pool(name="keep", bufs=1))
+        psum = ctx.enter_context(tc.psum_pool(name="psum", bufs=8))
+
+        offs_sb = lists.tile([P, S // GROUP], U16, name="offs_sb")
+        rg_sb = lists.tile([P, S // GROUP], U16, name="rg_sb")
+        nc.sync.dma_start(offs_sb[:], offs)
+
+        warm = keep.tile([P, 8], F32, name="warm")
+        nc.gpsimd.memset(warm[:], 0.0)
+        warm_out = keep.tile([P, 8], F32, name="warm_out")
+        nc.scalar.activation(out=warm_out[:], in_=warm[:], func=RELU)
+
+        scale_table = keep.tile([P, T], U8, name="scale_table", align_bytes=64)
+        nc.vector.memset(scale_table[:].bitcast(I32), 0)
+        scale_rows = x_scales[0].bitcast(I32)
+        for e in range(2):
+            nc.scalar.dma_start(scale_table[:].bitcast(I32)[e:P:GROUP, :], scale_rows[e:16:2, :])
+
+        w1_raw = shared.tile([P, PACK, H], F32, name="w1_raw", offset=0)
+        nc.sync.dma_start(w1_raw[:], w1.rearrange("(p j) c -> p j c", j=PACK))
+        word_table = shared.tile([P, T], I32, name="word_table", offset=4 * TABLE_BYTES)
+        nc.sync.dma_start(word_table[:], x_words[0].rearrange("p n t -> p (n t)").bitcast(I32))
+        bias = keep.tile([P, PACK], F32, name="bias")
+        nc.scalar.dma_start(bias[:], b1.rearrange("(p t) o -> p (t o)", t=PACK))
+        nc.sync.dma_start(rg_sb[:], rg)
+        w2_raw = keep.tile([P, PACK, N], F32, name="w2_raw")
+        nc.sync.dma_start(w2_raw[:], w2.rearrange("(p j) c -> p j c", j=PACK))
+
+        picked_scales = keep.tile([P, S], U8, name="picked_scales", align_bytes=64)
+        nc.vector.tensor_copy(out=picked_scales[:], in_=scale_table[:].indirect(offs_sb[:]))
+        x_plane = keep.tile([P, S], U8, name="x_plane", align_bytes=64)
+        nc.vector.tensor_copy(out=x_plane[:].bitcast(I32), in_=picked_scales[:].bitcast(I32))
+        for e in range(2):
+            nc.scalar.dma_start(x_plane[:].bitcast(I32)[2 + e : P : 32, :], picked_scales[:].bitcast(I32)[GROUP + e : P : 32, :])
+
+        w1_grouped = keep.tile([P, PACK * H], BF16, name="w1_grouped", align_bytes=64)
+        cast_weight(nc, w1_raw, w1_grouped, W1_VECTOR_COLS)
+        w1_codes = keep.tile([P, H], U32, name="w1_codes", align_bytes=64)
+        w1_plane = keep.tile([P, H], U8, name="w1_plane", align_bytes=64)
+        nc.vector.quantize_mx(out=w1_codes[:].bitcast(FP8X4), scales=w1_plane[:], in_=w1_grouped[:])
+
+        x_codes = []
+        for c, (lo, hi) in enumerate(CHUNKS):
+            codes = keep.tile([P, hi - lo], U32, name="x_codes%d" % c, align_bytes=64)
+            nc.vector.tensor_copy(out=codes[:], in_=word_table[:].bitcast(U32).indirect(offs_sb[:, lo // GROUP : hi // GROUP]))
+            x_codes.append(codes)
+
+        scl_rows = scl.rearrange("(p t) u -> t p u", t=PACK)
+        shf_rows = shf.rearrange("(p t) u -> t p u", t=PACK)
+        out_rows = out.rearrange("(p t) s -> t p s", t=PACK)
+        scl_tables, shf_tables = [], []
+        for t in range(PACK):
+            scl_t = shared.tile([P, U], F32, name="scl%d" % t, offset=2 * t * TABLE_BYTES)
+            nc.sync.dma_start(scl_t[:], scl_rows[t])
+            shf_t = shared.tile([P, U], F32, name="shf%d" % t, offset=(2 * t + 1) * TABLE_BYTES)
+            nc.sync.dma_start(shf_t[:], shf_rows[t])
+            scl_tables.append(scl_t)
+            shf_tables.append(shf_t)
+
+        w2_grouped = keep.tile([P, PACK * N], BF16, name="w2_grouped", align_bytes=64)
+        w2_codes = keep.tile([P, N], U32, name="w2_codes", align_bytes=64)
+        w2_plane = keep.tile([P, N], U8, name="w2_plane", align_bytes=64)
+
+        def first_layer(c):
+            lo, hi = CHUNKS[c]
+            h_rows = keep.tile([P, PACK, hi - lo], BF16, name="h_rows%d" % c, align_bytes=64)
+            for t in range(PACK):
+                acc = psum.tile([P, hi - lo], F32, name="acc", tag="bank")
+                nc.tensor.matmul_mx(
+                    out=acc[:],
+                    lhsT=w1_codes[:, t * P : (t + 1) * P].bitcast(FP8X4),
+                    lhsT_scale=w1_plane[:, t * P : (t + 1) * P],
+                    rhs=x_codes[c][:].bitcast(FP8X4),
+                    rhs_scale=x_plane[:, lo:hi],
+                    start=True,
+                    stop=True,
+                )
+                nc.scalar.activation(out=h_rows[:, t, :], in_=acc[:], func=RELU, bias=bias[:, t : t + 1])
+            return h_rows
+
+        def quantize_hidden(c, h_rows, copy):
+            lo, hi = CHUNKS[c]
+            h_grouped = keep.tile([P, hi - lo, PACK], BF16, name="h_grouped%d" % c, align_bytes=64, tag="handover" if c == 1 else "h_grouped")
+            copy(
+                out=h_grouped[:].rearrange("p (c i) t -> p c t i", i=4),
+                in_=h_rows[:].rearrange("p t (c i) -> p c t i", i=4),
+            )
+            h_codes = keep.tile([P, hi - lo], U32, name="h_codes%d" % c, align_bytes=64, tag="handover" if c == 0 else "h_codes")
+            h_plane = keep.tile([P, hi - lo], U8, name="h_plane%d" % c, align_bytes=64)
+            nc.vector.quantize_mx(out=h_codes[:].bitcast(FP8X4), scales=h_plane[:], in_=h_grouped[:].rearrange("p n t -> p (n t)"))
+            return h_codes, h_plane
+
+        def second_layer(c, h_codes, h_plane):
+            lo, hi = CHUNKS[c]
+            ys = []
+            for t in range(PACK):
+                acc = psum.tile([P, hi - lo], F32, name="acc", tag="bank")
+                nc.tensor.matmul_mx(
+                    out=acc[:],
+                    lhsT=w2_codes[:, t * P : (t + 1) * P].bitcast(FP8X4),
+                    lhsT_scale=w2_plane[:, t * P : (t + 1) * P],
+                    rhs=h_codes[:].bitcast(FP8X4),
+                    rhs_scale=h_plane[:],
+                    start=True,
+                    stop=True,
+                )
+                y = keep.tile([P, hi - lo], F32, name="y%d_%d" % (c, t))
+                nc.scalar.copy(out=y[:], in_=acc[:])
+                ys.append(y)
+            return ys
+
+        def scale_and_shift(c, ys):
+            lo, hi = CHUNKS[c]
+            ranges = rg_sb[:, lo // GROUP : hi // GROUP]
+            scaled = []
+            for step in range(PACK + 1):
+                if step < PACK:
+                    z = keep.tile([P, hi - lo], F32, name="z%d_%d" % (c, step), align_bytes=64, tag="handover" if (c, step) == (0, 3) else "z%d_%d" % (c, step))
+                    nc.vector.tensor_tensor(z[:], scl_tables[step][:].indirect(ranges), ys[step][:], MULT)
+                    scaled.append(z)
+                if step > 0:
+                    t = step - 1
+                    res = keep.tile([P, hi - lo], F32, name="res%d_%d" % (c, t))
+                    nc.vector.tensor_tensor(res[:], shf_tables[t][:].indirect(ranges), scaled[t][:], ADD)
+                    nc.sync.dma_start(out_rows[t][:, lo:hi], res[:])
+
+        h_rows_a = first_layer(0)
+        hidden_a = quantize_hidden(0, h_rows_a, nc.vector.tensor_copy)
+        cast_weight(nc, w2_raw, w2_grouped, W2_VECTOR_COLS)
+        for t in range(PACK):
+            nc.vector.quantize_mx(
+                out=w2_codes[:, t * P : (t + 1) * P].bitcast(FP8X4),
+                scales=w2_plane[:, t * P : (t + 1) * P],
+                in_=w2_grouped[:, t * PACK * P : (t + 1) * PACK * P],
+            )
+        h_rows_b = first_layer(1)
+        ys_a = second_layer(0, *hidden_a)
+        hidden_b = quantize_hidden(1, h_rows_b, nc.scalar.copy)
+        scale_and_shift(0, ys_a)
+        ys_b = second_layer(1, *hidden_b)
+        scale_and_shift(1, ys_b)

@@ -19,17 +19,11 @@ RELU = mybir.ActivationFunctionType.Relu
 P = 128
 PACK = 4
 GROUP = 16
-CHUNKS = ((0, 256), (256, 512))
-W1_VECTOR_COLS = 88
-W2_VECTOR_COLS = 88
+HALF = S // 2
+CHUNKS = ((0, 128), (128, 256), (256, 512))
+W1_VECTOR_COLS = 48
 TABLE_BYTES = U * 4
-
-
-def cast_weight(nc, raw, grouped, split):
-    dst = grouped[:].rearrange("p (t m j) -> p m t j", t=PACK, j=PACK)
-    src = raw[:].rearrange("p j (m t) -> p m t j", t=PACK)
-    nc.vector.tensor_copy(out=dst[:, 0:split], in_=src[:, 0:split])
-    nc.scalar.copy(out=dst[:, split:P], in_=src[:, split:P])
+EARLY = 2
 
 
 def tile_picked_decode2_relu_p_kernel(tc, x_words, x_scales, w1, b1, w2, scl, shf, offs, rg, out):
@@ -38,78 +32,102 @@ def tile_picked_decode2_relu_p_kernel(tc, x_words, x_scales, w1, b1, w2, scl, sh
         lists = ctx.enter_context(tc.tile_pool(name="lists", bufs=1))
         shared = ctx.enter_context(tc.tile_pool(name="shared", bufs=1))
         keep = ctx.enter_context(tc.tile_pool(name="keep", bufs=1))
-        psum = ctx.enter_context(tc.psum_pool(name="psum", bufs=8))
+        psum = ctx.enter_context(tc.psum_pool(name="psum", bufs=1))
 
-        offs_sb = lists.tile([P, S // GROUP], U16, name="offs_sb")
-        rg_sb = lists.tile([P, S // GROUP], U16, name="rg_sb")
-        nc.sync.dma_start(offs_sb[:], offs)
+        scl_rows = scl.rearrange("(p t) u -> t p u", t=PACK)
+        shf_rows = shf.rearrange("(p t) u -> t p u", t=PACK)
+        out_rows = out.rearrange("(p t) s -> t p s", t=PACK)
+
+        scale_table = shared.tile([P, T], U8, name="scale_table", align_bytes=64, offset=9 * TABLE_BYTES + TABLE_BYTES // 2)
+        nc.vector.memset(scale_table[:].bitcast(I32), 0)
+        scale_rows = x_scales[0].bitcast(I32)
+        for e in range(2):
+            nc.sync.dma_start(scale_table[:].bitcast(I32)[e:P:GROUP, :], scale_rows[e:16:2, :])
+        x_plane = keep.tile([P, S], U8, name="x_plane", align_bytes=64)
+        nc.gpsimd.memset(x_plane[:].bitcast(I32), 0)
 
         warm = keep.tile([P, 8], F32, name="warm")
         nc.gpsimd.memset(warm[:], 0.0)
         warm_out = keep.tile([P, 8], F32, name="warm_out")
         nc.scalar.activation(out=warm_out[:], in_=warm[:], func=RELU)
 
-        scale_table = keep.tile([P, T], U8, name="scale_table", align_bytes=64)
-        nc.vector.memset(scale_table[:].bitcast(I32), 0)
-        scale_rows = x_scales[0].bitcast(I32)
-        for e in range(2):
-            nc.scalar.dma_start(scale_table[:].bitcast(I32)[e:P:GROUP, :], scale_rows[e:16:2, :])
+        offs_sb = lists.tile([P, S // GROUP], U16, name="offs_sb")
+        rg_sb = lists.tile([P, S // GROUP], U16, name="rg_sb")
+        scl_tables = [keep.tile([P, U], F32, name="scl%d" % t) for t in range(EARLY)]
+        nc.sync.dma_start(rg_sb[:], rg)
+        nc.sync.dma_start(scl_tables[0][:], scl_rows[0])
+        nc.sync.dma_start(offs_sb[:], offs)
+        nc.sync.dma_start(scl_tables[1][:], scl_rows[1])
 
         w1_raw = shared.tile([P, PACK, H], F32, name="w1_raw", offset=0)
         nc.sync.dma_start(w1_raw[:], w1.rearrange("(p j) c -> p j c", j=PACK))
         word_table = shared.tile([P, T], I32, name="word_table", offset=4 * TABLE_BYTES)
         nc.sync.dma_start(word_table[:], x_words[0].rearrange("p n t -> p (n t)").bitcast(I32))
         bias = keep.tile([P, PACK], F32, name="bias")
-        nc.scalar.dma_start(bias[:], b1.rearrange("(p t) o -> p (t o)", t=PACK))
-        nc.sync.dma_start(rg_sb[:], rg)
-        w2_raw = keep.tile([P, PACK, N], F32, name="w2_raw")
-        nc.sync.dma_start(w2_raw[:], w2.rearrange("(p j) c -> p j c", j=PACK))
+        nc.sync.dma_start(bias[:], b1.rearrange("(p t) o -> p (t o)", t=PACK))
 
         picked_scales = keep.tile([P, S], U8, name="picked_scales", align_bytes=64)
         nc.vector.tensor_copy(out=picked_scales[:], in_=scale_table[:].indirect(offs_sb[:]))
-        x_plane = keep.tile([P, S], U8, name="x_plane", align_bytes=64)
-        nc.vector.tensor_copy(out=x_plane[:].bitcast(I32), in_=picked_scales[:].bitcast(I32))
-        for e in range(2):
-            nc.scalar.dma_start(x_plane[:].bitcast(I32)[2 + e : P : 32, :], picked_scales[:].bitcast(I32)[GROUP + e : P : 32, :])
+        for r in range(4):
+            src = GROUP * (r // 2) + r % 2
+            nc.sync.dma_start(x_plane[:].bitcast(I32)[r:P:32, :], picked_scales[:].bitcast(I32)[src:P:32, :])
+        w2_rows = w2.rearrange("(p j) c -> p j c", j=PACK)
+        w2_raw = []
+        for u in range(2):
+            part = shared.tile([P, PACK, N // 2], F32, name="w2_raw%d" % u, offset=(8 + 2 * u) * TABLE_BYTES)
+            nc.sync.dma_start(part[:], w2_rows[:, :, u * N // 2 : (u + 1) * N // 2])
+            w2_raw.append(part)
+
+        picked_scl = []
+        for t in range(EARLY):
+            picked = keep.tile([P, S], F32, name="picked_scl%d" % t)
+            for lo in (0, HALF):
+                nc.vector.tensor_copy(out=picked[:, lo : lo + HALF], in_=scl_tables[t][:].indirect(rg_sb[:, lo // GROUP : (lo + HALF) // GROUP]))
+            picked_scl.append(picked)
 
         w1_grouped = keep.tile([P, PACK * H], BF16, name="w1_grouped", align_bytes=64)
-        cast_weight(nc, w1_raw, w1_grouped, W1_VECTOR_COLS)
+        dst = w1_grouped[:].rearrange("p (t m j) -> p m t j", t=PACK, j=PACK)
+        src = w1_raw[:].rearrange("p j (m t) -> p m t j", t=PACK)
+        nc.vector.tensor_copy(out=dst[:, 0:W1_VECTOR_COLS], in_=src[:, 0:W1_VECTOR_COLS])
+        nc.scalar.copy(out=dst[:, W1_VECTOR_COLS:P], in_=src[:, W1_VECTOR_COLS:P])
         w1_codes = keep.tile([P, H], U32, name="w1_codes", align_bytes=64)
         w1_plane = keep.tile([P, H], U8, name="w1_plane", align_bytes=64)
         nc.vector.quantize_mx(out=w1_codes[:].bitcast(FP8X4), scales=w1_plane[:], in_=w1_grouped[:])
 
         x_codes = []
-        for c, (lo, hi) in enumerate(CHUNKS):
-            codes = keep.tile([P, hi - lo], U32, name="x_codes%d" % c, align_bytes=64)
-            nc.vector.tensor_copy(out=codes[:], in_=word_table[:].bitcast(U32).indirect(offs_sb[:, lo // GROUP : hi // GROUP]))
+        for lo in (0, HALF):
+            codes = keep.tile([P, HALF], U32, name="x_codes%d" % lo, align_bytes=64)
+            nc.vector.tensor_copy(out=codes[:], in_=word_table[:].bitcast(U32).indirect(offs_sb[:, lo // GROUP : (lo + HALF) // GROUP]))
             x_codes.append(codes)
 
-        scl_rows = scl.rearrange("(p t) u -> t p u", t=PACK)
-        shf_rows = shf.rearrange("(p t) u -> t p u", t=PACK)
-        out_rows = out.rearrange("(p t) s -> t p s", t=PACK)
-        scl_tables, shf_tables = [], []
+        shf_tables = []
+        slot = 0
         for t in range(PACK):
-            scl_t = shared.tile([P, U], F32, name="scl%d" % t, offset=2 * t * TABLE_BYTES)
-            nc.sync.dma_start(scl_t[:], scl_rows[t])
-            shf_t = shared.tile([P, U], F32, name="shf%d" % t, offset=(2 * t + 1) * TABLE_BYTES)
+            if t >= EARLY:
+                scl_t = shared.tile([P, U], F32, name="scl%d" % t, offset=slot * TABLE_BYTES)
+                nc.sync.dma_start(scl_t[:], scl_rows[t])
+                scl_tables.append(scl_t)
+                slot = slot + 1
+            shf_t = shared.tile([P, U], F32, name="shf%d" % t, offset=slot * TABLE_BYTES)
             nc.sync.dma_start(shf_t[:], shf_rows[t])
-            scl_tables.append(scl_t)
             shf_tables.append(shf_t)
+            slot = slot + 1
 
-        w2_grouped = keep.tile([P, PACK * N], BF16, name="w2_grouped", align_bytes=64)
+        w2_grouped = keep.tile([P, PACK * N], BF16, name="w2_grouped", align_bytes=64, tag="w2_stage")
         w2_codes = keep.tile([P, N], U32, name="w2_codes", align_bytes=64)
         w2_plane = keep.tile([P, N], U8, name="w2_plane", align_bytes=64)
 
-        def first_layer(c):
+        def first_layer(c, banks):
             lo, hi = CHUNKS[c]
+            half = lo // HALF
             h_rows = keep.tile([P, PACK, hi - lo], BF16, name="h_rows%d" % c, align_bytes=64)
-            for t in range(PACK):
-                acc = psum.tile([P, hi - lo], F32, name="acc", tag="bank")
+            for t, bank in enumerate(banks):
+                acc = psum.tile([P, hi - lo], F32, name="acc", tag="bank%d" % bank)
                 nc.tensor.matmul_mx(
                     out=acc[:],
                     lhsT=w1_codes[:, t * P : (t + 1) * P].bitcast(FP8X4),
                     lhsT_scale=w1_plane[:, t * P : (t + 1) * P],
-                    rhs=x_codes[c][:].bitcast(FP8X4),
+                    rhs=x_codes[half][:, lo - half * HALF : hi - half * HALF].bitcast(FP8X4),
                     rhs_scale=x_plane[:, lo:hi],
                     start=True,
                     stop=True,
@@ -117,64 +135,105 @@ def tile_picked_decode2_relu_p_kernel(tc, x_words, x_scales, w1, b1, w2, scl, sh
                 nc.scalar.activation(out=h_rows[:, t, :], in_=acc[:], func=RELU, bias=bias[:, t : t + 1])
             return h_rows
 
-        def quantize_hidden(c, h_rows, copy):
-            lo, hi = CHUNKS[c]
-            h_grouped = keep.tile([P, hi - lo, PACK], BF16, name="h_grouped%d" % c, align_bytes=64, tag="handover" if c == 1 else "h_grouped")
+        def interleave(h_grouped, h_rows, copy):
             copy(
                 out=h_grouped[:].rearrange("p (c i) t -> p c t i", i=4),
                 in_=h_rows[:].rearrange("p t (c i) -> p c t i", i=4),
             )
-            h_codes = keep.tile([P, hi - lo], U32, name="h_codes%d" % c, align_bytes=64, tag="handover" if c == 0 else "h_codes")
-            h_plane = keep.tile([P, hi - lo], U8, name="h_plane%d" % c, align_bytes=64)
+
+        def quantize_hidden(h_grouped, codes_tag, plane_tag):
+            width = h_grouped.shape[1]
+            h_codes = keep.tile([P, width], U32, name="h_codes", align_bytes=64, tag=codes_tag)
+            h_plane = keep.tile([P, width], U8, name="h_plane", align_bytes=64, tag=plane_tag)
             nc.vector.quantize_mx(out=h_codes[:].bitcast(FP8X4), scales=h_plane[:], in_=h_grouped[:].rearrange("p n t -> p (n t)"))
             return h_codes, h_plane
 
-        def second_layer(c, h_codes, h_plane):
-            lo, hi = CHUNKS[c]
-            ys = []
-            for t in range(PACK):
-                acc = psum.tile([P, hi - lo], F32, name="acc", tag="bank")
-                nc.tensor.matmul_mx(
-                    out=acc[:],
-                    lhsT=w2_codes[:, t * P : (t + 1) * P].bitcast(FP8X4),
-                    lhsT_scale=w2_plane[:, t * P : (t + 1) * P],
-                    rhs=h_codes[:].bitcast(FP8X4),
-                    rhs_scale=h_plane[:],
-                    start=True,
-                    stop=True,
-                )
-                y = keep.tile([P, hi - lo], F32, name="y%d_%d" % (c, t))
-                nc.scalar.copy(out=y[:], in_=acc[:])
-                ys.append(y)
-            return ys
+        def product(acc, t, hidden):
+            nc.tensor.matmul_mx(
+                out=acc,
+                lhsT=w2_codes[:, t * P : (t + 1) * P].bitcast(FP8X4),
+                lhsT_scale=w2_plane[:, t * P : (t + 1) * P],
+                rhs=hidden[0][:].bitcast(FP8X4),
+                rhs_scale=hidden[1][:],
+                start=True,
+                stop=True,
+            )
 
-        def scale_and_shift(c, ys):
-            lo, hi = CHUNKS[c]
-            ranges = rg_sb[:, lo // GROUP : hi // GROUP]
-            scaled = []
-            for step in range(PACK + 1):
-                if step < PACK:
-                    z = keep.tile([P, hi - lo], F32, name="z%d_%d" % (c, step), align_bytes=64, tag="handover" if (c, step) == (0, 3) else "z%d_%d" % (c, step))
-                    nc.vector.tensor_tensor(z[:], scl_tables[step][:].indirect(ranges), ys[step][:], MULT)
-                    scaled.append(z)
-                if step > 0:
-                    t = step - 1
-                    res = keep.tile([P, hi - lo], F32, name="res%d_%d" % (c, t))
-                    nc.vector.tensor_tensor(res[:], shf_tables[t][:].indirect(ranges), scaled[t][:], ADD)
-                    nc.sync.dma_start(out_rows[t][:, lo:hi], res[:])
+        def cast_w2(u):
+            dst = w2_grouped[:].rearrange("p (t m j) -> p m t j", t=PACK, j=PACK)
+            nc.vector.tensor_copy(out=dst[:, 64 * u : 64 * (u + 1)], in_=w2_raw[u][:].rearrange("p j (m t) -> p m t j", t=PACK))
 
-        h_rows_a = first_layer(0)
-        hidden_a = quantize_hidden(0, h_rows_a, nc.vector.tensor_copy)
-        cast_weight(nc, w2_raw, w2_grouped, W2_VECTOR_COLS)
+        h_rows_a = first_layer(0, (0, 1, 2, 3))
+        h_rows_b = first_layer(1, (4, 5, 6, 7))
+        grouped_b = keep.tile([P, 128, PACK], BF16, name="grouped_b", align_bytes=64)
+        interleave(grouped_b, h_rows_b, nc.scalar.copy)
+        h_rows_c = first_layer(2, (0, 1, 2, 3))
+        cast_w2(0)
+        grouped_a = shared.tile([P, 128, PACK], BF16, name="grouped_a", offset=8 * TABLE_BYTES)
+        interleave(grouped_a, h_rows_a, nc.vector.tensor_copy)
+        hidden_a = quantize_hidden(grouped_a, "codes_a", "plane_a")
+        cast_w2(1)
         for t in range(PACK):
             nc.vector.quantize_mx(
                 out=w2_codes[:, t * P : (t + 1) * P].bitcast(FP8X4),
                 scales=w2_plane[:, t * P : (t + 1) * P],
                 in_=w2_grouped[:, t * PACK * P : (t + 1) * PACK * P],
             )
-        h_rows_b = first_layer(1)
-        ys_a = second_layer(0, *hidden_a)
-        hidden_b = quantize_hidden(1, h_rows_b, nc.scalar.copy)
-        scale_and_shift(0, ys_a)
-        ys_b = second_layer(1, *hidden_b)
-        scale_and_shift(1, ys_b)
+        hidden_b = quantize_hidden(grouped_b, "w2_stage", "handover")
+
+        ys = {}
+        for c, hidden in ((0, hidden_a), (1, hidden_b)):
+            for t in range(EARLY):
+                acc = psum.tile([P, 128], F32, name="acc", tag="bank%d" % (4 + 2 * c + t))
+                product(acc[:], t, hidden)
+                ys[t, CHUNKS[c][0]] = acc
+        for t in range(EARLY, PACK):
+            acc = psum.tile([P, HALF], F32, name="acc", tag="bank%d" % (t - EARLY))
+            product(acc[:, 0:128], t, hidden_a)
+            product(acc[:, 128:256], t, hidden_b)
+            y = keep.tile([P, HALF], F32, name="y0_%d" % t)
+            nc.scalar.copy(out=y[:], in_=acc[:])
+            ys[t, 0] = y
+        grouped_c = keep.tile([P, HALF, PACK], BF16, name="grouped_c", align_bytes=64, tag="handover")
+        interleave(grouped_c, h_rows_c, nc.scalar.copy)
+        hidden_c = quantize_hidden(grouped_c, "codes_c", "plane_c")
+
+        def last_products():
+            for t in range(PACK):
+                acc = psum.tile([P, HALF], F32, name="acc", tag="bank%d" % (2 + t))
+                product(acc[:], t, hidden_c)
+                if t < EARLY:
+                    ys[t, HALF] = acc
+                else:
+                    y = keep.tile([P, HALF], F32, name="y1_%d" % t)
+                    nc.scalar.copy(out=y[:], in_=acc[:])
+                    ys[t, HALF] = y
+
+        zs, results = {}, {}
+
+        def scale(t, lo, hi):
+            z = keep.tile([P, hi - lo], F32, name="z", align_bytes=64, tag="handover" if (t, lo) == (3, 0) else "z%d_%d" % (t, lo))
+            if t < EARLY:
+                nc.vector.tensor_tensor(z[:], ys[t, lo][:], picked_scl[t][:, lo:hi], MULT)
+            else:
+                nc.vector.tensor_tensor(z[:], scl_tables[t][:].indirect(rg_sb[:, lo // GROUP : hi // GROUP]), ys[t, lo][:], MULT)
+            zs[t, lo] = z
+
+        def shift(t, lo, hi):
+            half = lo // HALF
+            if (half, t) not in results:
+                results[half, t] = keep.tile([P, HALF], F32, name="res%d_%d" % (half, t))
+            cols = slice(lo - half * HALF, hi - half * HALF)
+            nc.vector.tensor_tensor(results[half, t][:, cols], shf_tables[t][:].indirect(rg_sb[:, lo // GROUP : hi // GROUP]), zs[t, lo][:], ADD)
+            if hi % HALF == 0:
+                nc.sync.dma_start(out_rows[t][:, half * HALF : hi], results[half, t][:])
+
+        steps = [(0, 0, 128), (1, 0, 128), (0, 128, 256), (1, 128, 256), (2, 0, 256), (3, 0, 256)]
+        steps = steps + [(t, 256, 512) for t in range(PACK)]
+        for i in range(len(steps) + 1):
+            if i == 6:
+                last_products()
+            if i < len(steps):
+                scale(*steps[i])
+            if i > 0:
+                shift(*steps[i - 1])

@@ -21,7 +21,7 @@ PACK = 4
 GROUP = 16
 HALF = S // 2
 CHUNKS = ((0, 128), (128, 256), (256, 512))
-W1_VECTOR_COLS = 48
+W1_VECTOR_COLS = 96
 TABLE_BYTES = U * 4
 EARLY = 2
 
@@ -86,10 +86,11 @@ def tile_picked_decode2_relu_p_kernel(tc, x_words, x_scales, w1, b1, w2, scl, sh
             picked_scl.append(picked)
 
         w1_grouped = keep.tile([P, PACK * H], BF16, name="w1_grouped", align_bytes=64)
-        dst = w1_grouped[:].rearrange("p (t m j) -> p m t j", t=PACK, j=PACK)
-        src = w1_raw[:].rearrange("p j (m t) -> p m t j", t=PACK)
-        nc.vector.tensor_copy(out=dst[:, 0:W1_VECTOR_COLS], in_=src[:, 0:W1_VECTOR_COLS])
-        nc.scalar.copy(out=dst[:, W1_VECTOR_COLS:P], in_=src[:, W1_VECTOR_COLS:P])
+        dst = w1_grouped[:].rearrange("p (t m j) -> p m j t", t=PACK, j=PACK)
+        src = w1_raw[:].rearrange("p j (m t) -> p m j t", t=PACK)
+        nc.vector.tensor_copy(out=dst[:, 0:W1_VECTOR_COLS, :, 0:2], in_=src[:, 0:W1_VECTOR_COLS, :, 0:2])
+        nc.scalar.copy(out=dst[:, :, :, 2:4], in_=src[:, :, :, 2:4])
+        nc.scalar.copy(out=dst[:, W1_VECTOR_COLS:P, :, 0:2], in_=src[:, W1_VECTOR_COLS:P, :, 0:2])
         w1_codes = keep.tile([P, H], U32, name="w1_codes", align_bytes=64)
         w1_plane = keep.tile([P, H], U8, name="w1_plane", align_bytes=64)
         nc.vector.quantize_mx(out=w1_codes[:].bitcast(FP8X4), scales=w1_plane[:], in_=w1_grouped[:])
@@ -160,8 +161,10 @@ def tile_picked_decode2_relu_p_kernel(tc, x_words, x_scales, w1, b1, w2, scl, sh
             )
 
         def cast_w2(u):
-            dst = w2_grouped[:].rearrange("p (t m j) -> p m t j", t=PACK, j=PACK)
-            nc.vector.tensor_copy(out=dst[:, 64 * u : 64 * (u + 1)], in_=w2_raw[u][:].rearrange("p j (m t) -> p m t j", t=PACK))
+            dst = w2_grouped[:].rearrange("p (t m j) -> p m j t", t=PACK, j=PACK)
+            src = w2_raw[u][:].rearrange("p j (m t) -> p m j t", t=PACK)
+            for pair in (0, 2):
+                nc.vector.tensor_copy(out=dst[:, 64 * u : 64 * (u + 1), :, pair : pair + 2], in_=src[:, :, :, pair : pair + 2])
 
         h_rows_a = first_layer(0, (0, 1, 2, 3))
         h_rows_b = first_layer(1, (4, 5, 6, 7))

@@ -21,7 +21,7 @@ PACK = 4
 GROUP = 16
 HALF = S // 2
 CHUNKS = ((0, 128), (128, 256), (256, 512))
-W1_VECTOR_COLS = 96
+W1_VECTOR_COLS = 32
 TABLE_BYTES = U * 4
 EARLY = 2
 
@@ -46,6 +46,8 @@ def tile_picked_decode2_relu_p_kernel(tc, x_words, x_scales, w1, b1, w2, scl, sh
         x_plane = keep.tile([P, S], U8, name="x_plane", align_bytes=64)
         nc.gpsimd.memset(x_plane[:].bitcast(I32), 0)
 
+        bias = keep.tile([P, PACK], F32, name="bias")
+        nc.scalar.dma_start(bias[:], b1.rearrange("(p t) o -> p (t o)", t=PACK))
         warm = keep.tile([P, 8], F32, name="warm")
         nc.gpsimd.memset(warm[:], 0.0)
         warm_out = keep.tile([P, 8], F32, name="warm_out")
@@ -54,8 +56,8 @@ def tile_picked_decode2_relu_p_kernel(tc, x_words, x_scales, w1, b1, w2, scl, sh
         offs_sb = lists.tile([P, S // GROUP], U16, name="offs_sb")
         rg_sb = lists.tile([P, S // GROUP], U16, name="rg_sb")
         scl_tables = [keep.tile([P, U], F32, name="scl%d" % t) for t in range(EARLY)]
-        nc.sync.dma_start(rg_sb[:], rg)
         nc.sync.dma_start(scl_tables[0][:], scl_rows[0])
+        nc.sync.dma_start(rg_sb[:], rg)
         nc.sync.dma_start(offs_sb[:], offs)
         nc.sync.dma_start(scl_tables[1][:], scl_rows[1])
 
@@ -63,8 +65,6 @@ def tile_picked_decode2_relu_p_kernel(tc, x_words, x_scales, w1, b1, w2, scl, sh
         nc.sync.dma_start(w1_raw[:], w1.rearrange("(p j) c -> p j c", j=PACK))
         word_table = shared.tile([P, T], I32, name="word_table", offset=4 * TABLE_BYTES)
         nc.sync.dma_start(word_table[:], x_words[0].rearrange("p n t -> p (n t)").bitcast(I32))
-        bias = keep.tile([P, PACK], F32, name="bias")
-        nc.sync.dma_start(bias[:], b1.rearrange("(p t) o -> p (t o)", t=PACK))
 
         picked_scales = keep.tile([P, S], U8, name="picked_scales", align_bytes=64)
         nc.vector.tensor_copy(out=picked_scales[:], in_=scale_table[:].indirect(offs_sb[:]))
@@ -88,9 +88,9 @@ def tile_picked_decode2_relu_p_kernel(tc, x_words, x_scales, w1, b1, w2, scl, sh
         w1_grouped = keep.tile([P, PACK * H], BF16, name="w1_grouped", align_bytes=64)
         dst = w1_grouped[:].rearrange("p (t m j) -> p m j t", t=PACK, j=PACK)
         src = w1_raw[:].rearrange("p j (m t) -> p m j t", t=PACK)
-        nc.vector.tensor_copy(out=dst[:, 0:W1_VECTOR_COLS, :, 0:2], in_=src[:, 0:W1_VECTOR_COLS, :, 0:2])
-        nc.scalar.copy(out=dst[:, :, :, 2:4], in_=src[:, :, :, 2:4])
-        nc.scalar.copy(out=dst[:, W1_VECTOR_COLS:P, :, 0:2], in_=src[:, W1_VECTOR_COLS:P, :, 0:2])
+        nc.vector.tensor_copy(out=dst[:, :, :, 0:2], in_=src[:, :, :, 0:2])
+        nc.vector.tensor_copy(out=dst[:, 0:W1_VECTOR_COLS, :, 2:4], in_=src[:, 0:W1_VECTOR_COLS, :, 2:4])
+        nc.scalar.copy(out=dst[:, W1_VECTOR_COLS:P, :, 2:4], in_=src[:, W1_VECTOR_COLS:P, :, 2:4])
         w1_codes = keep.tile([P, H], U32, name="w1_codes", align_bytes=64)
         w1_plane = keep.tile([P, H], U8, name="w1_plane", align_bytes=64)
         nc.vector.quantize_mx(out=w1_codes[:].bitcast(FP8X4), scales=w1_plane[:], in_=w1_grouped[:])
@@ -226,6 +226,12 @@ def tile_picked_decode2_relu_p_kernel(tc, x_words, x_scales, w1, b1, w2, scl, sh
             half = lo // HALF
             if (half, t) not in results:
                 results[half, t] = keep.tile([P, HALF], F32, name="res%d_%d" % (half, t))
+            if (half, t) == (1, PACK - 1):
+                for a in (lo, lo + 128):
+                    cols = slice(a - HALF, a + 128 - HALF)
+                    nc.vector.tensor_tensor(results[half, t][:, cols], shf_tables[t][:].indirect(rg_sb[:, a // GROUP : (a + 128) // GROUP]), zs[t, lo][:, cols], ADD)
+                    nc.sync.dma_start(out_rows[t][:, a : a + 128], results[half, t][:, cols])
+                return
             cols = slice(lo - half * HALF, hi - half * HALF)
             nc.vector.tensor_tensor(results[half, t][:, cols], shf_tables[t][:].indirect(rg_sb[:, lo // GROUP : hi // GROUP]), zs[t, lo][:], ADD)
             if hi % HALF == 0:

@@ -21,9 +21,8 @@ PACK = 4
 GROUP = 16
 HALF = S // 2
 CHUNKS = ((0, 128), (128, 256), (256, 512))
-W1_VECTOR_COLS = 32
+W1_VECTOR_COLS = 64
 TABLE_BYTES = U * 4
-EARLY = 2
 
 
 def tile_picked_decode2_relu_p_kernel(tc, x_words, x_scales, w1, b1, w2, scl, shf, offs, rg, out):
@@ -38,7 +37,7 @@ def tile_picked_decode2_relu_p_kernel(tc, x_words, x_scales, w1, b1, w2, scl, sh
         shf_rows = shf.rearrange("(p t) u -> t p u", t=PACK)
         out_rows = out.rearrange("(p t) s -> t p s", t=PACK)
 
-        scale_table = shared.tile([P, T], U8, name="scale_table", align_bytes=64, offset=9 * TABLE_BYTES + TABLE_BYTES // 2)
+        scale_table = shared.tile([P, T], U8, name="scale_table", align_bytes=64, offset=4 * TABLE_BYTES + TABLE_BYTES // 2)
         nc.vector.memset(scale_table[:].bitcast(I32), 0)
         scale_rows = x_scales[0].bitcast(I32)
         for e in range(2):
@@ -55,7 +54,7 @@ def tile_picked_decode2_relu_p_kernel(tc, x_words, x_scales, w1, b1, w2, scl, sh
 
         offs_sb = lists.tile([P, S // GROUP], U16, name="offs_sb")
         rg_sb = lists.tile([P, S // GROUP], U16, name="rg_sb")
-        scl_tables = [keep.tile([P, U], F32, name="scl%d" % t) for t in range(EARLY)]
+        scl_tables = [keep.tile([P, U], F32, name="scl%d" % t) for t in range(PACK - 1)]
         nc.sync.dma_start(scl_tables[0][:], scl_rows[0])
         nc.sync.dma_start(rg_sb[:], rg)
         nc.sync.dma_start(offs_sb[:], offs)
@@ -63,7 +62,8 @@ def tile_picked_decode2_relu_p_kernel(tc, x_words, x_scales, w1, b1, w2, scl, sh
 
         w1_raw = shared.tile([P, PACK, H], F32, name="w1_raw", offset=0)
         nc.sync.dma_start(w1_raw[:], w1.rearrange("(p j) c -> p j c", j=PACK))
-        word_table = shared.tile([P, T], I32, name="word_table", offset=4 * TABLE_BYTES)
+        nc.sync.dma_start(scl_tables[2][:], scl_rows[2])
+        word_table = keep.tile([P, T], I32, name="word_table")
         nc.sync.dma_start(word_table[:], x_words[0].rearrange("p n t -> p (n t)").bitcast(I32))
 
         picked_scales = keep.tile([P, S], U8, name="picked_scales", align_bytes=64)
@@ -71,57 +71,54 @@ def tile_picked_decode2_relu_p_kernel(tc, x_words, x_scales, w1, b1, w2, scl, sh
         for r in range(4):
             src = GROUP * (r // 2) + r % 2
             nc.sync.dma_start(x_plane[:].bitcast(I32)[r:P:32, :], picked_scales[:].bitcast(I32)[src:P:32, :])
-        w2_rows = w2.rearrange("(p j) c -> p j c", j=PACK)
-        w2_raw = []
-        for u in range(2):
-            part = shared.tile([P, PACK, N // 2], F32, name="w2_raw%d" % u, offset=(8 + 2 * u) * TABLE_BYTES)
-            nc.sync.dma_start(part[:], w2_rows[:, :, u * N // 2 : (u + 1) * N // 2])
-            w2_raw.append(part)
+        last_scl = shared.tile([P, U], F32, name="last_scl", offset=4 * TABLE_BYTES)
+        nc.sync.dma_start(last_scl[:], scl_rows[PACK - 1])
+        scl_tables.append(last_scl)
+        w2_raw = shared.tile([P, PACK, N], F32, name="w2_raw", offset=5 * TABLE_BYTES)
+        nc.sync.dma_start(w2_raw[:], w2.rearrange("(p j) c -> p j c", j=PACK))
 
         picked_scl = []
-        for t in range(EARLY):
+
+        def pick_scl(t):
             picked = keep.tile([P, S], F32, name="picked_scl%d" % t)
             for lo in (0, HALF):
                 nc.vector.tensor_copy(out=picked[:, lo : lo + HALF], in_=scl_tables[t][:].indirect(rg_sb[:, lo // GROUP : (lo + HALF) // GROUP]))
             picked_scl.append(picked)
 
+        pick_scl(0)
+        pick_scl(1)
+
         w1_grouped = keep.tile([P, PACK * H], BF16, name="w1_grouped", align_bytes=64)
         dst = w1_grouped[:].rearrange("p (t m j) -> p m j t", t=PACK, j=PACK)
         src = w1_raw[:].rearrange("p j (m t) -> p m j t", t=PACK)
-        nc.vector.tensor_copy(out=dst[:, :, :, 0:2], in_=src[:, :, :, 0:2])
-        nc.vector.tensor_copy(out=dst[:, 0:W1_VECTOR_COLS, :, 2:4], in_=src[:, 0:W1_VECTOR_COLS, :, 2:4])
-        nc.scalar.copy(out=dst[:, W1_VECTOR_COLS:P, :, 2:4], in_=src[:, W1_VECTOR_COLS:P, :, 2:4])
+        nc.vector.tensor_copy(out=dst[:, 0:W1_VECTOR_COLS, :, 0:2], in_=src[:, 0:W1_VECTOR_COLS, :, 0:2])
+        nc.scalar.copy(out=dst[:, :, :, 2:4], in_=src[:, :, :, 2:4])
+        nc.scalar.copy(out=dst[:, W1_VECTOR_COLS:P, :, 0:2], in_=src[:, W1_VECTOR_COLS:P, :, 0:2])
         w1_codes = keep.tile([P, H], U32, name="w1_codes", align_bytes=64)
         w1_plane = keep.tile([P, H], U8, name="w1_plane", align_bytes=64)
         nc.vector.quantize_mx(out=w1_codes[:].bitcast(FP8X4), scales=w1_plane[:], in_=w1_grouped[:])
 
+        pick_scl(2)
         x_codes = []
         for lo in (0, HALF):
             codes = keep.tile([P, HALF], U32, name="x_codes%d" % lo, align_bytes=64)
             nc.vector.tensor_copy(out=codes[:], in_=word_table[:].bitcast(U32).indirect(offs_sb[:, lo // GROUP : (lo + HALF) // GROUP]))
             x_codes.append(codes)
 
+        pick_scl(3)
         shf_tables = []
-        slot = 0
         for t in range(PACK):
-            if t >= EARLY:
-                scl_t = shared.tile([P, U], F32, name="scl%d" % t, offset=slot * TABLE_BYTES)
-                nc.sync.dma_start(scl_t[:], scl_rows[t])
-                scl_tables.append(scl_t)
-                slot = slot + 1
-            shf_t = shared.tile([P, U], F32, name="shf%d" % t, offset=slot * TABLE_BYTES)
+            shf_t = shared.tile([P, U], F32, name="shf%d" % t, offset=t * TABLE_BYTES)
             nc.sync.dma_start(shf_t[:], shf_rows[t])
             shf_tables.append(shf_t)
-            slot = slot + 1
 
-        w2_grouped = keep.tile([P, PACK * N], BF16, name="w2_grouped", align_bytes=64, tag="w2_stage")
+        w2_grouped = keep.tile([P, PACK * N], BF16, name="w2_grouped", align_bytes=64)
         w2_codes = keep.tile([P, N], U32, name="w2_codes", align_bytes=64)
         w2_plane = keep.tile([P, N], U8, name="w2_plane", align_bytes=64)
 
-        def first_layer(c, banks):
+        def first_layer(c, banks, h_rows):
             lo, hi = CHUNKS[c]
             half = lo // HALF
-            h_rows = keep.tile([P, PACK, hi - lo], BF16, name="h_rows%d" % c, align_bytes=64)
             for t, bank in enumerate(banks):
                 acc = psum.tile([P, hi - lo], F32, name="acc", tag="bank%d" % bank)
                 nc.tensor.matmul_mx(
@@ -160,89 +157,72 @@ def tile_picked_decode2_relu_p_kernel(tc, x_words, x_scales, w1, b1, w2, scl, sh
                 stop=True,
             )
 
-        def cast_w2(u):
-            dst = w2_grouped[:].rearrange("p (t m j) -> p m j t", t=PACK, j=PACK)
-            src = w2_raw[u][:].rearrange("p j (m t) -> p m j t", t=PACK)
-            for pair in (0, 2):
-                nc.vector.tensor_copy(out=dst[:, 64 * u : 64 * (u + 1), :, pair : pair + 2], in_=src[:, :, :, pair : pair + 2])
-
-        h_rows_a = first_layer(0, (0, 1, 2, 3))
-        h_rows_b = first_layer(1, (4, 5, 6, 7))
-        grouped_b = keep.tile([P, 128, PACK], BF16, name="grouped_b", align_bytes=64)
-        interleave(grouped_b, h_rows_b, nc.scalar.copy)
-        h_rows_c = first_layer(2, (0, 1, 2, 3))
-        cast_w2(0)
-        grouped_a = shared.tile([P, 128, PACK], BF16, name="grouped_a", offset=8 * TABLE_BYTES)
-        interleave(grouped_a, h_rows_a, nc.vector.tensor_copy)
-        hidden_a = quantize_hidden(grouped_a, "codes_a", "plane_a")
-        cast_w2(1)
-        for t in range(PACK):
+        def quantize_w2(t):
             nc.vector.quantize_mx(
                 out=w2_codes[:, t * P : (t + 1) * P].bitcast(FP8X4),
                 scales=w2_plane[:, t * P : (t + 1) * P],
                 in_=w2_grouped[:, t * PACK * P : (t + 1) * PACK * P],
             )
-        hidden_b = quantize_hidden(grouped_b, "w2_stage", "handover")
 
-        ys = {}
-        for c, hidden in ((0, hidden_a), (1, hidden_b)):
-            for t in range(EARLY):
-                acc = psum.tile([P, 128], F32, name="acc", tag="bank%d" % (4 + 2 * c + t))
-                product(acc[:], t, hidden)
-                ys[t, CHUNKS[c][0]] = acc
-        for t in range(EARLY, PACK):
-            acc = psum.tile([P, HALF], F32, name="acc", tag="bank%d" % (t - EARLY))
-            product(acc[:, 0:128], t, hidden_a)
-            product(acc[:, 128:256], t, hidden_b)
-            y = keep.tile([P, HALF], F32, name="y0_%d" % t)
-            nc.scalar.copy(out=y[:], in_=acc[:])
-            ys[t, 0] = y
-        grouped_c = keep.tile([P, HALF, PACK], BF16, name="grouped_c", align_bytes=64, tag="handover")
-        interleave(grouped_c, h_rows_c, nc.scalar.copy)
-        hidden_c = quantize_hidden(grouped_c, "codes_c", "plane_c")
+        hidden = []
+        for c, copy in ((0, nc.vector.tensor_copy), (1, nc.scalar.copy)):
+            rows = keep.tile([P, PACK, 128], BF16, name="h_rows%d" % c)
+            first_layer(c, range(PACK * c, PACK * (c + 1)), rows)
+            grouped = keep.tile([P, 128, PACK], BF16, name="grouped%d" % c, align_bytes=64)
+            interleave(grouped, rows, copy)
+            hidden.append(quantize_hidden(grouped, "codes%d" % c, "plane%d" % c))
 
-        def last_products():
-            for t in range(PACK):
-                acc = psum.tile([P, HALF], F32, name="acc", tag="bank%d" % (2 + t))
-                product(acc[:], t, hidden_c)
-                if t < EARLY:
-                    ys[t, HALF] = acc
-                else:
-                    y = keep.tile([P, HALF], F32, name="y1_%d" % t)
-                    nc.scalar.copy(out=y[:], in_=acc[:])
-                    ys[t, HALF] = y
+        dst = w2_grouped[:].rearrange("p (t m j) -> p m j t", t=PACK, j=PACK)
+        src = w2_raw[:].rearrange("p j (m t) -> p m j t", t=PACK)
+        nc.vector.tensor_copy(out=dst[:, :, :, 0:2], in_=src[:, :, :, 0:2])
+        nc.scalar.copy(out=dst[:, :, :, 2:4], in_=src[:, :, :, 2:4])
 
-        zs, results = {}, {}
+        rows_c = shared.tile([P, PACK, HALF], BF16, name="h_rows2", offset=6 * TABLE_BYTES)
+        first_layer(2, range(PACK), rows_c)
+        grouped_c = keep.tile([P, HALF, PACK], BF16, name="grouped_c", align_bytes=64)
+        interleave(grouped_c, rows_c, nc.scalar.copy)
 
-        def scale(t, lo, hi):
-            z = keep.tile([P, hi - lo], F32, name="z", align_bytes=64, tag="handover" if (t, lo) == (3, 0) else "z%d_%d" % (t, lo))
-            if t < EARLY:
-                nc.vector.tensor_tensor(z[:], ys[t, lo][:], picked_scl[t][:, lo:hi], MULT)
+        zs = {}
+
+        def scale(half, t):
+            acc = psum.tile([P, HALF], F32, name="acc", tag="bank%d" % (PACK * (1 - half) + t))
+            if half == 0:
+                product(acc[:, 0:128], t, hidden[0])
+                product(acc[:, 128:256], t, hidden[1])
             else:
-                nc.vector.tensor_tensor(z[:], scl_tables[t][:].indirect(rg_sb[:, lo // GROUP : hi // GROUP]), ys[t, lo][:], MULT)
-            zs[t, lo] = z
+                product(acc[:], t, hidden[2])
+            z = keep.tile([P, HALF], F32, name="z%d_%d" % (half, t))
+            nc.vector.tensor_tensor(z[:], acc[:], picked_scl[t][:, half * HALF : (half + 1) * HALF], MULT)
+            zs[half, t] = z
 
-        def shift(t, lo, hi):
-            half = lo // HALF
-            if (half, t) not in results:
-                results[half, t] = keep.tile([P, HALF], F32, name="res%d_%d" % (half, t))
-            if (half, t) == (1, PACK - 1):
-                for a in (lo, lo + 128):
-                    cols = slice(a - HALF, a + 128 - HALF)
-                    nc.vector.tensor_tensor(results[half, t][:, cols], shf_tables[t][:].indirect(rg_sb[:, a // GROUP : (a + 128) // GROUP]), zs[t, lo][:, cols], ADD)
-                    nc.sync.dma_start(out_rows[t][:, a : a + 128], results[half, t][:, cols])
-                return
-            cols = slice(lo - half * HALF, hi - half * HALF)
-            nc.vector.tensor_tensor(results[half, t][:, cols], shf_tables[t][:].indirect(rg_sb[:, lo // GROUP : hi // GROUP]), zs[t, lo][:], ADD)
-            if hi % HALF == 0:
-                nc.sync.dma_start(out_rows[t][:, half * HALF : hi], results[half, t][:])
+        held = {(0, 1): 8 * TABLE_BYTES, (0, 2): 6 * TABLE_BYTES, (0, 3): 6 * TABLE_BYTES + TABLE_BYTES // 2}
 
-        steps = [(0, 0, 128), (1, 0, 128), (0, 128, 256), (1, 128, 256), (2, 0, 256), (3, 0, 256)]
-        steps = steps + [(t, 256, 512) for t in range(PACK)]
-        for i in range(len(steps) + 1):
-            if i == 6:
-                last_products()
-            if i < len(steps):
-                scale(*steps[i])
-            if i > 0:
-                shift(*steps[i - 1])
+        def shift(half, t):
+            if (half, t) in held:
+                res = shared.tile([P, HALF], F32, name="res%d_%d" % (half, t), offset=held[half, t])
+            else:
+                res = keep.tile([P, HALF], F32, name="res%d_%d" % (half, t))
+            width = HALF // 2 if (half, t) == (1, PACK - 1) else HALF
+            for lo in range(0, HALF, width):
+                first = half * HALF + lo
+                nc.vector.tensor_tensor(res[:, lo : lo + width], shf_tables[t][:].indirect(rg_sb[:, first // GROUP : (first + width) // GROUP]), zs[half, t][:, lo : lo + width], ADD)
+                nc.sync.dma_start(out_rows[t][:, first : first + width], res[:, lo : lo + width])
+
+        quantize_w2(0)
+        quantize_w2(1)
+        scale(0, 0)
+        scale(0, 1)
+        shift(0, 0)
+        quantize_w2(2)
+        quantize_w2(3)
+        shift(0, 1)
+        scale(0, 2)
+        scale(0, 3)
+        hidden.append(quantize_hidden(grouped_c, "codes2", "plane2"))
+        shift(0, 2)
+        shift(0, 3)
+        for t in range(PACK):
+            scale(1, t)
+            if t > 0:
+                shift(1, t - 1)
+        shift(1, PACK - 1)

@@ -37,7 +37,7 @@ def tile_picked_decode2_relu_p_kernel(tc, x_words, x_scales, w1, b1, w2, scl, sh
         shf_rows = shf.rearrange("(p t) u -> t p u", t=PACK)
         out_rows = out.rearrange("(p t) s -> t p s", t=PACK)
 
-        scale_table = shared.tile([P, T], U8, name="scale_table", align_bytes=64, offset=4 * TABLE_BYTES + TABLE_BYTES // 2)
+        scale_table = shared.tile([P, T], U8, name="scale_table", align_bytes=64, offset=5 * TABLE_BYTES + TABLE_BYTES // 2)
         nc.vector.memset(scale_table[:].bitcast(I32), 0)
         scale_rows = x_scales[0].bitcast(I32)
         for e in range(2):
@@ -54,15 +54,15 @@ def tile_picked_decode2_relu_p_kernel(tc, x_words, x_scales, w1, b1, w2, scl, sh
 
         offs_sb = lists.tile([P, S // GROUP], U16, name="offs_sb")
         rg_sb = lists.tile([P, S // GROUP], U16, name="rg_sb")
-        scl_tables = [keep.tile([P, U], F32, name="scl%d" % t) for t in range(PACK - 1)]
-        nc.sync.dma_start(scl_tables[0][:], scl_rows[0])
+        scl_tables = [keep.tile([P, 2 * U], F32, name="scl%d" % t) for t in range(PACK - 1)]
+        nc.sync.dma_start(scl_tables[0][:, 0:U], scl_rows[0])
         nc.sync.dma_start(rg_sb[:], rg)
         nc.sync.dma_start(offs_sb[:], offs)
-        nc.sync.dma_start(scl_tables[1][:], scl_rows[1])
+        nc.sync.dma_start(scl_tables[1][:, 0:U], scl_rows[1])
 
         w1_raw = shared.tile([P, PACK, H], F32, name="w1_raw", offset=0)
         nc.sync.dma_start(w1_raw[:], w1.rearrange("(p j) c -> p j c", j=PACK))
-        nc.sync.dma_start(scl_tables[2][:], scl_rows[2])
+        nc.sync.dma_start(scl_tables[2][:, 0:U], scl_rows[2])
         word_table = keep.tile([P, T], I32, name="word_table")
         nc.sync.dma_start(word_table[:], x_words[0].rearrange("p n t -> p (n t)").bitcast(I32))
 
@@ -71,18 +71,17 @@ def tile_picked_decode2_relu_p_kernel(tc, x_words, x_scales, w1, b1, w2, scl, sh
         for r in range(4):
             src = GROUP * (r // 2) + r % 2
             nc.sync.dma_start(x_plane[:].bitcast(I32)[r:P:32, :], picked_scales[:].bitcast(I32)[src:P:32, :])
-        last_scl = shared.tile([P, U], F32, name="last_scl", offset=4 * TABLE_BYTES)
-        nc.sync.dma_start(last_scl[:], scl_rows[PACK - 1])
+        last_scl = shared.tile([P, 2 * U], F32, name="last_scl", offset=4 * TABLE_BYTES)
+        nc.sync.dma_start(last_scl[:, 0:U], scl_rows[PACK - 1])
         scl_tables.append(last_scl)
-        w2_raw = shared.tile([P, PACK, N], F32, name="w2_raw", offset=5 * TABLE_BYTES)
+        w2_raw = shared.tile([P, PACK, N], F32, name="w2_raw", offset=6 * TABLE_BYTES)
         nc.sync.dma_start(w2_raw[:], w2.rearrange("(p j) c -> p j c", j=PACK))
 
         picked_scl = []
 
         def pick_scl(t):
             picked = keep.tile([P, S], F32, name="picked_scl%d" % t)
-            for lo in (0, HALF):
-                nc.vector.tensor_copy(out=picked[:, lo : lo + HALF], in_=scl_tables[t][:].indirect(rg_sb[:, lo // GROUP : (lo + HALF) // GROUP]))
+            nc.vector.tensor_copy(out=picked[:], in_=scl_tables[t][:].indirect(rg_sb[:]))
             picked_scl.append(picked)
 
         pick_scl(0)
@@ -112,7 +111,7 @@ def tile_picked_decode2_relu_p_kernel(tc, x_words, x_scales, w1, b1, w2, scl, sh
             nc.sync.dma_start(shf_t[:], shf_rows[t])
             shf_tables.append(shf_t)
 
-        w2_grouped = keep.tile([P, PACK * N], BF16, name="w2_grouped", align_bytes=64)
+        w2_grouped = [keep.tile([P, 2 * N], BF16, name="w2_grouped", align_bytes=64, tag="pair%d" % u) for u in range(2)]
         w2_codes = keep.tile([P, N], U32, name="w2_codes", align_bytes=64)
         w2_plane = keep.tile([P, N], U8, name="w2_plane", align_bytes=64)
 
@@ -157,27 +156,27 @@ def tile_picked_decode2_relu_p_kernel(tc, x_words, x_scales, w1, b1, w2, scl, sh
                 stop=True,
             )
 
-        def quantize_w2(t):
+        def quantize_w2(u):
             nc.vector.quantize_mx(
-                out=w2_codes[:, t * P : (t + 1) * P].bitcast(FP8X4),
-                scales=w2_plane[:, t * P : (t + 1) * P],
-                in_=w2_grouped[:, t * PACK * P : (t + 1) * PACK * P],
+                out=w2_codes[:, 2 * u * P : 2 * (u + 1) * P].bitcast(FP8X4),
+                scales=w2_plane[:, 2 * u * P : 2 * (u + 1) * P],
+                in_=w2_grouped[u][:],
             )
 
-        hidden = []
+        groups = []
         for c, copy in ((0, nc.vector.tensor_copy), (1, nc.scalar.copy)):
             rows = keep.tile([P, PACK, 128], BF16, name="h_rows%d" % c)
             first_layer(c, range(PACK * c, PACK * (c + 1)), rows)
             grouped = keep.tile([P, 128, PACK], BF16, name="grouped%d" % c, align_bytes=64)
             interleave(grouped, rows, copy)
-            hidden.append(quantize_hidden(grouped, "codes%d" % c, "plane%d" % c))
+            groups.append(grouped)
+        hidden = [quantize_hidden(groups[0], "codes0", "plane0")]
 
-        dst = w2_grouped[:].rearrange("p (t m j) -> p m j t", t=PACK, j=PACK)
         src = w2_raw[:].rearrange("p j (m t) -> p m j t", t=PACK)
-        nc.vector.tensor_copy(out=dst[:, :, :, 0:2], in_=src[:, :, :, 0:2])
-        nc.scalar.copy(out=dst[:, :, :, 2:4], in_=src[:, :, :, 2:4])
+        for u, copy in ((0, nc.vector.tensor_copy), (1, nc.scalar.copy)):
+            copy(out=w2_grouped[u][:].rearrange("p (t m j) -> p m j t", t=2, j=PACK), in_=src[:, :, :, 2 * u : 2 * u + 2])
 
-        rows_c = shared.tile([P, PACK, HALF], BF16, name="h_rows2", offset=6 * TABLE_BYTES)
+        rows_c = shared.tile([P, PACK, HALF], BF16, name="h_rows2", offset=7 * TABLE_BYTES)
         first_layer(2, range(PACK), rows_c)
         grouped_c = keep.tile([P, HALF, PACK], BF16, name="grouped_c", align_bytes=64)
         interleave(grouped_c, rows_c, nc.scalar.copy)
@@ -195,7 +194,7 @@ def tile_picked_decode2_relu_p_kernel(tc, x_words, x_scales, w1, b1, w2, scl, sh
             nc.vector.tensor_tensor(z[:], acc[:], picked_scl[t][:, half * HALF : (half + 1) * HALF], MULT)
             zs[half, t] = z
 
-        held = {(0, 1): 8 * TABLE_BYTES, (0, 2): 6 * TABLE_BYTES, (0, 3): 6 * TABLE_BYTES + TABLE_BYTES // 2}
+        held = {(0, 1): 9 * TABLE_BYTES, (0, 2): 7 * TABLE_BYTES, (0, 3): 7 * TABLE_BYTES + TABLE_BYTES // 2}
 
         def shift(half, t):
             if (half, t) in held:
@@ -209,12 +208,11 @@ def tile_picked_decode2_relu_p_kernel(tc, x_words, x_scales, w1, b1, w2, scl, sh
                 nc.sync.dma_start(out_rows[t][:, first : first + width], res[:, lo : lo + width])
 
         quantize_w2(0)
-        quantize_w2(1)
+        hidden.append(quantize_hidden(groups[1], "pair0", "plane1"))
         scale(0, 0)
         scale(0, 1)
         shift(0, 0)
-        quantize_w2(2)
-        quantize_w2(3)
+        quantize_w2(1)
         shift(0, 1)
         scale(0, 2)
         scale(0, 3)

@@ -20,9 +20,9 @@ P = 128
 PACK = 4
 GROUP = 16
 HALF = S // 2
-CHUNKS = ((0, 128), (128, 256), (256, 512))
+RUN = 4
 W1_VECTOR_COLS = 64
-TABLE_BYTES = U * 4
+ROW = U * 4
 
 
 def tile_picked_decode2_relu_p_kernel(tc, x_words, x_scales, w1, b1, w2, scl, shf, offs, rg, out):
@@ -33,15 +33,12 @@ def tile_picked_decode2_relu_p_kernel(tc, x_words, x_scales, w1, b1, w2, scl, sh
         keep = ctx.enter_context(tc.tile_pool(name="keep", bufs=1))
         psum = ctx.enter_context(tc.psum_pool(name="psum", bufs=1))
 
-        scl_rows = scl.rearrange("(p t) u -> t p u", t=PACK)
-        shf_rows = shf.rearrange("(p t) u -> t p u", t=PACK)
-        out_rows = out.rearrange("(p t) s -> t p s", t=PACK)
+        scl_rows = scl.rearrange("(a t b) u -> t a b u", t=PACK, b=RUN)
+        shf_rows = shf.rearrange("(a t b) u -> t a b u", t=PACK, b=RUN)
+        out_rows = out.rearrange("(a t b) s -> t a b s", t=PACK, b=RUN)
 
-        scale_table = shared.tile([P, T], U8, name="scale_table", align_bytes=64, offset=5 * TABLE_BYTES + TABLE_BYTES // 2)
+        scale_table = shared.tile([P, T], U8, name="scale_table", align_bytes=64, offset=8 * ROW + ROW // 2)
         nc.vector.memset(scale_table[:].bitcast(I32), 0)
-        scale_rows = x_scales[0].bitcast(I32)
-        for e in range(2):
-            nc.sync.dma_start(scale_table[:].bitcast(I32)[e:P:GROUP, :], scale_rows[e:16:2, :])
         x_plane = keep.tile([P, S], U8, name="x_plane", align_bytes=64)
         nc.gpsimd.memset(x_plane[:].bitcast(I32), 0)
 
@@ -52,40 +49,43 @@ def tile_picked_decode2_relu_p_kernel(tc, x_words, x_scales, w1, b1, w2, scl, sh
         warm_out = keep.tile([P, 8], F32, name="warm_out")
         nc.scalar.activation(out=warm_out[:], in_=warm[:], func=RELU)
 
+        def load_table(rows, name, offset):
+            table = shared.tile([P, 2 * U], F32, name=name, offset=offset)
+            nc.sync.dma_start(table[:, 0:U], rows)
+            return table
+
+        def load_scl(t, offset):
+            return load_table(scl_rows[t], "scl%d" % t, offset)
+
         offs_sb = lists.tile([P, S // GROUP], U16, name="offs_sb")
         rg_sb = lists.tile([P, S // GROUP], U16, name="rg_sb")
-        scl_tables = [keep.tile([P, 2 * U], F32, name="scl%d" % t) for t in range(PACK - 1)]
-        nc.sync.dma_start(scl_tables[0][:, 0:U], scl_rows[0])
+        scl_tables = [load_scl(0, 15 * ROW)]
         nc.sync.dma_start(rg_sb[:], rg)
         nc.sync.dma_start(offs_sb[:], offs)
-        nc.sync.dma_start(scl_tables[1][:, 0:U], scl_rows[1])
-
+        nc.sync.dma_start(scale_table[:].bitcast(I32)[0:P:8, :], x_scales[0].bitcast(I32))
+        scl_tables.append(load_scl(1, 11 * ROW))
         w1_raw = shared.tile([P, PACK, H], F32, name="w1_raw", offset=0)
         nc.sync.dma_start(w1_raw[:], w1.rearrange("(p j) c -> p j c", j=PACK))
-        nc.sync.dma_start(scl_tables[2][:, 0:U], scl_rows[2])
+        scl_tables.append(load_scl(2, 17 * ROW))
         word_table = keep.tile([P, T], I32, name="word_table")
         nc.sync.dma_start(word_table[:], x_words[0].rearrange("p n t -> p (n t)").bitcast(I32))
 
         picked_scales = keep.tile([P, S], U8, name="picked_scales", align_bytes=64)
         nc.vector.tensor_copy(out=picked_scales[:], in_=scale_table[:].indirect(offs_sb[:]))
         for r in range(4):
-            src = GROUP * (r // 2) + r % 2
-            nc.sync.dma_start(x_plane[:].bitcast(I32)[r:P:32, :], picked_scales[:].bitcast(I32)[src:P:32, :])
-        last_scl = shared.tile([P, 2 * U], F32, name="last_scl", offset=4 * TABLE_BYTES)
-        nc.sync.dma_start(last_scl[:, 0:U], scl_rows[PACK - 1])
-        scl_tables.append(last_scl)
-        w2_raw = shared.tile([P, PACK, N], F32, name="w2_raw", offset=6 * TABLE_BYTES)
-        nc.sync.dma_start(w2_raw[:], w2.rearrange("(p j) c -> p j c", j=PACK))
+            nc.sync.dma_start(x_plane[:].bitcast(I32)[r:P:32, :], picked_scales[:].bitcast(I32)[8 * r : P : 32, :])
+        scl_tables.append(load_scl(3, 7 * ROW))
+        shf_tables = [load_table(shf_rows[0], "shf0", 9 * ROW)]
 
-        picked_scl = []
+        picked_scl = keep.tile([P, PACK, S], F32, name="picked_scl")
 
         def pick_scl(t):
-            picked = keep.tile([P, S], F32, name="picked_scl%d" % t)
-            nc.vector.tensor_copy(out=picked[:], in_=scl_tables[t][:].indirect(rg_sb[:]))
-            picked_scl.append(picked)
+            nc.vector.tensor_copy(out=picked_scl[:, t, :], in_=scl_tables[t][:].indirect(rg_sb[:]))
 
         pick_scl(0)
         pick_scl(1)
+        w2_raw = shared.tile([P, PACK, N], F32, name="w2_raw", offset=11 * ROW)
+        nc.sync.dma_start(w2_raw[:], w2.rearrange("(p j) c -> p j c", j=PACK))
 
         w1_grouped = keep.tile([P, PACK * H], BF16, name="w1_grouped", align_bytes=64)
         dst = w1_grouped[:].rearrange("p (t m j) -> p m j t", t=PACK, j=PACK)
@@ -93,68 +93,58 @@ def tile_picked_decode2_relu_p_kernel(tc, x_words, x_scales, w1, b1, w2, scl, sh
         nc.vector.tensor_copy(out=dst[:, 0:W1_VECTOR_COLS, :, 0:2], in_=src[:, 0:W1_VECTOR_COLS, :, 0:2])
         nc.scalar.copy(out=dst[:, :, :, 2:4], in_=src[:, :, :, 2:4])
         nc.scalar.copy(out=dst[:, W1_VECTOR_COLS:P, :, 0:2], in_=src[:, W1_VECTOR_COLS:P, :, 0:2])
+        pick_scl(2)
         w1_codes = keep.tile([P, H], U32, name="w1_codes", align_bytes=64)
         w1_plane = keep.tile([P, H], U8, name="w1_plane", align_bytes=64)
         nc.vector.quantize_mx(out=w1_codes[:].bitcast(FP8X4), scales=w1_plane[:], in_=w1_grouped[:])
 
-        pick_scl(2)
+        for t in range(1, PACK):
+            shf_t = shared.tile([P, U], F32, name="shf%d" % t, offset=t * ROW)
+            nc.sync.dma_start(shf_t[:], shf_rows[t])
+            shf_tables.append(shf_t)
+
         x_codes = []
         for lo in (0, HALF):
             codes = keep.tile([P, HALF], U32, name="x_codes%d" % lo, align_bytes=64)
             nc.vector.tensor_copy(out=codes[:], in_=word_table[:].bitcast(U32).indirect(offs_sb[:, lo // GROUP : (lo + HALF) // GROUP]))
             x_codes.append(codes)
-
         pick_scl(3)
-        shf_tables = []
-        for t in range(PACK):
-            shf_t = shared.tile([P, U], F32, name="shf%d" % t, offset=t * TABLE_BYTES)
-            nc.sync.dma_start(shf_t[:], shf_rows[t])
-            shf_tables.append(shf_t)
+        picked_shf0 = keep.tile([P, S], F32, name="picked_shf0")
+        nc.vector.tensor_copy(out=picked_shf0[:], in_=shf_tables[0][:].indirect(rg_sb[:]))
 
-        w2_grouped = [keep.tile([P, 2 * N], BF16, name="w2_grouped", align_bytes=64, tag="pair%d" % u) for u in range(2)]
-        w2_codes = keep.tile([P, N], U32, name="w2_codes", align_bytes=64)
-        w2_plane = keep.tile([P, N], U8, name="w2_plane", align_bytes=64)
-
-        def first_layer(c, banks, h_rows):
-            lo, hi = CHUNKS[c]
-            half = lo // HALF
-            for t, bank in enumerate(banks):
-                acc = psum.tile([P, hi - lo], F32, name="acc", tag="bank%d" % bank)
+        def first_layer(half, h_rows, copy):
+            for t in range(PACK):
+                acc = psum.tile([P, HALF], F32, name="acc", tag="bank%d" % (PACK * half + t))
                 nc.tensor.matmul_mx(
                     out=acc[:],
                     lhsT=w1_codes[:, t * P : (t + 1) * P].bitcast(FP8X4),
                     lhsT_scale=w1_plane[:, t * P : (t + 1) * P],
-                    rhs=x_codes[half][:, lo - half * HALF : hi - half * HALF].bitcast(FP8X4),
-                    rhs_scale=x_plane[:, lo:hi],
+                    rhs=x_codes[half][:].bitcast(FP8X4),
+                    rhs_scale=x_plane[:, half * HALF : (half + 1) * HALF],
                     start=True,
                     stop=True,
                 )
                 nc.scalar.activation(out=h_rows[:, t, :], in_=acc[:], func=RELU, bias=bias[:, t : t + 1])
-            return h_rows
-
-        def interleave(h_grouped, h_rows, copy):
+            grouped = keep.tile([P, HALF, PACK], BF16, name="h_grouped%d" % half, align_bytes=64)
             copy(
-                out=h_grouped[:].rearrange("p (c i) t -> p c t i", i=4),
+                out=grouped[:].rearrange("p (c i) t -> p c t i", i=4),
                 in_=h_rows[:].rearrange("p t (c i) -> p c t i", i=4),
             )
+            return grouped
 
-        def quantize_hidden(h_grouped, codes_tag, plane_tag):
-            width = h_grouped.shape[1]
-            h_codes = keep.tile([P, width], U32, name="h_codes", align_bytes=64, tag=codes_tag)
-            h_plane = keep.tile([P, width], U8, name="h_plane", align_bytes=64, tag=plane_tag)
-            nc.vector.quantize_mx(out=h_codes[:].bitcast(FP8X4), scales=h_plane[:], in_=h_grouped[:].rearrange("p n t -> p (n t)"))
+        def quantize_hidden(half, grouped):
+            h_codes = keep.tile([P, HALF], U32, name="h_codes%d" % half, align_bytes=64)
+            h_plane = keep.tile([P, HALF], U8, name="h_plane%d" % half, align_bytes=64)
+            nc.vector.quantize_mx(out=h_codes[:].bitcast(FP8X4), scales=h_plane[:], in_=grouped[:].rearrange("p n t -> p (n t)"))
             return h_codes, h_plane
 
-        def product(acc, t, hidden):
-            nc.tensor.matmul_mx(
-                out=acc,
-                lhsT=w2_codes[:, t * P : (t + 1) * P].bitcast(FP8X4),
-                lhsT_scale=w2_plane[:, t * P : (t + 1) * P],
-                rhs=hidden[0][:].bitcast(FP8X4),
-                rhs_scale=hidden[1][:],
-                start=True,
-                stop=True,
-            )
+        w2_codes = keep.tile([P, N], U32, name="w2_codes", align_bytes=64)
+        w2_plane = keep.tile([P, N], U8, name="w2_plane", align_bytes=64)
+        w2_grouped = [keep.tile([P, 2 * N], BF16, name="w2_grouped", align_bytes=64, tag="pair%d" % u) for u in range(2)]
+        w2_cols = w2_raw[:].rearrange("p j (a t b) -> p t a j b", t=PACK, b=RUN)
+
+        def cast_w2(u, copy):
+            copy(out=w2_grouped[u][:].rearrange("p (t a b j) -> p t a j b", t=2, b=RUN, j=PACK), in_=w2_cols[:, 2 * u : 2 * u + 2])
 
         def quantize_w2(u):
             nc.vector.quantize_mx(
@@ -163,40 +153,34 @@ def tile_picked_decode2_relu_p_kernel(tc, x_words, x_scales, w1, b1, w2, scl, sh
                 in_=w2_grouped[u][:],
             )
 
-        groups = []
-        for c, copy in ((0, nc.vector.tensor_copy), (1, nc.scalar.copy)):
-            rows = keep.tile([P, PACK, 128], BF16, name="h_rows%d" % c)
-            first_layer(c, range(PACK * c, PACK * (c + 1)), rows)
-            grouped = keep.tile([P, 128, PACK], BF16, name="grouped%d" % c, align_bytes=64)
-            interleave(grouped, rows, copy)
-            groups.append(grouped)
-        hidden = [quantize_hidden(groups[0], "codes0", "plane0")]
-
-        src = w2_raw[:].rearrange("p j (m t) -> p m j t", t=PACK)
-        for u, copy in ((0, nc.vector.tensor_copy), (1, nc.scalar.copy)):
-            copy(out=w2_grouped[u][:].rearrange("p (t m j) -> p m j t", t=2, j=PACK), in_=src[:, :, :, 2 * u : 2 * u + 2])
-
-        rows_c = shared.tile([P, PACK, HALF], BF16, name="h_rows2", offset=7 * TABLE_BYTES)
-        first_layer(2, range(PACK), rows_c)
-        grouped_c = keep.tile([P, HALF, PACK], BF16, name="grouped_c", align_bytes=64)
-        interleave(grouped_c, rows_c, nc.scalar.copy)
+        rows0 = keep.tile([P, PACK, HALF], BF16, name="h_rows0")
+        grouped0 = first_layer(0, rows0, nc.vector.tensor_copy)
+        hidden = [quantize_hidden(0, grouped0)]
+        cast_w2(0, nc.scalar.copy)
+        cast_w2(1, nc.scalar.copy)
+        rows1 = shared.tile([P, PACK, HALF], BF16, name="h_rows1", offset=11 * ROW)
+        grouped1 = first_layer(1, rows1, nc.scalar.copy)
 
         zs = {}
 
         def scale(half, t):
-            acc = psum.tile([P, HALF], F32, name="acc", tag="bank%d" % (PACK * (1 - half) + t))
-            if half == 0:
-                product(acc[:, 0:128], t, hidden[0])
-                product(acc[:, 128:256], t, hidden[1])
-            else:
-                product(acc[:], t, hidden[2])
+            acc = psum.tile([P, HALF], F32, name="acc", tag="bank%d" % (PACK * half + t))
+            nc.tensor.matmul_mx(
+                out=acc[:],
+                lhsT=w2_codes[:, t * P : (t + 1) * P].bitcast(FP8X4),
+                lhsT_scale=w2_plane[:, t * P : (t + 1) * P],
+                rhs=hidden[half][0][:].bitcast(FP8X4),
+                rhs_scale=hidden[half][1][:],
+                start=True,
+                stop=True,
+            )
             z = keep.tile([P, HALF], F32, name="z%d_%d" % (half, t))
-            nc.vector.tensor_tensor(z[:], acc[:], picked_scl[t][:, half * HALF : (half + 1) * HALF], MULT)
+            nc.vector.tensor_tensor(z[:], acc[:], picked_scl[:, t, half * HALF : (half + 1) * HALF], MULT)
             zs[half, t] = z
 
-        held = {(0, 1): 9 * TABLE_BYTES, (0, 2): 7 * TABLE_BYTES, (0, 3): 7 * TABLE_BYTES + TABLE_BYTES // 2}
+        held = {(0, 0): 12 * ROW, (0, 3): 11 * ROW}
 
-        def shift(half, t):
+        def shift(half, t, picked=None):
             if (half, t) in held:
                 res = shared.tile([P, HALF], F32, name="res%d_%d" % (half, t), offset=held[half, t])
             else:
@@ -204,23 +188,28 @@ def tile_picked_decode2_relu_p_kernel(tc, x_words, x_scales, w1, b1, w2, scl, sh
             width = HALF // 2 if (half, t) == (1, PACK - 1) else HALF
             for lo in range(0, HALF, width):
                 first = half * HALF + lo
-                nc.vector.tensor_tensor(res[:, lo : lo + width], shf_tables[t][:].indirect(rg_sb[:, first // GROUP : (first + width) // GROUP]), zs[half, t][:, lo : lo + width], ADD)
-                nc.sync.dma_start(out_rows[t][:, first : first + width], res[:, lo : lo + width])
+                shifts = shf_tables[t][:].indirect(rg_sb[:, first // GROUP : (first + width) // GROUP]) if picked is None else picked
+                nc.vector.tensor_tensor(res[:, lo : lo + width], shifts, zs[half, t][:, lo : lo + width], ADD)
+                nc.sync.dma_start(out_rows[t][:, :, first : first + width], res[:, lo : lo + width])
 
         quantize_w2(0)
-        hidden.append(quantize_hidden(groups[1], "pair0", "plane1"))
+        picked_shf1 = keep.tile([P, HALF], F32, name="picked_shf1", align_bytes=64, tag="pair0")
+        nc.vector.tensor_copy(out=picked_shf1[:], in_=shf_tables[1][:].indirect(rg_sb[:, 0 : HALF // GROUP]))
         scale(0, 0)
         scale(0, 1)
-        shift(0, 0)
         quantize_w2(1)
-        shift(0, 1)
+        shift(0, 0, picked_shf0[:, 0:HALF])
+        shift(0, 1, picked_shf1[:])
         scale(0, 2)
         scale(0, 3)
-        hidden.append(quantize_hidden(grouped_c, "codes2", "plane2"))
         shift(0, 2)
+        hidden.append(quantize_hidden(1, grouped1))
         shift(0, 3)
-        for t in range(PACK):
-            scale(1, t)
-            if t > 0:
-                shift(1, t - 1)
-        shift(1, PACK - 1)
+        scale(1, 0)
+        scale(1, 1)
+        shift(1, 0, picked_shf0[:, HALF:S])
+        scale(1, 2)
+        shift(1, 1)
+        scale(1, 3)
+        shift(1, 2)
+        shift(1, 3)

@@ -132,32 +132,40 @@ def tile_picked_decode2_relu_p_kernel(tc, x_words, x_scales, w1, b1, w2, scl, sh
             )
             return grouped
 
-        def quantize_hidden(half, grouped):
-            h_codes = keep.tile([P, HALF], U32, name="h_codes%d" % half, align_bytes=64)
+        def quantize_hidden(half, grouped, codes_tag):
+            h_codes = keep.tile([P, HALF], U32, name="h_codes", align_bytes=64, tag=codes_tag)
             h_plane = keep.tile([P, HALF], U8, name="h_plane%d" % half, align_bytes=64)
             nc.vector.quantize_mx(out=h_codes[:].bitcast(FP8X4), scales=h_plane[:], in_=grouped[:].rearrange("p n t -> p (n t)"))
             return h_codes, h_plane
 
         w2_codes = keep.tile([P, N], U32, name="w2_codes", align_bytes=64)
         w2_plane = keep.tile([P, N], U8, name="w2_plane", align_bytes=64)
-        w2_grouped = [keep.tile([P, 2 * N], BF16, name="w2_grouped", align_bytes=64, tag="pair%d" % u) for u in range(2)]
+        w2_spans = ((0, 1), (1, 2), (2, 4))
+        w2_grouped = [keep.tile([P, (hi - lo) * N], BF16, name="w2_grouped", align_bytes=64, tag="span%d" % lo) for lo, hi in w2_spans]
         w2_cols = w2_raw[:].rearrange("p j (a t b) -> p t a j b", t=PACK, b=RUN)
 
-        def cast_w2(u, copy):
-            copy(out=w2_grouped[u][:].rearrange("p (t a b j) -> p t a j b", t=2, b=RUN, j=PACK), in_=w2_cols[:, 2 * u : 2 * u + 2])
+        def cast_w2(t, copy):
+            u = min(t, 2)
+            lo = (t - w2_spans[u][0]) * N
+            copy(out=w2_grouped[u][:, lo : lo + N].rearrange("p (a b j) -> p a j b", b=RUN, j=PACK), in_=w2_cols[:, t])
 
         def quantize_w2(u):
+            lo, hi = w2_spans[u]
             nc.vector.quantize_mx(
-                out=w2_codes[:, 2 * u * P : 2 * (u + 1) * P].bitcast(FP8X4),
-                scales=w2_plane[:, 2 * u * P : 2 * (u + 1) * P],
+                out=w2_codes[:, lo * P : hi * P].bitcast(FP8X4),
+                scales=w2_plane[:, lo * P : hi * P],
                 in_=w2_grouped[u][:],
             )
 
         rows0 = keep.tile([P, PACK, HALF], BF16, name="h_rows0")
-        grouped0 = first_layer(0, rows0, nc.vector.tensor_copy)
-        hidden = [quantize_hidden(0, grouped0)]
-        cast_w2(0, nc.scalar.copy)
-        cast_w2(1, nc.scalar.copy)
+        grouped0 = first_layer(0, rows0, nc.scalar.copy)
+        cast_w2(0, nc.vector.tensor_copy)
+        cast_w2(1, nc.vector.tensor_copy)
+        cast_w2(3, nc.scalar.copy)
+        quantize_w2(0)
+        quantize_w2(1)
+        hidden = [quantize_hidden(0, grouped0, "span0")]
+        cast_w2(2, nc.vector.tensor_copy)
         rows1 = shared.tile([P, PACK, HALF], BF16, name="h_rows1", offset=11 * ROW)
         grouped1 = first_layer(1, rows1, nc.scalar.copy)
 
@@ -178,7 +186,7 @@ def tile_picked_decode2_relu_p_kernel(tc, x_words, x_scales, w1, b1, w2, scl, sh
             nc.vector.tensor_tensor(z[:], acc[:], picked_scl[:, t, half * HALF : (half + 1) * HALF], MULT)
             zs[half, t] = z
 
-        held = {(0, 0): 12 * ROW, (0, 3): 11 * ROW}
+        held = {(0, 2): 11 * ROW + ROW // 2, (0, 3): 11 * ROW}
 
         def shift(half, t, picked=None):
             if (half, t) in held:
@@ -192,18 +200,17 @@ def tile_picked_decode2_relu_p_kernel(tc, x_words, x_scales, w1, b1, w2, scl, sh
                 nc.vector.tensor_tensor(res[:, lo : lo + width], shifts, zs[half, t][:, lo : lo + width], ADD)
                 nc.sync.dma_start(out_rows[t][:, :, first : first + width], res[:, lo : lo + width])
 
-        quantize_w2(0)
-        picked_shf1 = keep.tile([P, HALF], F32, name="picked_shf1", align_bytes=64, tag="pair0")
+        picked_shf1 = keep.tile([P, HALF], F32, name="picked_shf1", align_bytes=64, tag="span1")
         nc.vector.tensor_copy(out=picked_shf1[:], in_=shf_tables[1][:].indirect(rg_sb[:, 0 : HALF // GROUP]))
+        quantize_w2(2)
         scale(0, 0)
         scale(0, 1)
-        quantize_w2(1)
         shift(0, 0, picked_shf0[:, 0:HALF])
-        shift(0, 1, picked_shf1[:])
         scale(0, 2)
+        shift(0, 1, picked_shf1[:])
         scale(0, 3)
+        hidden.append(quantize_hidden(1, grouped1, "codes1"))
         shift(0, 2)
-        hidden.append(quantize_hidden(1, grouped1))
         shift(0, 3)
         scale(1, 0)
         scale(1, 1)

@@ -161,11 +161,11 @@ def tile_picked_decode2_relu_p_kernel(tc, x_words, x_scales, w1, b1, w2, scl, sh
         grouped0 = first_layer(0, rows0, nc.scalar.copy)
         cast_w2(0, nc.vector.tensor_copy)
         cast_w2(1, nc.vector.tensor_copy)
+        cast_w2(2, nc.vector.tensor_copy)
         cast_w2(3, nc.scalar.copy)
         quantize_w2(0)
         quantize_w2(1)
         hidden = [quantize_hidden(0, grouped0, "span0")]
-        cast_w2(2, nc.vector.tensor_copy)
         rows1 = shared.tile([P, PACK, HALF], BF16, name="h_rows1", offset=11 * ROW)
         grouped1 = first_layer(1, rows1, nc.scalar.copy)
 
@@ -188,35 +188,32 @@ def tile_picked_decode2_relu_p_kernel(tc, x_words, x_scales, w1, b1, w2, scl, sh
 
         held = {(0, 2): 11 * ROW + ROW // 2, (0, 3): 11 * ROW}
 
-        def shift(half, t, picked=None):
+        def shift(half, t, picked=None, engine=nc.vector):
             if (half, t) in held:
-                res = shared.tile([P, HALF], F32, name="res%d_%d" % (half, t), offset=held[half, t])
+                res = shared.tile([P, HALF], F32, name="res%d_%d" % (half, t), offset=held[half, t])[:]
+            elif t == 1:
+                res = picked_scl[:, 2, half * HALF : (half + 1) * HALF]
             else:
-                res = keep.tile([P, HALF], F32, name="res%d_%d" % (half, t))
+                res = keep.tile([P, HALF], F32, name="res%d_%d" % (half, t))[:]
             width = HALF // 2 if (half, t) == (1, PACK - 1) else HALF
             for lo in range(0, HALF, width):
                 first = half * HALF + lo
                 shifts = shf_tables[t][:].indirect(rg_sb[:, first // GROUP : (first + width) // GROUP]) if picked is None else picked
-                nc.vector.tensor_tensor(res[:, lo : lo + width], shifts, zs[half, t][:, lo : lo + width], ADD)
+                engine.tensor_tensor(res[:, lo : lo + width], shifts, zs[half, t][:, lo : lo + width], ADD)
                 nc.sync.dma_start(out_rows[t][:, :, first : first + width], res[:, lo : lo + width])
 
         picked_shf1 = keep.tile([P, HALF], F32, name="picked_shf1", align_bytes=64, tag="span1")
         nc.vector.tensor_copy(out=picked_shf1[:], in_=shf_tables[1][:].indirect(rg_sb[:, 0 : HALF // GROUP]))
         quantize_w2(2)
-        scale(0, 0)
-        scale(0, 1)
-        shift(0, 0, picked_shf0[:, 0:HALF])
-        scale(0, 2)
+        for t in range(PACK):
+            scale(0, t)
+        shift(0, 0, picked_shf0[:, 0:HALF], nc.gpsimd)
         shift(0, 1, picked_shf1[:])
-        scale(0, 3)
         hidden.append(quantize_hidden(1, grouped1, "codes1"))
         shift(0, 2)
         shift(0, 3)
-        scale(1, 0)
-        scale(1, 1)
-        shift(1, 0, picked_shf0[:, HALF:S])
-        scale(1, 2)
-        shift(1, 1)
-        scale(1, 3)
-        shift(1, 2)
-        shift(1, 3)
+        for t in range(PACK):
+            scale(1, t)
+        shift(1, 0, picked_shf0[:, HALF:S], nc.gpsimd)
+        for t in range(1, PACK):
+            shift(1, t)

@@ -23,6 +23,7 @@ HALF = S // 2
 RUN = 4
 W1_VECTOR_COLS = 64
 ROW = U * 4
+HOLD = 21 * ROW
 
 
 def tile_picked_decode2_relu_p_kernel(tc, x_words, x_scales, w1, b1, w2, scl, shf, offs, rg, out):
@@ -40,7 +41,6 @@ def tile_picked_decode2_relu_p_kernel(tc, x_words, x_scales, w1, b1, w2, scl, sh
         scale_table = shared.tile([P, T], U8, name="scale_table", align_bytes=64, offset=8 * ROW + ROW // 2)
         nc.vector.memset(scale_table[:].bitcast(I32), 0)
         x_plane = keep.tile([P, S], U8, name="x_plane", align_bytes=64)
-        nc.gpsimd.memset(x_plane[:].bitcast(I32), 0)
 
         bias = keep.tile([P, PACK], F32, name="bias")
         nc.scalar.dma_start(bias[:], b1.rearrange("(p t) o -> p (t o)", t=PACK))
@@ -59,23 +59,31 @@ def tile_picked_decode2_relu_p_kernel(tc, x_words, x_scales, w1, b1, w2, scl, sh
 
         offs_sb = lists.tile([P, S // GROUP], U16, name="offs_sb")
         rg_sb = lists.tile([P, S // GROUP], U16, name="rg_sb")
-        scl_tables = [load_scl(0, 15 * ROW)]
+        scl_tables = [load_scl(0, 16 * ROW)]
         nc.sync.dma_start(rg_sb[:], rg)
         nc.sync.dma_start(offs_sb[:], offs)
         nc.sync.dma_start(scale_table[:].bitcast(I32)[0:P:8, :], x_scales[0].bitcast(I32))
-        scl_tables.append(load_scl(1, 11 * ROW))
+        scl_tables.append(load_scl(1, 12 * ROW))
         w1_raw = shared.tile([P, PACK, H], F32, name="w1_raw", offset=0)
         nc.sync.dma_start(w1_raw[:], w1.rearrange("(p j) c -> p j c", j=PACK))
-        scl_tables.append(load_scl(2, 17 * ROW))
+        scl_tables.append(load_scl(2, 18 * ROW))
         word_table = keep.tile([P, T], I32, name="word_table")
         nc.sync.dma_start(word_table[:], x_words[0].rearrange("p n t -> p (n t)").bitcast(I32))
 
         picked_scales = keep.tile([P, S], U8, name="picked_scales", align_bytes=64)
         nc.vector.tensor_copy(out=picked_scales[:], in_=scale_table[:].indirect(offs_sb[:]))
-        for r in range(4):
+        nc.vector.tensor_copy(out=x_plane[:].bitcast(I32), in_=picked_scales[:].bitcast(I32))
+        for r in range(1, 4):
             nc.sync.dma_start(x_plane[:].bitcast(I32)[r:P:32, :], picked_scales[:].bitcast(I32)[8 * r : P : 32, :])
         scl_tables.append(load_scl(3, 7 * ROW))
-        shf_tables = [load_table(shf_rows[0], "shf0", 9 * ROW)]
+
+        def load_w2(side, offset):
+            raw = shared.tile([P, PACK, N // 2], F32, name="w2_raw%d" % side, offset=offset)
+            nc.sync.dma_start(raw[:], w2.rearrange("(p j) c -> p j c", j=PACK)[:, :, side * N // 2 : (side + 1) * N // 2])
+            return raw
+
+        w2_raw = [load_w2(0, 9 * ROW)]
+        shf_tables = [load_table(shf_rows[0], "shf0", 11 * ROW)]
 
         picked_scl = keep.tile([P, PACK, S], F32, name="picked_scl")
 
@@ -84,8 +92,7 @@ def tile_picked_decode2_relu_p_kernel(tc, x_words, x_scales, w1, b1, w2, scl, sh
 
         pick_scl(0)
         pick_scl(1)
-        w2_raw = shared.tile([P, PACK, N], F32, name="w2_raw", offset=11 * ROW)
-        nc.sync.dma_start(w2_raw[:], w2.rearrange("(p j) c -> p j c", j=PACK))
+        w2_raw.append(load_w2(1, 13 * ROW + ROW // 2))
 
         w1_grouped = keep.tile([P, PACK * H], BF16, name="w1_grouped", align_bytes=64)
         dst = w1_grouped[:].rearrange("p (t m j) -> p m j t", t=PACK, j=PACK)
@@ -132,41 +139,40 @@ def tile_picked_decode2_relu_p_kernel(tc, x_words, x_scales, w1, b1, w2, scl, sh
             )
             return grouped
 
-        def quantize_hidden(half, grouped, codes_tag):
-            h_codes = keep.tile([P, HALF], U32, name="h_codes", align_bytes=64, tag=codes_tag)
-            h_plane = keep.tile([P, HALF], U8, name="h_plane%d" % half, align_bytes=64)
+        def quantize_hidden(half, grouped, h_plane):
+            h_codes = keep.tile([P, HALF], U32, name="h_codes%d" % half, align_bytes=64)
             nc.vector.quantize_mx(out=h_codes[:].bitcast(FP8X4), scales=h_plane[:], in_=grouped[:].rearrange("p n t -> p (n t)"))
             return h_codes, h_plane
 
         w2_codes = keep.tile([P, N], U32, name="w2_codes", align_bytes=64)
         w2_plane = keep.tile([P, N], U8, name="w2_plane", align_bytes=64)
-        w2_spans = ((0, 1), (1, 2), (2, 4))
-        w2_grouped = [keep.tile([P, (hi - lo) * N], BF16, name="w2_grouped", align_bytes=64, tag="span%d" % lo) for lo, hi in w2_spans]
-        w2_cols = w2_raw[:].rearrange("p j (a t b) -> p t a j b", t=PACK, b=RUN)
+        w2_grouped = [shared.tile([P, N], BF16, name="w2_grouped%d" % t, align_bytes=64, offset=HOLD + offset) for t, offset in enumerate((0, 5120, 1024, 2560))]
+
+        def w2_views(t, side, order):
+            dst = w2_grouped[t][:, side * N // 2 : (side + 1) * N // 2].rearrange("p (a b j) -> p " + order, b=RUN, j=PACK)
+            src = w2_raw[side][:].rearrange("p j (a t b) -> p t " + order, t=PACK, b=RUN)[:, t]
+            return dst, src
 
         def cast_w2(t, copy):
-            u = min(t, 2)
-            lo = (t - w2_spans[u][0]) * N
-            copy(out=w2_grouped[u][:, lo : lo + N].rearrange("p (a b j) -> p a j b", b=RUN, j=PACK), in_=w2_cols[:, t])
+            dst, src = w2_views(t, 1, "a j b")
+            copy(out=dst, in_=src)
 
-        def quantize_w2(u):
-            lo, hi = w2_spans[u]
-            nc.vector.quantize_mx(
-                out=w2_codes[:, lo * P : hi * P].bitcast(FP8X4),
-                scales=w2_plane[:, lo * P : hi * P],
-                in_=w2_grouped[u][:],
-            )
+        def quantize_w2(t):
+            nc.vector.quantize_mx(out=w2_codes[:, t * P : (t + 1) * P].bitcast(FP8X4), scales=w2_plane[:, t * P : (t + 1) * P], in_=w2_grouped[t][:])
 
+        for t in range(PACK):
+            dst, src = w2_views(t, 0, "a b j")
+            nc.gpsimd.tensor_scalar(out=dst, in0=src, scalar1=1.0, scalar2=0.0, op0=MULT, op1=ADD)
         rows0 = keep.tile([P, PACK, HALF], BF16, name="h_rows0")
         grouped0 = first_layer(0, rows0, nc.scalar.copy)
         cast_w2(0, nc.vector.tensor_copy)
         cast_w2(1, nc.vector.tensor_copy)
-        cast_w2(2, nc.vector.tensor_copy)
+        cast_w2(2, nc.scalar.copy)
         cast_w2(3, nc.scalar.copy)
         quantize_w2(0)
         quantize_w2(1)
-        hidden = [quantize_hidden(0, grouped0, "span0")]
-        rows1 = shared.tile([P, PACK, HALF], BF16, name="h_rows1", offset=11 * ROW)
+        hidden = [quantize_hidden(0, grouped0, shared.tile([P, HALF], U8, name="h_plane0", align_bytes=64, offset=HOLD + 256))]
+        rows1 = shared.tile([P, PACK, HALF], BF16, name="h_rows1", offset=HOLD + 256 - ROW)
         grouped1 = first_layer(1, rows1, nc.scalar.copy)
 
         zs = {}
@@ -182,11 +188,14 @@ def tile_picked_decode2_relu_p_kernel(tc, x_words, x_scales, w1, b1, w2, scl, sh
                 start=True,
                 stop=True,
             )
-            z = keep.tile([P, HALF], F32, name="z%d_%d" % (half, t))
+            if half == 0 and t < 2:
+                z = shared.tile([P, HALF], F32, name="z0_%d" % t, offset=HOLD + 512 + t * 1024)
+            else:
+                z = keep.tile([P, HALF], F32, name="z%d_%d" % (half, t))
             nc.vector.tensor_tensor(z[:], acc[:], picked_scl[:, t, half * HALF : (half + 1) * HALF], MULT)
             zs[half, t] = z
 
-        held = {(0, 2): 11 * ROW + ROW // 2, (0, 3): 11 * ROW}
+        held = {(0, 2): HOLD + 256 - ROW, (0, 3): HOLD + 256 - ROW // 2}
 
         def shift(half, t, picked=None, engine=nc.vector):
             if (half, t) in held:
@@ -202,14 +211,15 @@ def tile_picked_decode2_relu_p_kernel(tc, x_words, x_scales, w1, b1, w2, scl, sh
                 engine.tensor_tensor(res[:, lo : lo + width], shifts, zs[half, t][:, lo : lo + width], ADD)
                 nc.sync.dma_start(out_rows[t][:, :, first : first + width], res[:, lo : lo + width])
 
-        picked_shf1 = keep.tile([P, HALF], F32, name="picked_shf1", align_bytes=64, tag="span1")
+        picked_shf1 = shared.tile([P, HALF], F32, name="picked_shf1", offset=HOLD + 5120)
         nc.vector.tensor_copy(out=picked_shf1[:], in_=shf_tables[1][:].indirect(rg_sb[:, 0 : HALF // GROUP]))
         quantize_w2(2)
+        quantize_w2(3)
         for t in range(PACK):
             scale(0, t)
         shift(0, 0, picked_shf0[:, 0:HALF], nc.gpsimd)
         shift(0, 1, picked_shf1[:])
-        hidden.append(quantize_hidden(1, grouped1, "codes1"))
+        hidden.append(quantize_hidden(1, grouped1, keep.tile([P, HALF], U8, name="h_plane1", align_bytes=64)))
         shift(0, 2)
         shift(0, 3)
         for t in range(PACK):

@@ -38,7 +38,7 @@ def tile_picked_decode2_relu_p_kernel(tc, x_words, x_scales, w1, b1, w2, scl, sh
         shf_rows = shf.rearrange("(a t b) u -> t a b u", t=PACK, b=RUN)
         out_rows = out.rearrange("(a t b) s -> t a b s", t=PACK, b=RUN)
 
-        scale_table = shared.tile([P, T], U8, name="scale_table", align_bytes=64, offset=8 * ROW + ROW // 2)
+        scale_table = shared.tile([P, T], U8, name="scale_table", align_bytes=64, offset=6 * ROW + ROW // 2)
         nc.vector.memset(scale_table[:].bitcast(I32), 0)
         x_plane = keep.tile([P, S], U8, name="x_plane", align_bytes=64)
 
@@ -70,11 +70,11 @@ def tile_picked_decode2_relu_p_kernel(tc, x_words, x_scales, w1, b1, w2, scl, sh
         word_table = keep.tile([P, T], I32, name="word_table")
         nc.sync.dma_start(word_table[:], x_words[0].rearrange("p n t -> p (n t)").bitcast(I32))
 
-        picked_scales = keep.tile([P, S], U8, name="picked_scales", align_bytes=64)
+        picked_scales = shared.tile([P, S], U8, name="picked_scales", align_bytes=64, offset=10 * ROW)
         nc.vector.tensor_copy(out=picked_scales[:], in_=scale_table[:].indirect(offs_sb[:]))
         nc.vector.tensor_copy(out=x_plane[:].bitcast(I32), in_=picked_scales[:].bitcast(I32))
         for r in range(1, 4):
-            nc.sync.dma_start(x_plane[:].bitcast(I32)[r:P:32, :], picked_scales[:].bitcast(I32)[8 * r : P : 32, :])
+            nc.sync.dma_start(x_plane[:].bitcast(I32)[r:P:32, :], x_plane[:].bitcast(I32)[8 * r : P : 32, :])
         scl_tables.append(load_scl(3, 7 * ROW))
 
         def load_w2(side, offset):
@@ -87,17 +87,25 @@ def tile_picked_decode2_relu_p_kernel(tc, x_words, x_scales, w1, b1, w2, scl, sh
 
         picked_scl = keep.tile([P, PACK, S], F32, name="picked_scl")
 
-        def pick_scl(t):
-            nc.vector.tensor_copy(out=picked_scl[:, t, :], in_=scl_tables[t][:].indirect(rg_sb[:]))
+        def pick_scl(t, width=S):
+            for lo in range(0, S, width):
+                nc.vector.tensor_copy(out=picked_scl[:, t, lo : lo + width], in_=scl_tables[t][:].indirect(rg_sb[:, lo // GROUP : (lo + width) // GROUP]))
 
         pick_scl(0)
-        pick_scl(1)
+        pick_scl(1, HALF)
         w2_raw.append(load_w2(1, 13 * ROW + ROW // 2))
 
         w1_grouped = keep.tile([P, PACK * H], BF16, name="w1_grouped", align_bytes=64)
         dst = w1_grouped[:].rearrange("p (t m j) -> p m j t", t=PACK, j=PACK)
         src = w1_raw[:].rearrange("p j (m t) -> p m j t", t=PACK)
-        nc.vector.tensor_copy(out=dst[:, 0:W1_VECTOR_COLS, :, 0:2], in_=src[:, 0:W1_VECTOR_COLS, :, 0:2])
+        nc.gpsimd.tensor_scalar(
+            out=w1_grouped[:].rearrange("p (t m j) -> p t m j", t=PACK, j=PACK)[:, 0:2, 0:W1_VECTOR_COLS],
+            in0=w1_raw[:].rearrange("p j (m t) -> p t m j", t=PACK)[:, 0:2, 0:W1_VECTOR_COLS],
+            scalar1=1.0,
+            scalar2=0.0,
+            op0=MULT,
+            op1=ADD,
+        )
         nc.scalar.copy(out=dst[:, :, :, 2:4], in_=src[:, :, :, 2:4])
         nc.scalar.copy(out=dst[:, W1_VECTOR_COLS:P, :, 0:2], in_=src[:, W1_VECTOR_COLS:P, :, 0:2])
         pick_scl(2)

@@ -21,6 +21,7 @@ PACK = 4
 GROUP = 16
 HALF = S // 2
 RUN = 4
+EARLY = 384
 W1_VECTOR_COLS = 64
 ROW = U * 4
 HOLD = 21 * ROW
@@ -83,7 +84,8 @@ def tile_picked_decode2_relu_p_kernel(tc, x_words, x_scales, w1, b1, w2, scl, sh
             return raw
 
         w2_raw = [load_w2(0, 9 * ROW)]
-        shf_tables = [load_table(shf_rows[0], "shf0", 11 * ROW)]
+        shf_tables = [shared.tile([P, U], F32, name="shf0", offset=11 * ROW + ROW // 2)]
+        nc.sync.dma_start(shf_tables[0][:], shf_rows[0])
 
         picked_scl = keep.tile([P, PACK, S], F32, name="picked_scl")
 
@@ -124,8 +126,8 @@ def tile_picked_decode2_relu_p_kernel(tc, x_words, x_scales, w1, b1, w2, scl, sh
             nc.vector.tensor_copy(out=codes[:], in_=word_table[:].bitcast(U32).indirect(offs_sb[:, lo // GROUP : (lo + HALF) // GROUP]))
             x_codes.append(codes)
         pick_scl(3)
-        picked_shf0 = keep.tile([P, S], F32, name="picked_shf0")
-        nc.vector.tensor_copy(out=picked_shf0[:], in_=shf_tables[0][:].indirect(rg_sb[:]))
+        picked_shf0 = keep.tile([P, EARLY + N // 2], F32, name="picked_shf0", align_bytes=64)
+        nc.vector.tensor_copy(out=picked_shf0[:, 0:EARLY], in_=shf_tables[0][:].indirect(rg_sb[:, 0 : EARLY // GROUP]))
 
         def first_layer(half, h_rows, copy):
             for t in range(PACK):
@@ -154,33 +156,32 @@ def tile_picked_decode2_relu_p_kernel(tc, x_words, x_scales, w1, b1, w2, scl, sh
 
         w2_codes = keep.tile([P, N], U32, name="w2_codes", align_bytes=64)
         w2_plane = keep.tile([P, N], U8, name="w2_plane", align_bytes=64)
-        w2_grouped = [shared.tile([P, N], BF16, name="w2_grouped%d" % t, align_bytes=64, offset=HOLD + offset) for t, offset in enumerate((0, 5120, 1024, 2560))]
+        first_staged = shared.tile([P, N], BF16, name="first_staged", align_bytes=64, offset=HOLD)
+        last_staged = shared.tile([P, 2, N], BF16, name="last_staged", align_bytes=64, offset=HOLD + 2048)
+        w2_staged = [first_staged[:], picked_shf0[:, EARLY : EARLY + N // 2].bitcast(BF16), last_staged[:, 0, :], last_staged[:, 1, :]]
+        w2_cols = [raw[:].rearrange("p j (a t b) -> p t a j b", t=PACK, b=RUN) for raw in w2_raw]
 
-        def w2_views(t, side, order):
-            dst = w2_grouped[t][:, side * N // 2 : (side + 1) * N // 2].rearrange("p (a b j) -> p " + order, b=RUN, j=PACK)
-            src = w2_raw[side][:].rearrange("p j (a t b) -> p t " + order, t=PACK, b=RUN)[:, t]
-            return dst, src
-
-        def cast_w2(t, copy):
-            dst, src = w2_views(t, 1, "a j b")
-            copy(out=dst, in_=src)
-
-        def quantize_w2(t):
-            nc.vector.quantize_mx(out=w2_codes[:, t * P : (t + 1) * P].bitcast(FP8X4), scales=w2_plane[:, t * P : (t + 1) * P], in_=w2_grouped[t][:])
+        def quantize_w2(lo, hi, staged):
+            nc.vector.quantize_mx(out=w2_codes[:, lo * P : hi * P].bitcast(FP8X4), scales=w2_plane[:, lo * P : hi * P], in_=staged)
 
         for t in range(PACK):
-            dst, src = w2_views(t, 0, "a b j")
-            nc.gpsimd.tensor_scalar(out=dst, in0=src, scalar1=1.0, scalar2=0.0, op0=MULT, op1=ADD)
-        rows0 = keep.tile([P, PACK, HALF], BF16, name="h_rows0")
+            nc.gpsimd.tensor_scalar(
+                out=w2_staged[t][:, 0 : N // 2].rearrange("p (a b j) -> p a b j", b=RUN, j=PACK),
+                in0=w2_cols[0][:, t].rearrange("p a j b -> p a b j"),
+                scalar1=1.0,
+                scalar2=0.0,
+                op0=MULT,
+                op1=ADD,
+            )
+        rows0 = keep.tile([P, PACK, HALF], BF16, name="h_rows", tag="rows")
         grouped0 = first_layer(0, rows0, nc.scalar.copy)
-        cast_w2(0, nc.vector.tensor_copy)
-        cast_w2(1, nc.vector.tensor_copy)
-        cast_w2(2, nc.scalar.copy)
-        cast_w2(3, nc.scalar.copy)
-        quantize_w2(0)
-        quantize_w2(1)
-        hidden = [quantize_hidden(0, grouped0, shared.tile([P, HALF], U8, name="h_plane0", align_bytes=64, offset=HOLD + 256))]
-        rows1 = shared.tile([P, PACK, HALF], BF16, name="h_rows1", offset=HOLD + 256 - ROW)
+        for t in range(2):
+            nc.vector.tensor_copy(out=w2_staged[t][:, N // 2 : N].rearrange("p (a b j) -> p a j b", b=RUN, j=PACK), in_=w2_cols[1][:, t])
+        quantize_w2(0, 1, w2_staged[0])
+        quantize_w2(1, 2, w2_staged[1])
+        hidden = [quantize_hidden(0, grouped0, shared.tile([P, HALF], U8, name="h_plane0", align_bytes=64, offset=HOLD))]
+        nc.vector.tensor_copy(out=last_staged[:, :, N // 2 : N].rearrange("p t (a b j) -> p t a j b", b=RUN, j=PACK), in_=w2_cols[1][:, 2:4])
+        rows1 = keep.tile([P, PACK, HALF], BF16, name="h_rows", tag="rows")
         grouped1 = first_layer(1, rows1, nc.scalar.copy)
 
         zs = {}
@@ -197,17 +198,17 @@ def tile_picked_decode2_relu_p_kernel(tc, x_words, x_scales, w1, b1, w2, scl, sh
                 stop=True,
             )
             if half == 0 and t < 2:
-                z = shared.tile([P, HALF], F32, name="z0_%d" % t, offset=HOLD + 512 + t * 1024)
+                z = shared.tile([P, HALF], F32, name="z0_%d" % t, offset=HOLD + 2048 + t * 1024)
             else:
                 z = keep.tile([P, HALF], F32, name="z%d_%d" % (half, t))
             nc.vector.tensor_tensor(z[:], acc[:], picked_scl[:, t, half * HALF : (half + 1) * HALF], MULT)
             zs[half, t] = z
 
-        held = {(0, 2): HOLD + 256 - ROW, (0, 3): HOLD + 256 - ROW // 2}
+        held = {(0, 2): 0, (0, 3): HALF}
 
         def shift(half, t, picked=None, engine=nc.vector):
             if (half, t) in held:
-                res = shared.tile([P, HALF], F32, name="res%d_%d" % (half, t), offset=held[half, t])[:]
+                res = rows1[:].rearrange("p t n -> p (t n)").bitcast(F32)[:, held[half, t] : held[half, t] + HALF]
             elif t == 1:
                 res = picked_scl[:, 2, half * HALF : (half + 1) * HALF]
             else:
@@ -219,14 +220,12 @@ def tile_picked_decode2_relu_p_kernel(tc, x_words, x_scales, w1, b1, w2, scl, sh
                 engine.tensor_tensor(res[:, lo : lo + width], shifts, zs[half, t][:, lo : lo + width], ADD)
                 nc.sync.dma_start(out_rows[t][:, :, first : first + width], res[:, lo : lo + width])
 
-        picked_shf1 = shared.tile([P, HALF], F32, name="picked_shf1", offset=HOLD + 5120)
-        nc.vector.tensor_copy(out=picked_shf1[:], in_=shf_tables[1][:].indirect(rg_sb[:, 0 : HALF // GROUP]))
-        quantize_w2(2)
-        quantize_w2(3)
+        nc.vector.tensor_copy(out=picked_shf0[:, EARLY:S], in_=shf_tables[0][:].indirect(rg_sb[:, EARLY // GROUP : S // GROUP]))
+        quantize_w2(2, 4, last_staged[:].rearrange("p t c -> p (t c)"))
         for t in range(PACK):
             scale(0, t)
         shift(0, 0, picked_shf0[:, 0:HALF], nc.gpsimd)
-        shift(0, 1, picked_shf1[:])
+        shift(0, 1)
         hidden.append(quantize_hidden(1, grouped1, keep.tile([P, HALF], U8, name="h_plane1", align_bytes=64)))
         shift(0, 2)
         shift(0, 3)

@@ -45,10 +45,8 @@ def tile_picked_decode2_relu_p_kernel(tc, x_words, x_scales, w1, b1, w2, scl, sh
 
         bias = keep.tile([P, PACK], F32, name="bias")
         nc.scalar.dma_start(bias[:], b1.rearrange("(p t) o -> p (t o)", t=PACK))
-        warm = keep.tile([P, 8], F32, name="warm")
-        nc.gpsimd.memset(warm[:], 0.0)
-        warm_out = keep.tile([P, 8], F32, name="warm_out")
-        nc.scalar.activation(out=warm_out[:], in_=warm[:], func=RELU)
+        warm_out = keep.tile([P, PACK], F32, name="warm_out")
+        nc.scalar.activation(out=warm_out[:], in_=bias[:], func=RELU)
 
         def load_table(rows, name, offset):
             table = shared.tile([P, 2 * U], F32, name=name, offset=offset)
@@ -145,7 +143,7 @@ def tile_picked_decode2_relu_p_kernel(tc, x_words, x_scales, w1, b1, w2, scl, sh
             grouped = keep.tile([P, HALF, PACK], BF16, name="h_grouped%d" % half, align_bytes=64)
             copy(
                 out=grouped[:].rearrange("p (c i) t -> p c t i", i=4),
-                in_=h_rows[:].rearrange("p t (c i) -> p c t i", i=4),
+                in_=h_rows.rearrange("p t (c i) -> p c t i", i=4),
             )
             return grouped
 
@@ -173,7 +171,8 @@ def tile_picked_decode2_relu_p_kernel(tc, x_words, x_scales, w1, b1, w2, scl, sh
                 op0=MULT,
                 op1=ADD,
             )
-        rows0 = keep.tile([P, PACK, HALF], BF16, name="h_rows", tag="rows")
+        rows = keep.tile([P, PACK + 1, HALF], BF16, name="h_rows")
+        rows0 = rows[:, 1 : PACK + 1, :]
         grouped0 = first_layer(0, rows0, nc.scalar.copy)
         for t in range(2):
             nc.vector.tensor_copy(out=w2_staged[t][:, N // 2 : N].rearrange("p (a b j) -> p a j b", b=RUN, j=PACK), in_=w2_cols[1][:, t])
@@ -181,7 +180,7 @@ def tile_picked_decode2_relu_p_kernel(tc, x_words, x_scales, w1, b1, w2, scl, sh
         quantize_w2(1, 2, w2_staged[1])
         hidden = [quantize_hidden(0, grouped0, shared.tile([P, HALF], U8, name="h_plane0", align_bytes=64, offset=HOLD))]
         nc.vector.tensor_copy(out=last_staged[:, :, N // 2 : N].rearrange("p t (a b j) -> p t a j b", b=RUN, j=PACK), in_=w2_cols[1][:, 2:4])
-        rows1 = keep.tile([P, PACK, HALF], BF16, name="h_rows", tag="rows")
+        rows1 = rows[:, 0:PACK, :]
         grouped1 = first_layer(1, rows1, nc.scalar.copy)
 
         zs = {}
@@ -208,7 +207,7 @@ def tile_picked_decode2_relu_p_kernel(tc, x_words, x_scales, w1, b1, w2, scl, sh
 
         def shift(half, t, picked=None, engine=nc.vector):
             if (half, t) in held:
-                res = rows1[:].rearrange("p t n -> p (t n)").bitcast(F32)[:, held[half, t] : held[half, t] + HALF]
+                res = rows1.rearrange("p t n -> p (t n)").bitcast(F32)[:, held[half, t] : held[half, t] + HALF]
             elif t == 1:
                 res = picked_scl[:, 2, half * HALF : (half + 1) * HALF]
             else:

@@ -15,6 +15,7 @@ FP8X4 = mybir.dt.float8_e4m3fn_x4
 MULT = mybir.AluOpType.mult
 ADD = mybir.AluOpType.add
 RELU = mybir.ActivationFunctionType.Relu
+COPY = mybir.ActivationFunctionType.Copy
 
 P = 128
 PACK = 4
@@ -22,9 +23,10 @@ GROUP = 16
 HALF = S // 2
 RUN = 4
 EARLY = 384
-W1_VECTOR_COLS = 64
-ROW = U * 4
-HOLD = 21 * ROW
+W1_VECTOR_EXTRA = 32
+KIB = 1024
+HOLD = 32 * KIB
+ROWS_AT = 40 * KIB
 
 
 def tile_picked_decode2_relu_p_kernel(tc, x_words, x_scales, w1, b1, w2, scl, shf, offs, rg, out):
@@ -39,7 +41,7 @@ def tile_picked_decode2_relu_p_kernel(tc, x_words, x_scales, w1, b1, w2, scl, sh
         shf_rows = shf.rearrange("(a t b) u -> t a b u", t=PACK, b=RUN)
         out_rows = out.rearrange("(a t b) s -> t a b s", t=PACK, b=RUN)
 
-        scale_table = shared.tile([P, T], U8, name="scale_table", align_bytes=64, offset=6 * ROW + ROW // 2)
+        scale_table = keep.tile([P, T], U8, name="scale_table", align_bytes=64)
         nc.vector.memset(scale_table[:].bitcast(I32), 0)
         x_plane = keep.tile([P, S], U8, name="x_plane", align_bytes=64)
 
@@ -48,82 +50,65 @@ def tile_picked_decode2_relu_p_kernel(tc, x_words, x_scales, w1, b1, w2, scl, sh
         warm_out = keep.tile([P, PACK], F32, name="warm_out")
         nc.scalar.activation(out=warm_out[:], in_=bias[:], func=RELU)
 
-        def load_table(rows, name, offset):
-            table = shared.tile([P, 2 * U], F32, name=name, offset=offset)
+        def load_table(rows, name, offset, cols=U):
+            table = shared.tile([P, cols], F32, name=name, offset=offset)
             nc.sync.dma_start(table[:, 0:U], rows)
             return table
-
-        def load_scl(t, offset):
-            return load_table(scl_rows[t], "scl%d" % t, offset)
-
-        offs_sb = lists.tile([P, S // GROUP], U16, name="offs_sb")
-        rg_sb = lists.tile([P, S // GROUP], U16, name="rg_sb")
-        scl_tables = [load_scl(0, 16 * ROW)]
-        nc.sync.dma_start(rg_sb[:], rg)
-        nc.sync.dma_start(offs_sb[:], offs)
-        nc.sync.dma_start(scale_table[:].bitcast(I32)[0:P:8, :], x_scales[0].bitcast(I32))
-        scl_tables.append(load_scl(1, 12 * ROW))
-        w1_raw = shared.tile([P, PACK, H], F32, name="w1_raw", offset=0)
-        nc.sync.dma_start(w1_raw[:], w1.rearrange("(p j) c -> p j c", j=PACK))
-        scl_tables.append(load_scl(2, 18 * ROW))
-        word_table = keep.tile([P, T], I32, name="word_table")
-        nc.sync.dma_start(word_table[:], x_words[0].rearrange("p n t -> p (n t)").bitcast(I32))
-
-        picked_scales = shared.tile([P, S], U8, name="picked_scales", align_bytes=64, offset=10 * ROW)
-        nc.vector.tensor_copy(out=picked_scales[:], in_=scale_table[:].indirect(offs_sb[:]))
-        nc.vector.tensor_copy(out=x_plane[:].bitcast(I32), in_=picked_scales[:].bitcast(I32))
-        for r in range(1, 4):
-            nc.sync.dma_start(x_plane[:].bitcast(I32)[r:P:32, :], x_plane[:].bitcast(I32)[8 * r : P : 32, :])
-        scl_tables.append(load_scl(3, 7 * ROW))
 
         def load_w2(side, offset):
             raw = shared.tile([P, PACK, N // 2], F32, name="w2_raw%d" % side, offset=offset)
             nc.sync.dma_start(raw[:], w2.rearrange("(p j) c -> p j c", j=PACK)[:, :, side * N // 2 : (side + 1) * N // 2])
             return raw
 
-        w2_raw = [load_w2(0, 9 * ROW)]
-        shf_tables = [shared.tile([P, U], F32, name="shf0", offset=11 * ROW + ROW // 2)]
-        nc.sync.dma_start(shf_tables[0][:], shf_rows[0])
+        offs_sb = lists.tile([P, S // GROUP], U16, name="offs_sb")
+        rg_sb = lists.tile([P, S // GROUP], U16, name="rg_sb")
+        scl_tables, shf_tables = {}, {}
+        scl_tables[0] = load_table(scl_rows[0], "scl0", 48 * KIB, 2 * U)
+        nc.sync.dma_start(rg_sb[:], rg)
+        nc.sync.dma_start(offs_sb[:], offs)
+        nc.sync.dma_start(scale_table[:].bitcast(I32)[0:P:8, :], x_scales[0].bitcast(I32))
+        scl_tables[1] = load_table(scl_rows[1], "scl1", 52 * KIB, 2 * U)
+        w1_raw = keep.tile([P, PACK, H], F32, name="w1_raw")
+        nc.sync.dma_start(w1_raw[:], w1.rearrange("(p j) c -> p j c", j=PACK))
+        word_table = keep.tile([P, T], I32, name="word_table")
+        nc.sync.dma_start(word_table[:], x_words[0].rearrange("p n t -> p (n t)").bitcast(I32))
 
-        picked_scl = keep.tile([P, PACK, S], F32, name="picked_scl")
+        picked_scales = shared.tile([P, 21 * KIB], U8, name="picked_scales", align_bytes=64, offset=0)
+        nc.vector.tensor_copy(out=picked_scales[:, 0:S], in_=scale_table[:].indirect(offs_sb[:]))
+        nc.vector.tensor_copy(out=x_plane[:].bitcast(I32), in_=picked_scales[:, 0:S].bitcast(I32))
+        for r in range(1, 4):
+            nc.sync.dma_start(x_plane[:].bitcast(I32)[r:P:32, :], x_plane[:].bitcast(I32)[8 * r : P : 32, :])
+        scl_tables[2] = load_table(scl_rows[2], "scl2", 0, 2 * U)
+        w2_raw = [load_w2(0, 4 * KIB)]
+        shf_tables[0] = load_table(shf_rows[0], "shf0", 8 * KIB)
+        w2_raw.append(load_w2(1, 10 * KIB))
+        scl_tables[3] = load_table(scl_rows[3], "scl3", 14 * KIB)
+        for t in range(1, PACK):
+            shf_tables[t] = load_table(shf_rows[t], "shf%d" % t, (14 + 2 * t) * KIB)
 
-        def pick_scl(t, width=S):
-            for lo in range(0, S, width):
-                nc.vector.tensor_copy(out=picked_scl[:, t, lo : lo + width], in_=scl_tables[t][:].indirect(rg_sb[:, lo // GROUP : (lo + width) // GROUP]))
+        def entries(lo, width):
+            return rg_sb[:, lo // GROUP : (lo + width) // GROUP]
 
-        pick_scl(0)
-        pick_scl(1, HALF)
-        w2_raw.append(load_w2(1, 13 * ROW + ROW // 2))
+        picked_scl = keep.tile([P, PACK - 1, S], F32, name="picked_scl")
+        for t in range(2):
+            nc.scalar.activation(out=picked_scl[:, t, :], in_=scl_tables[t][:].indirect(entries(0, S)), func=COPY)
 
         w1_grouped = keep.tile([P, PACK * H], BF16, name="w1_grouped", align_bytes=64)
         dst = w1_grouped[:].rearrange("p (t m j) -> p m j t", t=PACK, j=PACK)
         src = w1_raw[:].rearrange("p j (m t) -> p m j t", t=PACK)
-        nc.gpsimd.tensor_scalar(
-            out=w1_grouped[:].rearrange("p (t m j) -> p t m j", t=PACK, j=PACK)[:, 0:2, 0:W1_VECTOR_COLS],
-            in0=w1_raw[:].rearrange("p j (m t) -> p t m j", t=PACK)[:, 0:2, 0:W1_VECTOR_COLS],
-            scalar1=1.0,
-            scalar2=0.0,
-            op0=MULT,
-            op1=ADD,
-        )
-        nc.scalar.copy(out=dst[:, :, :, 2:4], in_=src[:, :, :, 2:4])
-        nc.scalar.copy(out=dst[:, W1_VECTOR_COLS:P, :, 0:2], in_=src[:, W1_VECTOR_COLS:P, :, 0:2])
-        pick_scl(2)
+        nc.vector.tensor_copy(out=dst[:, :, :, 0:2], in_=src[:, :, :, 0:2])
+        nc.vector.tensor_copy(out=dst[:, 0:W1_VECTOR_EXTRA, :, 2:4], in_=src[:, 0:W1_VECTOR_EXTRA, :, 2:4])
+        nc.scalar.copy(out=dst[:, W1_VECTOR_EXTRA:P, :, 2:4], in_=src[:, W1_VECTOR_EXTRA:P, :, 2:4])
         w1_codes = keep.tile([P, H], U32, name="w1_codes", align_bytes=64)
         w1_plane = keep.tile([P, H], U8, name="w1_plane", align_bytes=64)
         nc.vector.quantize_mx(out=w1_codes[:].bitcast(FP8X4), scales=w1_plane[:], in_=w1_grouped[:])
-
-        for t in range(1, PACK):
-            shf_t = shared.tile([P, U], F32, name="shf%d" % t, offset=t * ROW)
-            nc.sync.dma_start(shf_t[:], shf_rows[t])
-            shf_tables.append(shf_t)
 
         x_codes = []
         for lo in (0, HALF):
             codes = keep.tile([P, HALF], U32, name="x_codes%d" % lo, align_bytes=64)
             nc.vector.tensor_copy(out=codes[:], in_=word_table[:].bitcast(U32).indirect(offs_sb[:, lo // GROUP : (lo + HALF) // GROUP]))
             x_codes.append(codes)
-        pick_scl(3)
+        nc.vector.tensor_copy(out=picked_scl[:, 2, :], in_=scl_tables[2][:].indirect(entries(0, S)))
         picked_shf0 = keep.tile([P, EARLY + N // 2], F32, name="picked_shf0", align_bytes=64)
         nc.vector.tensor_copy(out=picked_shf0[:, 0:EARLY], in_=shf_tables[0][:].indirect(rg_sb[:, 0 : EARLY // GROUP]))
 
@@ -171,7 +156,7 @@ def tile_picked_decode2_relu_p_kernel(tc, x_words, x_scales, w1, b1, w2, scl, sh
                 op0=MULT,
                 op1=ADD,
             )
-        rows = keep.tile([P, PACK + 1, HALF], BF16, name="h_rows")
+        rows = shared.tile([P, 2 * PACK, HALF], BF16, name="h_rows", offset=ROWS_AT)
         rows0 = rows[:, 1 : PACK + 1, :]
         grouped0 = first_layer(0, rows0, nc.scalar.copy)
         for t in range(2):
@@ -182,6 +167,16 @@ def tile_picked_decode2_relu_p_kernel(tc, x_words, x_scales, w1, b1, w2, scl, sh
         nc.vector.tensor_copy(out=last_staged[:, :, N // 2 : N].rearrange("p t (a b j) -> p t a j b", b=RUN, j=PACK), in_=w2_cols[1][:, 2:4])
         rows1 = rows[:, 0:PACK, :]
         grouped1 = first_layer(1, rows1, nc.scalar.copy)
+
+        def pick_late(table, half, name, offset):
+            picked = shared.tile([P, HALF], F32, name=name, offset=offset)
+            nc.scalar.activation(out=picked[:], in_=table[:].indirect(entries(half * HALF, HALF)), func=COPY)
+            return picked
+
+        late_scl, late_shf = [], []
+        for half in range(2):
+            late_scl.append(pick_late(scl_tables[3], half, "picked_scl3_%d" % half, ROWS_AT + 2 * half * KIB))
+            late_shf.append(pick_late(shf_tables[1], half, "picked_shf1_%d" % half, ROWS_AT + (2 * half + 1) * KIB))
 
         zs = {}
 
@@ -200,36 +195,31 @@ def tile_picked_decode2_relu_p_kernel(tc, x_words, x_scales, w1, b1, w2, scl, sh
                 z = shared.tile([P, HALF], F32, name="z0_%d" % t, offset=HOLD + 2048 + t * 1024)
             else:
                 z = keep.tile([P, HALF], F32, name="z%d_%d" % (half, t))
-            nc.vector.tensor_tensor(z[:], acc[:], picked_scl[:, t, half * HALF : (half + 1) * HALF], MULT)
+            scales = late_scl[half][:] if t == PACK - 1 else picked_scl[:, t, half * HALF : (half + 1) * HALF]
+            nc.vector.tensor_tensor(z[:], acc[:], scales, MULT)
             zs[half, t] = z
 
-        held = {(0, 2): 0, (0, 3): HALF}
-
-        def shift(half, t, picked=None, engine=nc.vector):
-            if (half, t) in held:
-                res = rows1.rearrange("p t n -> p (t n)").bitcast(F32)[:, held[half, t] : held[half, t] + HALF]
-            elif t == 1:
-                res = picked_scl[:, 2, half * HALF : (half + 1) * HALF]
-            else:
-                res = keep.tile([P, HALF], F32, name="res%d_%d" % (half, t))[:]
-            width = HALF // 2 if (half, t) == (1, PACK - 1) else HALF
+        def shift(half, t, picked=None, engine=nc.vector, width=HALF):
+            res = keep.tile([P, HALF], F32, name="res%d_%d" % (half, t))
             for lo in range(0, HALF, width):
                 first = half * HALF + lo
-                shifts = shf_tables[t][:].indirect(rg_sb[:, first // GROUP : (first + width) // GROUP]) if picked is None else picked
+                shifts = shf_tables[t][:].indirect(entries(first, width)) if picked is None else picked
                 engine.tensor_tensor(res[:, lo : lo + width], shifts, zs[half, t][:, lo : lo + width], ADD)
                 nc.sync.dma_start(out_rows[t][:, :, first : first + width], res[:, lo : lo + width])
 
         nc.vector.tensor_copy(out=picked_shf0[:, EARLY:S], in_=shf_tables[0][:].indirect(rg_sb[:, EARLY // GROUP : S // GROUP]))
         quantize_w2(2, 4, last_staged[:].rearrange("p t c -> p (t c)"))
-        for t in range(PACK):
+        for t in range(PACK - 1):
             scale(0, t)
         shift(0, 0, picked_shf0[:, 0:HALF], nc.gpsimd)
-        shift(0, 1)
-        hidden.append(quantize_hidden(1, grouped1, keep.tile([P, HALF], U8, name="h_plane1", align_bytes=64)))
         shift(0, 2)
+        hidden.append(quantize_hidden(1, grouped1, keep.tile([P, HALF], U8, name="h_plane1", align_bytes=64)))
+        scale(0, 3)
         shift(0, 3)
         for t in range(PACK):
             scale(1, t)
+        shift(0, 1, late_shf[0][:], nc.gpsimd)
         shift(1, 0, picked_shf0[:, HALF:S], nc.gpsimd)
-        for t in range(1, PACK):
-            shift(1, t)
+        shift(1, 2)
+        shift(1, 1, late_shf[1][:])
+        shift(1, 3, width=HALF // 2)

@@ -22,10 +22,8 @@ PACK = 4
 GROUP = 16
 HALF = S // 2
 RUN = 4
-EARLY = 384
 W1_VECTOR_EXTRA = 32
 KIB = 1024
-HOLD = 32 * KIB
 ROWS_AT = 40 * KIB
 
 
@@ -55,11 +53,6 @@ def tile_picked_decode2_relu_p_kernel(tc, x_words, x_scales, w1, b1, w2, scl, sh
             nc.sync.dma_start(table[:, 0:U], rows)
             return table
 
-        def load_w2(side, offset):
-            raw = shared.tile([P, PACK, N // 2], F32, name="w2_raw%d" % side, offset=offset)
-            nc.sync.dma_start(raw[:], w2.rearrange("(p j) c -> p j c", j=PACK)[:, :, side * N // 2 : (side + 1) * N // 2])
-            return raw
-
         offs_sb = lists.tile([P, S // GROUP], U16, name="offs_sb")
         rg_sb = lists.tile([P, S // GROUP], U16, name="rg_sb")
         scl_tables, shf_tables = {}, {}
@@ -73,18 +66,18 @@ def tile_picked_decode2_relu_p_kernel(tc, x_words, x_scales, w1, b1, w2, scl, sh
         word_table = keep.tile([P, T], I32, name="word_table")
         nc.sync.dma_start(word_table[:], x_words[0].rearrange("p n t -> p (n t)").bitcast(I32))
 
-        picked_scales = shared.tile([P, 21 * KIB], U8, name="picked_scales", align_bytes=64, offset=0)
+        picked_scales = shared.tile([P, 23 * KIB], U8, name="picked_scales", align_bytes=64, offset=0)
         nc.vector.tensor_copy(out=picked_scales[:, 0:S], in_=scale_table[:].indirect(offs_sb[:]))
         nc.vector.tensor_copy(out=x_plane[:].bitcast(I32), in_=picked_scales[:, 0:S].bitcast(I32))
         for r in range(1, 4):
             nc.sync.dma_start(x_plane[:].bitcast(I32)[r:P:32, :], x_plane[:].bitcast(I32)[8 * r : P : 32, :])
         scl_tables[2] = load_table(scl_rows[2], "scl2", 0, 2 * U)
-        w2_raw = [load_w2(0, 4 * KIB)]
-        shf_tables[0] = load_table(shf_rows[0], "shf0", 8 * KIB)
-        w2_raw.append(load_w2(1, 10 * KIB))
-        scl_tables[3] = load_table(scl_rows[3], "scl3", 14 * KIB)
+        w2_raw = shared.tile([P, PACK, N], F32, name="w2_raw", offset=4 * KIB)
+        nc.sync.dma_start(w2_raw[:], w2.rearrange("(p j) c -> p j c", j=PACK))
+        shf_tables[0] = load_table(shf_rows[0], "shf0", 12 * KIB)
+        scl_tables[3] = load_table(scl_rows[3], "scl3", 14 * KIB, 2 * U)
         for t in range(1, PACK):
-            shf_tables[t] = load_table(shf_rows[t], "shf%d" % t, (14 + 2 * t) * KIB)
+            shf_tables[t] = load_table(shf_rows[t], "shf%d" % t, (16 + 2 * t) * KIB)
 
         def entries(lo, width):
             return rg_sb[:, lo // GROUP : (lo + width) // GROUP]
@@ -109,10 +102,8 @@ def tile_picked_decode2_relu_p_kernel(tc, x_words, x_scales, w1, b1, w2, scl, sh
             nc.vector.tensor_copy(out=codes[:], in_=word_table[:].bitcast(U32).indirect(offs_sb[:, lo // GROUP : (lo + HALF) // GROUP]))
             x_codes.append(codes)
         nc.vector.tensor_copy(out=picked_scl[:, 2, :], in_=scl_tables[2][:].indirect(entries(0, S)))
-        picked_shf0 = keep.tile([P, EARLY + N // 2], F32, name="picked_shf0", align_bytes=64)
-        nc.vector.tensor_copy(out=picked_shf0[:, 0:EARLY], in_=shf_tables[0][:].indirect(rg_sb[:, 0 : EARLY // GROUP]))
 
-        def first_layer(half, h_rows, copy):
+        def first_layer(half, h_rows):
             for t in range(PACK):
                 acc = psum.tile([P, HALF], F32, name="acc", tag="bank%d" % (PACK * half + t))
                 nc.tensor.matmul_mx(
@@ -125,101 +116,85 @@ def tile_picked_decode2_relu_p_kernel(tc, x_words, x_scales, w1, b1, w2, scl, sh
                     stop=True,
                 )
                 nc.scalar.activation(out=h_rows[:, t, :], in_=acc[:], func=RELU, bias=bias[:, t : t + 1])
-            grouped = keep.tile([P, HALF, PACK], BF16, name="h_grouped%d" % half, align_bytes=64)
-            copy(
-                out=grouped[:].rearrange("p (c i) t -> p c t i", i=4),
-                in_=h_rows.rearrange("p t (c i) -> p c t i", i=4),
-            )
+
+        def interleave(half, h_rows, copy):
+            grouped = keep.tile([P, HALF * PACK], BF16, name="h_grouped%d" % half, align_bytes=64)
+            copy(out=grouped[:].rearrange("p (c i t) -> p c t i", i=4, t=PACK), in_=h_rows[:, 0:PACK, :].rearrange("p t (c i) -> p c t i", i=4))
             return grouped
 
-        def quantize_hidden(half, grouped, h_plane):
-            h_codes = keep.tile([P, HALF], U32, name="h_codes%d" % half, align_bytes=64)
-            nc.vector.quantize_mx(out=h_codes[:].bitcast(FP8X4), scales=h_plane[:], in_=grouped[:].rearrange("p n t -> p (n t)"))
-            return h_codes, h_plane
-
+        h_codes = keep.tile([P, S], U32, name="h_codes", align_bytes=64)
+        h_plane = keep.tile([P, S], U8, name="h_plane", align_bytes=64)
         w2_codes = keep.tile([P, N], U32, name="w2_codes", align_bytes=64)
         w2_plane = keep.tile([P, N], U8, name="w2_plane", align_bytes=64)
-        first_staged = shared.tile([P, N], BF16, name="first_staged", align_bytes=64, offset=HOLD)
-        last_staged = shared.tile([P, 2, N], BF16, name="last_staged", align_bytes=64, offset=HOLD + 2048)
-        w2_staged = [first_staged[:], picked_shf0[:, EARLY : EARLY + N // 2].bitcast(BF16), last_staged[:, 0, :], last_staged[:, 1, :]]
-        w2_cols = [raw[:].rearrange("p j (a t b) -> p t a j b", t=PACK, b=RUN) for raw in w2_raw]
+        w2_cols = w2_raw[:].rearrange("p j (a t b) -> p t a j b", t=PACK, b=RUN)
 
-        def quantize_w2(lo, hi, staged):
-            nc.vector.quantize_mx(out=w2_codes[:, lo * P : hi * P].bitcast(FP8X4), scales=w2_plane[:, lo * P : hi * P], in_=staged)
+        def quantize(codes, plane, half, staged):
+            cols = slice(half * HALF, (half + 1) * HALF)
+            nc.vector.quantize_mx(out=codes[:, cols].bitcast(FP8X4), scales=plane[:, cols], in_=staged[:])
 
-        for t in range(PACK):
-            nc.gpsimd.tensor_scalar(
-                out=w2_staged[t][:, 0 : N // 2].rearrange("p (a b j) -> p a b j", b=RUN, j=PACK),
-                in0=w2_cols[0][:, t].rearrange("p a j b -> p a b j"),
-                scalar1=1.0,
-                scalar2=0.0,
-                op0=MULT,
-                op1=ADD,
-            )
-        rows = shared.tile([P, 2 * PACK, HALF], BF16, name="h_rows", offset=ROWS_AT)
-        rows0 = rows[:, 1 : PACK + 1, :]
-        grouped0 = first_layer(0, rows0, nc.scalar.copy)
-        for t in range(2):
-            nc.vector.tensor_copy(out=w2_staged[t][:, N // 2 : N].rearrange("p (a b j) -> p a j b", b=RUN, j=PACK), in_=w2_cols[1][:, t])
-        quantize_w2(0, 1, w2_staged[0])
-        quantize_w2(1, 2, w2_staged[1])
-        hidden = [quantize_hidden(0, grouped0, shared.tile([P, HALF], U8, name="h_plane0", align_bytes=64, offset=HOLD))]
-        nc.vector.tensor_copy(out=last_staged[:, :, N // 2 : N].rearrange("p t (a b j) -> p t a j b", b=RUN, j=PACK), in_=w2_cols[1][:, 2:4])
-        rows1 = rows[:, 0:PACK, :]
-        grouped1 = first_layer(1, rows1, nc.scalar.copy)
+        def cast_w2(pair):
+            staged = keep.tile([P, 2 * N], BF16, name="w2_staged%d" % pair, align_bytes=64)
+            nc.vector.tensor_copy(out=staged[:].rearrange("p (t a b j) -> p t a j b", t=2, b=RUN, j=PACK), in_=w2_cols[:, 2 * pair : 2 * pair + 2])
+            return staged
 
-        def pick_late(table, half, name, offset):
-            picked = shared.tile([P, HALF], F32, name=name, offset=offset)
-            nc.scalar.activation(out=picked[:], in_=table[:].indirect(entries(half * HALF, HALF)), func=COPY)
+        rows0 = keep.tile([P, PACK, HALF], BF16, name="h_rows0")
+        rows1 = shared.tile([P, 4 * PACK, HALF], BF16, name="h_rows1", offset=ROWS_AT)
+        first_layer(0, rows0)
+        first_layer(1, rows1)
+        grouped0 = interleave(0, rows0, nc.vector.tensor_copy)
+        grouped1 = interleave(1, rows1, nc.scalar.copy)
+        staged0 = cast_w2(0)
+        quantize(h_codes, h_plane, 0, grouped0)
+        quantize(w2_codes, w2_plane, 0, staged0)
+        staged1 = cast_w2(1)
+        quantize(h_codes, h_plane, 1, grouped1)
+        quantize(w2_codes, w2_plane, 1, staged1)
+
+        def pick_late(table, name, slot, width):
+            picked = shared.tile([P, S], F32, name=name, offset=ROWS_AT + slot * 2 * KIB)
+            for lo in range(0, S, width):
+                nc.scalar.activation(out=picked[:, lo : lo + width], in_=table[:].indirect(entries(lo, width)), func=COPY)
             return picked
 
-        late_scl, late_shf = [], []
-        for half in range(2):
-            late_scl.append(pick_late(scl_tables[3], half, "picked_scl3_%d" % half, ROWS_AT + 2 * half * KIB))
-            late_shf.append(pick_late(shf_tables[1], half, "picked_shf1_%d" % half, ROWS_AT + (2 * half + 1) * KIB))
+        picked_shf = {0: pick_late(shf_tables[0], "picked_shf0", 0, HALF)}
+        picked_scl3 = pick_late(scl_tables[3], "picked_scl3", 1, S)
+        picked_shf[1] = pick_late(shf_tables[1], "picked_shf1", 2, HALF)
+        picked_shf[3] = pick_late(shf_tables[3], "picked_shf3", 3, HALF)
 
-        zs = {}
+        zs = [keep.tile([P, S], F32, name="z%d" % t) for t in range(PACK)]
+        res = [keep.tile([P, S], F32, name="res%d" % t) for t in range(PACK)]
 
-        def scale(half, t):
-            acc = psum.tile([P, HALF], F32, name="acc", tag="bank%d" % (PACK * half + t))
+        def scale(t, lo, width, bank):
+            span = slice(lo, lo + width)
+            acc = psum.tile([P, width], F32, name="acc", tag="bank%d" % bank)
             nc.tensor.matmul_mx(
                 out=acc[:],
                 lhsT=w2_codes[:, t * P : (t + 1) * P].bitcast(FP8X4),
                 lhsT_scale=w2_plane[:, t * P : (t + 1) * P],
-                rhs=hidden[half][0][:].bitcast(FP8X4),
-                rhs_scale=hidden[half][1][:],
+                rhs=h_codes[:, span].bitcast(FP8X4),
+                rhs_scale=h_plane[:, span],
                 start=True,
                 stop=True,
             )
-            if half == 0 and t < 2:
-                z = shared.tile([P, HALF], F32, name="z0_%d" % t, offset=HOLD + 2048 + t * 1024)
-            else:
-                z = keep.tile([P, HALF], F32, name="z%d_%d" % (half, t))
-            scales = late_scl[half][:] if t == PACK - 1 else picked_scl[:, t, half * HALF : (half + 1) * HALF]
-            nc.vector.tensor_tensor(z[:], acc[:], scales, MULT)
-            zs[half, t] = z
+            scales = picked_scl3[:, span] if t == PACK - 1 else picked_scl[:, t, span]
+            nc.vector.tensor_tensor(zs[t][:, span], acc[:], scales, MULT)
 
-        def shift(half, t, picked=None, engine=nc.vector, width=HALF):
-            res = keep.tile([P, HALF], F32, name="res%d_%d" % (half, t))
-            for lo in range(0, HALF, width):
-                first = half * HALF + lo
-                shifts = shf_tables[t][:].indirect(entries(first, width)) if picked is None else picked
-                engine.tensor_tensor(res[:, lo : lo + width], shifts, zs[half, t][:, lo : lo + width], ADD)
-                nc.sync.dma_start(out_rows[t][:, :, first : first + width], res[:, lo : lo + width])
+        def shift(t, lo, width, engine=nc.vector):
+            span = slice(lo, lo + width)
+            shifts = picked_shf[t][:, span] if t in picked_shf else shf_tables[t][:].indirect(entries(lo, width))
+            engine.tensor_tensor(res[t][:, span], shifts, zs[t][:, span], ADD)
+            nc.sync.dma_start(out_rows[t][:, :, span], res[t][:, span])
 
-        nc.vector.tensor_copy(out=picked_shf0[:, EARLY:S], in_=shf_tables[0][:].indirect(rg_sb[:, EARLY // GROUP : S // GROUP]))
-        quantize_w2(2, 4, last_staged[:].rearrange("p t c -> p (t c)"))
-        for t in range(PACK - 1):
-            scale(0, t)
-        shift(0, 0, picked_shf0[:, 0:HALF], nc.gpsimd)
-        shift(0, 2)
-        hidden.append(quantize_hidden(1, grouped1, keep.tile([P, HALF], U8, name="h_plane1", align_bytes=64)))
-        scale(0, 3)
-        shift(0, 3)
-        for t in range(PACK):
-            scale(1, t)
-        shift(0, 1, late_shf[0][:], nc.gpsimd)
-        shift(1, 0, picked_shf0[:, HALF:S], nc.gpsimd)
-        shift(1, 2)
-        shift(1, 1, late_shf[1][:])
-        shift(1, 3, width=HALF // 2)
+        scale(0, 0, HALF, 0)
+        scale(1, 0, HALF, 1)
+        scale(0, HALF, HALF, 2)
+        scale(1, HALF, HALF, 3)
+        shift(0, 0, HALF, nc.gpsimd)
+        shift(0, HALF, HALF, nc.gpsimd)
+        scale(2, 0, S, 4)
+        scale(3, 0, S, 5)
+        shift(2, 0, HALF)
+        shift(1, 0, S)
+        shift(2, HALF, HALF)
+        shift(3, 0, HALF)
+        shift(3, HALF, HALF)

@@ -66,23 +66,23 @@ def tile_picked_decode2_relu_p_kernel(tc, x_words, x_scales, w1, b1, w2, scl, sh
         word_table = keep.tile([P, T], I32, name="word_table")
         nc.sync.dma_start(word_table[:], x_words[0].rearrange("p n t -> p (n t)").bitcast(I32))
 
-        picked_scales = shared.tile([P, 23 * KIB], U8, name="picked_scales", align_bytes=64, offset=0)
+        scl_tables[2] = load_table(scl_rows[2], "scl2", 56 * KIB)
+
+        picked_scales = shared.tile([P, 21 * KIB], U8, name="picked_scales", align_bytes=64, offset=0)
         nc.vector.tensor_copy(out=picked_scales[:, 0:S], in_=scale_table[:].indirect(offs_sb[:]))
         nc.vector.tensor_copy(out=x_plane[:].bitcast(I32), in_=picked_scales[:, 0:S].bitcast(I32))
         for r in range(1, 4):
             nc.sync.dma_start(x_plane[:].bitcast(I32)[r:P:32, :], x_plane[:].bitcast(I32)[8 * r : P : 32, :])
-        scl_tables[2] = load_table(scl_rows[2], "scl2", 0, 2 * U)
-        w2_raw = shared.tile([P, PACK, N], F32, name="w2_raw", offset=4 * KIB)
+        scl_tables[3] = load_table(scl_rows[3], "scl3", 2 * KIB, 2 * U)
+        w2_raw = shared.tile([P, PACK, N], F32, name="w2_raw", offset=6 * KIB)
         nc.sync.dma_start(w2_raw[:], w2.rearrange("(p j) c -> p j c", j=PACK))
-        shf_tables[0] = load_table(shf_rows[0], "shf0", 12 * KIB)
-        scl_tables[3] = load_table(scl_rows[3], "scl3", 14 * KIB, 2 * U)
-        for t in range(1, PACK):
-            shf_tables[t] = load_table(shf_rows[t], "shf%d" % t, (16 + 2 * t) * KIB)
+        for t in range(PACK):
+            shf_tables[t] = load_table(shf_rows[t], "shf%d" % t, (14 + 2 * t) * KIB)
 
         def entries(lo, width):
             return rg_sb[:, lo // GROUP : (lo + width) // GROUP]
 
-        picked_scl = keep.tile([P, PACK - 1, S], F32, name="picked_scl")
+        picked_scl = keep.tile([P, PACK, S], F32, name="picked_scl")
         for t in range(2):
             nc.scalar.activation(out=picked_scl[:, t, :], in_=scl_tables[t][:].indirect(entries(0, S)), func=COPY)
 
@@ -101,7 +101,9 @@ def tile_picked_decode2_relu_p_kernel(tc, x_words, x_scales, w1, b1, w2, scl, sh
             codes = keep.tile([P, HALF], U32, name="x_codes%d" % lo, align_bytes=64)
             nc.vector.tensor_copy(out=codes[:], in_=word_table[:].bitcast(U32).indirect(offs_sb[:, lo // GROUP : (lo + HALF) // GROUP]))
             x_codes.append(codes)
-        nc.vector.tensor_copy(out=picked_scl[:, 2, :], in_=scl_tables[2][:].indirect(entries(0, S)))
+        nc.scalar.activation(out=picked_scl[:, 2, 0:HALF], in_=scl_tables[2][:].indirect(entries(0, HALF)), func=COPY)
+        nc.vector.tensor_copy(out=picked_scl[:, 2, HALF:S], in_=scl_tables[2][:].indirect(entries(HALF, HALF)))
+        nc.vector.tensor_copy(out=picked_scl[:, 3, :], in_=scl_tables[3][:].indirect(entries(0, S)))
 
         def first_layer(half, h_rows):
             for t in range(PACK):
@@ -150,16 +152,13 @@ def tile_picked_decode2_relu_p_kernel(tc, x_words, x_scales, w1, b1, w2, scl, sh
         quantize(h_codes, h_plane, 1, grouped1)
         quantize(w2_codes, w2_plane, 1, staged1)
 
-        def pick_late(table, name, slot, width):
+        def pick_late(table, name, slot, width, count=S):
             picked = shared.tile([P, S], F32, name=name, offset=ROWS_AT + slot * 2 * KIB)
-            for lo in range(0, S, width):
+            for lo in range(0, count, width):
                 nc.scalar.activation(out=picked[:, lo : lo + width], in_=table[:].indirect(entries(lo, width)), func=COPY)
             return picked
 
-        picked_shf = {0: pick_late(shf_tables[0], "picked_shf0", 0, HALF)}
-        picked_scl3 = pick_late(scl_tables[3], "picked_scl3", 1, S)
-        picked_shf[1] = pick_late(shf_tables[1], "picked_shf1", 2, HALF)
-        picked_shf[3] = pick_late(shf_tables[3], "picked_shf3", 3, HALF)
+        picked_shf = [pick_late(shf_tables[t], "picked_shf%d" % t, t, HALF, HALF if t == PACK - 1 else S) for t in range(PACK)]
 
         zs = [keep.tile([P, S], F32, name="z%d" % t) for t in range(PACK)]
         res = [keep.tile([P, S], F32, name="res%d" % t) for t in range(PACK)]
@@ -176,12 +175,11 @@ def tile_picked_decode2_relu_p_kernel(tc, x_words, x_scales, w1, b1, w2, scl, sh
                 start=True,
                 stop=True,
             )
-            scales = picked_scl3[:, span] if t == PACK - 1 else picked_scl[:, t, span]
-            nc.vector.tensor_tensor(zs[t][:, span], acc[:], scales, MULT)
+            nc.vector.tensor_tensor(zs[t][:, span], acc[:], picked_scl[:, t, span], MULT)
 
-        def shift(t, lo, width, engine=nc.vector):
+        def shift(t, lo, width, engine=nc.vector, fused=False):
             span = slice(lo, lo + width)
-            shifts = picked_shf[t][:, span] if t in picked_shf else shf_tables[t][:].indirect(entries(lo, width))
+            shifts = shf_tables[t][:].indirect(entries(lo, width)) if fused else picked_shf[t][:, span]
             engine.tensor_tensor(res[t][:, span], shifts, zs[t][:, span], ADD)
             nc.sync.dma_start(out_rows[t][:, :, span], res[t][:, span])
 
@@ -191,10 +189,12 @@ def tile_picked_decode2_relu_p_kernel(tc, x_words, x_scales, w1, b1, w2, scl, sh
         scale(1, HALF, HALF, 3)
         shift(0, 0, HALF, nc.gpsimd)
         shift(0, HALF, HALF, nc.gpsimd)
+        shift(1, 0, HALF, nc.gpsimd)
         scale(2, 0, S, 4)
         scale(3, 0, S, 5)
+        shift(1, HALF, HALF)
+        shift(3, HALF, HALF, fused=True)
         shift(2, 0, HALF)
-        shift(1, 0, S)
         shift(2, HALF, HALF)
-        shift(3, 0, HALF)
-        shift(3, HALF, HALF)
+        shift(3, 0, HALF // 2)
+        shift(3, HALF // 2, HALF // 2)

@@ -60,31 +60,32 @@ def tile_picked_decode2_relu_p_kernel(tc, x_words, x_scales, w1, b1, w2, scl, sh
         nc.sync.dma_start(rg_sb[:], rg)
         nc.sync.dma_start(offs_sb[:], offs)
         nc.sync.dma_start(scale_table[:].bitcast(I32)[0:P:8, :], x_scales[0].bitcast(I32))
-        scl_tables[1] = load_table(scl_rows[1], "scl1", 52 * KIB, 2 * U)
-        w1_raw = keep.tile([P, PACK, H], F32, name="w1_raw")
+        scl_tables[1] = load_table(scl_rows[1], "scl1", 8 * KIB, 4 * U)
+        w1_raw = shared.tile([P, PACK, H], F32, name="w1_raw", offset=20 * KIB)
         nc.sync.dma_start(w1_raw[:], w1.rearrange("(p j) c -> p j c", j=PACK))
         word_table = keep.tile([P, T], I32, name="word_table")
         nc.sync.dma_start(word_table[:], x_words[0].rearrange("p n t -> p (n t)").bitcast(I32))
 
         scl_tables[2] = load_table(scl_rows[2], "scl2", 56 * KIB)
 
-        picked_scales = shared.tile([P, 21 * KIB], U8, name="picked_scales", align_bytes=64, offset=0)
+        picked_scales = shared.tile([P, S], U8, name="picked_scales", align_bytes=64, offset=60 * KIB)
         nc.vector.tensor_copy(out=picked_scales[:, 0:S], in_=scale_table[:].indirect(offs_sb[:]))
         nc.vector.tensor_copy(out=x_plane[:].bitcast(I32), in_=picked_scales[:, 0:S].bitcast(I32))
         for r in range(1, 4):
-            nc.sync.dma_start(x_plane[:].bitcast(I32)[r:P:32, :], x_plane[:].bitcast(I32)[8 * r : P : 32, :])
-        scl_tables[3] = load_table(scl_rows[3], "scl3", 2 * KIB, 2 * U)
-        w2_raw = shared.tile([P, PACK, N], F32, name="w2_raw", offset=6 * KIB)
+            nc.scalar.dma_start(x_plane[:].bitcast(I32)[r:P:32, :], x_plane[:].bitcast(I32)[8 * r : P : 32, :])
+        scl_tables[3] = load_table(scl_rows[3], "scl3", 9 * KIB, 2 * U)
+        w2_raw = shared.tile([P, PACK, N], F32, name="w2_raw", offset=1 * KIB)
         nc.sync.dma_start(w2_raw[:], w2.rearrange("(p j) c -> p j c", j=PACK))
         for t in range(PACK):
-            shf_tables[t] = load_table(shf_rows[t], "shf%d" % t, (14 + 2 * t) * KIB)
+            shf_tables[t] = load_table(shf_rows[t], "shf%d" % t, (13, 15, 20, 22)[t] * KIB)
 
         def entries(lo, width):
             return rg_sb[:, lo // GROUP : (lo + width) // GROUP]
 
-        picked_scl = keep.tile([P, PACK, S], F32, name="picked_scl")
-        for t in range(2):
-            nc.scalar.activation(out=picked_scl[:, t, :], in_=scl_tables[t][:].indirect(entries(0, S)), func=COPY)
+        picked_scl = {t: keep.tile([P, S], F32, name="picked_scl%d" % t) for t in (0, 2, 3)}
+        picked_scl[1] = shared.tile([P, S], F32, name="picked_scl1", offset=60 * KIB)
+        nc.scalar.activation(out=picked_scl[0][:], in_=scl_tables[0][:].indirect(entries(0, S)), func=COPY)
+        nc.vector.tensor_copy(out=picked_scl[1][:], in_=scl_tables[1][:].indirect(entries(0, S)))
 
         w1_grouped = keep.tile([P, PACK * H], BF16, name="w1_grouped", align_bytes=64)
         dst = w1_grouped[:].rearrange("p (t m j) -> p m j t", t=PACK, j=PACK)
@@ -101,9 +102,9 @@ def tile_picked_decode2_relu_p_kernel(tc, x_words, x_scales, w1, b1, w2, scl, sh
             codes = keep.tile([P, HALF], U32, name="x_codes%d" % lo, align_bytes=64)
             nc.vector.tensor_copy(out=codes[:], in_=word_table[:].bitcast(U32).indirect(offs_sb[:, lo // GROUP : (lo + HALF) // GROUP]))
             x_codes.append(codes)
-        nc.scalar.activation(out=picked_scl[:, 2, 0:HALF], in_=scl_tables[2][:].indirect(entries(0, HALF)), func=COPY)
-        nc.vector.tensor_copy(out=picked_scl[:, 2, HALF:S], in_=scl_tables[2][:].indirect(entries(HALF, HALF)))
-        nc.vector.tensor_copy(out=picked_scl[:, 3, :], in_=scl_tables[3][:].indirect(entries(0, S)))
+        nc.scalar.activation(out=picked_scl[2][:, 0:HALF], in_=scl_tables[2][:].indirect(entries(0, HALF)), func=COPY)
+        nc.vector.tensor_copy(out=picked_scl[2][:, HALF:S], in_=scl_tables[2][:].indirect(entries(HALF, HALF)))
+        nc.vector.tensor_copy(out=picked_scl[3][:], in_=scl_tables[3][:].indirect(entries(0, S)))
 
         def first_layer(half, h_rows):
             for t in range(PACK):
@@ -152,20 +153,17 @@ def tile_picked_decode2_relu_p_kernel(tc, x_words, x_scales, w1, b1, w2, scl, sh
         quantize(h_codes, h_plane, 1, grouped1)
         quantize(w2_codes, w2_plane, 1, staged1)
 
-        def pick_late(table, name, slot, width, count=S):
-            picked = shared.tile([P, S], F32, name=name, offset=ROWS_AT + slot * 2 * KIB)
-            for lo in range(0, count, width):
-                nc.scalar.activation(out=picked[:, lo : lo + width], in_=table[:].indirect(entries(lo, width)), func=COPY)
-            return picked
-
-        picked_shf = [pick_late(shf_tables[t], "picked_shf%d" % t, t, HALF, HALF if t == PACK - 1 else S) for t in range(PACK)]
+        picked_shf = [shared.tile([P, S], F32, name="picked_shf%d" % t, offset=ROWS_AT + t * 2 * KIB) for t in range(PACK)]
+        for t, half in ((0, 0), (1, 0), (0, 1), (1, 1), (2, 0), (2, 1), (3, 0)):
+            lo = half * HALF
+            nc.scalar.activation(out=picked_shf[t][:, lo : lo + HALF], in_=shf_tables[t][:].indirect(entries(lo, HALF)), func=COPY)
 
         zs = [keep.tile([P, S], F32, name="z%d" % t) for t in range(PACK)]
         res = [keep.tile([P, S], F32, name="res%d" % t) for t in range(PACK)]
 
-        def scale(t, lo, width, bank):
-            span = slice(lo, lo + width)
-            acc = psum.tile([P, width], F32, name="acc", tag="bank%d" % bank)
+        def scale(t, half):
+            span = slice(half * HALF, (half + 1) * HALF)
+            acc = psum.tile([P, HALF], F32, name="acc", tag="bank%d" % (PACK * half + t))
             nc.tensor.matmul_mx(
                 out=acc[:],
                 lhsT=w2_codes[:, t * P : (t + 1) * P].bitcast(FP8X4),
@@ -175,26 +173,31 @@ def tile_picked_decode2_relu_p_kernel(tc, x_words, x_scales, w1, b1, w2, scl, sh
                 start=True,
                 stop=True,
             )
-            nc.vector.tensor_tensor(zs[t][:, span], acc[:], picked_scl[:, t, span], MULT)
+            nc.vector.tensor_tensor(zs[t][:, span], acc[:], picked_scl[t][:, span], MULT)
 
-        def shift(t, lo, width, engine=nc.vector, fused=False):
+        def add(t, lo, width, engine=nc.vector, fused=False):
             span = slice(lo, lo + width)
             shifts = shf_tables[t][:].indirect(entries(lo, width)) if fused else picked_shf[t][:, span]
             engine.tensor_tensor(res[t][:, span], shifts, zs[t][:, span], ADD)
-            nc.sync.dma_start(out_rows[t][:, :, span], res[t][:, span])
 
-        scale(0, 0, HALF, 0)
-        scale(1, 0, HALF, 1)
-        scale(0, HALF, HALF, 2)
-        scale(1, HALF, HALF, 3)
+        def store(t, lo, width):
+            nc.sync.dma_start(out_rows[t][:, :, lo : lo + width], res[t][:, lo : lo + width])
+
+        def shift(t, lo, width, engine=nc.vector, fused=False):
+            add(t, lo, width, engine, fused)
+            store(t, lo, width)
+
+        for half in range(2):
+            for t in range(PACK):
+                scale(t, half)
         shift(0, 0, HALF, nc.gpsimd)
-        shift(0, HALF, HALF, nc.gpsimd)
         shift(1, 0, HALF, nc.gpsimd)
-        scale(2, 0, S, 4)
-        scale(3, 0, S, 5)
+        add(0, HALF, P, nc.gpsimd)
         shift(1, HALF, HALF)
+        add(0, HALF + P, P)
+        store(0, HALF, HALF)
         shift(3, HALF, HALF, fused=True)
         shift(2, 0, HALF)
         shift(2, HALF, HALF)
-        shift(3, 0, HALF // 2)
-        shift(3, HALF // 2, HALF // 2)
+        shift(3, 0, P)
+        shift(3, P, P)

@@ -43,10 +43,6 @@ def tile_picked_decode2_relu_p_kernel(tc, x_words, x_scales, w1, b1, w2, scl, sh
         nc.vector.memset(scale_table[:].bitcast(I32), 0)
         x_plane = keep.tile([P, S], U8, name="x_plane", align_bytes=64)
 
-        bias = keep.tile([P, PACK], F32, name="bias")
-        nc.scalar.dma_start(bias[:], b1.rearrange("(p t) o -> p (t o)", t=PACK))
-        warm_out = keep.tile([P, PACK], F32, name="warm_out")
-        nc.scalar.activation(out=warm_out[:], in_=bias[:], func=RELU)
 
         def load_table(rows, name, offset, cols=U):
             table = shared.tile([P, cols], F32, name=name, offset=offset)
@@ -56,50 +52,52 @@ def tile_picked_decode2_relu_p_kernel(tc, x_words, x_scales, w1, b1, w2, scl, sh
         offs_sb = lists.tile([P, S // GROUP], U16, name="offs_sb")
         rg_sb = lists.tile([P, S // GROUP], U16, name="rg_sb")
         scl_tables, shf_tables = {}, {}
-        scl_tables[0] = load_table(scl_rows[0], "scl0", 48 * KIB, 2 * U)
-        nc.sync.dma_start(rg_sb[:], rg)
+        scl_tables[1] = load_table(scl_rows[1], "scl1", 52 * KIB, 2 * U)
         nc.sync.dma_start(offs_sb[:], offs)
+        nc.sync.dma_start(rg_sb[:], rg)
         nc.sync.dma_start(scale_table[:].bitcast(I32)[0:P:8, :], x_scales[0].bitcast(I32))
-        scl_tables[1] = load_table(scl_rows[1], "scl1", 8 * KIB, 4 * U)
-        w1_raw = shared.tile([P, PACK, H], F32, name="w1_raw", offset=20 * KIB)
+        scl_tables[0] = load_table(scl_rows[0], "scl0", 48 * KIB, 2 * U)
+        w1_raw = shared.tile([P, PACK, H], F32, name="w1_raw", offset=28 * KIB)
         nc.sync.dma_start(w1_raw[:], w1.rearrange("(p j) c -> p j c", j=PACK))
         word_table = keep.tile([P, T], I32, name="word_table")
         nc.sync.dma_start(word_table[:], x_words[0].rearrange("p n t -> p (n t)").bitcast(I32))
-
         scl_tables[2] = load_table(scl_rows[2], "scl2", 56 * KIB)
 
-        picked_scales = shared.tile([P, S], U8, name="picked_scales", align_bytes=64, offset=60 * KIB)
+        picked_scales = shared.tile([P, 24 * KIB], U8, name="picked_scales", align_bytes=64, offset=0)
         nc.vector.tensor_copy(out=picked_scales[:, 0:S], in_=scale_table[:].indirect(offs_sb[:]))
         nc.vector.tensor_copy(out=x_plane[:].bitcast(I32), in_=picked_scales[:, 0:S].bitcast(I32))
         for r in range(1, 4):
-            nc.scalar.dma_start(x_plane[:].bitcast(I32)[r:P:32, :], x_plane[:].bitcast(I32)[8 * r : P : 32, :])
-        scl_tables[3] = load_table(scl_rows[3], "scl3", 9 * KIB, 2 * U)
-        w2_raw = shared.tile([P, PACK, N], F32, name="w2_raw", offset=1 * KIB)
+            nc.sync.dma_start(x_plane[:].bitcast(I32)[r:P:32, :], x_plane[:].bitcast(I32)[8 * r : P : 32, :])
+        bias = shared.tile([P, PACK], F32, name="bias", offset=23 * KIB)
+        nc.sync.dma_start(bias[:], b1.rearrange("(p t) o -> p (t o)", t=PACK))
+        scl_tables[3] = load_table(scl_rows[3], "scl3", 2 * KIB, 2 * U)
+        w2_raw = shared.tile([P, PACK, N], F32, name="w2_raw", offset=6 * KIB)
         nc.sync.dma_start(w2_raw[:], w2.rearrange("(p j) c -> p j c", j=PACK))
         for t in range(PACK):
-            shf_tables[t] = load_table(shf_rows[t], "shf%d" % t, (13, 15, 20, 22)[t] * KIB)
+            shf_tables[t] = load_table(shf_rows[t], "shf%d" % t, (14 + 2 * t) * KIB)
 
         def entries(lo, width):
             return rg_sb[:, lo // GROUP : (lo + width) // GROUP]
 
-        picked_scl = {t: keep.tile([P, S], F32, name="picked_scl%d" % t) for t in (0, 2, 3)}
-        picked_scl[1] = shared.tile([P, S], F32, name="picked_scl1", offset=60 * KIB)
-        nc.scalar.activation(out=picked_scl[0][:], in_=scl_tables[0][:].indirect(entries(0, S)), func=COPY)
+        picked_scl = {t: shared.tile([P, S], F32, name="picked_scl%d" % t, offset=(58 + 2 * t) * KIB) for t in (2, 3)}
+        picked_scl[1] = shared.tile([P, S], F32, name="picked_scl1", offset=0)
         nc.vector.tensor_copy(out=picked_scl[1][:], in_=scl_tables[1][:].indirect(entries(0, S)))
 
-        w1_grouped = keep.tile([P, PACK * H], BF16, name="w1_grouped", align_bytes=64)
-        dst = w1_grouped[:].rearrange("p (t m j) -> p m j t", t=PACK, j=PACK)
+        w1_grouped = shared.tile([P, 6 * H], BF16, name="w1_grouped", align_bytes=64, offset=60 * KIB)
+        dst = w1_grouped[:, 0 : PACK * H].rearrange("p (t m j) -> p m j t", t=PACK, j=PACK)
         src = w1_raw[:].rearrange("p j (m t) -> p m j t", t=PACK)
         nc.vector.tensor_copy(out=dst[:, :, :, 0:2], in_=src[:, :, :, 0:2])
         nc.vector.tensor_copy(out=dst[:, 0:W1_VECTOR_EXTRA, :, 2:4], in_=src[:, 0:W1_VECTOR_EXTRA, :, 2:4])
-        nc.scalar.copy(out=dst[:, W1_VECTOR_EXTRA:P, :, 2:4], in_=src[:, W1_VECTOR_EXTRA:P, :, 2:4])
+        nc.scalar.activation(out=dst[:, W1_VECTOR_EXTRA:P, :, 2:4], in_=src[:, W1_VECTOR_EXTRA:P, :, 2:4], func=COPY)
+        picked_scl[0] = shared.tile([P, S], F32, name="picked_scl0", offset=28 * KIB)
+        nc.scalar.activation(out=picked_scl[0][:], in_=scl_tables[0][:].indirect(entries(0, S)), func=COPY)
         w1_codes = keep.tile([P, H], U32, name="w1_codes", align_bytes=64)
         w1_plane = keep.tile([P, H], U8, name="w1_plane", align_bytes=64)
-        nc.vector.quantize_mx(out=w1_codes[:].bitcast(FP8X4), scales=w1_plane[:], in_=w1_grouped[:])
+        nc.vector.quantize_mx(out=w1_codes[:].bitcast(FP8X4), scales=w1_plane[:], in_=w1_grouped[:, 0 : PACK * H])
 
         x_codes = []
         for lo in (0, HALF):
-            codes = keep.tile([P, HALF], U32, name="x_codes%d" % lo, align_bytes=64)
+            codes = shared.tile([P, HALF], U32, name="x_codes%d" % lo, align_bytes=64, offset=60 * KIB + 4 * lo)
             nc.vector.tensor_copy(out=codes[:], in_=word_table[:].bitcast(U32).indirect(offs_sb[:, lo // GROUP : (lo + HALF) // GROUP]))
             x_codes.append(codes)
         nc.scalar.activation(out=picked_scl[2][:, 0:HALF], in_=scl_tables[2][:].indirect(entries(0, HALF)), func=COPY)

@@ -52,11 +52,11 @@ def tile_picked_decode2_relu_p_kernel(tc, x_words, x_scales, w1, b1, w2, scl, sh
         offs_sb = lists.tile([P, S // GROUP], U16, name="offs_sb")
         rg_sb = lists.tile([P, S // GROUP], U16, name="rg_sb")
         scl_tables, shf_tables = {}, {}
-        scl_tables[1] = load_table(scl_rows[1], "scl1", 52 * KIB, 2 * U)
-        nc.sync.dma_start(offs_sb[:], offs)
+        scl_tables[1] = load_table(scl_rows[1], "scl1", 52 * KIB)
         nc.sync.dma_start(rg_sb[:], rg)
-        nc.sync.dma_start(scale_table[:].bitcast(I32)[0:P:8, :], x_scales[0].bitcast(I32))
+        nc.sync.dma_start(offs_sb[:], offs)
         scl_tables[0] = load_table(scl_rows[0], "scl0", 48 * KIB, 2 * U)
+        nc.sync.dma_start(scale_table[:].bitcast(I32)[0:P:8, :], x_scales[0].bitcast(I32))
         w1_raw = shared.tile([P, PACK, H], F32, name="w1_raw", offset=28 * KIB)
         nc.sync.dma_start(w1_raw[:], w1.rearrange("(p j) c -> p j c", j=PACK))
         word_table = keep.tile([P, T], I32, name="word_table")
@@ -80,8 +80,9 @@ def tile_picked_decode2_relu_p_kernel(tc, x_words, x_scales, w1, b1, w2, scl, sh
             return rg_sb[:, lo // GROUP : (lo + width) // GROUP]
 
         picked_scl = {t: shared.tile([P, S], F32, name="picked_scl%d" % t, offset=(58 + 2 * t) * KIB) for t in (2, 3)}
-        picked_scl[1] = shared.tile([P, S], F32, name="picked_scl1", offset=0)
-        nc.vector.tensor_copy(out=picked_scl[1][:], in_=scl_tables[1][:].indirect(entries(0, S)))
+        scl1_halves = [keep.tile([P, HALF], F32, name="picked_scl1_0"), shared.tile([P, HALF], F32, name="picked_scl1_1", offset=22 * KIB)]
+        for half in range(2):
+            nc.vector.tensor_copy(out=scl1_halves[half][:], in_=scl_tables[1][:].indirect(entries(half * HALF, HALF)))
 
         w1_grouped = shared.tile([P, 6 * H], BF16, name="w1_grouped", align_bytes=64, offset=60 * KIB)
         dst = w1_grouped[:, 0 : PACK * H].rearrange("p (t m j) -> p m j t", t=PACK, j=PACK)
@@ -118,42 +119,42 @@ def tile_picked_decode2_relu_p_kernel(tc, x_words, x_scales, w1, b1, w2, scl, sh
                 )
                 nc.scalar.activation(out=h_rows[:, t, :], in_=acc[:], func=RELU, bias=bias[:, t : t + 1])
 
-        def interleave(half, h_rows, copy):
-            grouped = keep.tile([P, HALF * PACK], BF16, name="h_grouped%d" % half, align_bytes=64)
+        def interleave(grouped, h_rows, copy):
             copy(out=grouped[:].rearrange("p (c i t) -> p c t i", i=4, t=PACK), in_=h_rows[:, 0:PACK, :].rearrange("p t (c i) -> p c t i", i=4))
-            return grouped
 
-        h_codes = keep.tile([P, S], U32, name="h_codes", align_bytes=64)
-        h_plane = keep.tile([P, S], U8, name="h_plane", align_bytes=64)
-        w2_codes = keep.tile([P, N], U32, name="w2_codes", align_bytes=64)
-        w2_plane = keep.tile([P, N], U8, name="w2_plane", align_bytes=64)
+        def quantize(staged, name, plane):
+            codes = keep.tile([P, HALF], U32, name=name, align_bytes=64)
+            nc.vector.quantize_mx(out=codes[:].bitcast(FP8X4), scales=plane[:], in_=staged[:, 0 : HALF * PACK])
+            return codes, plane
+
+        def new_plane(name):
+            return keep.tile([P, HALF], U8, name=name, align_bytes=64)
+
         w2_cols = w2_raw[:].rearrange("p j (a t b) -> p t a j b", t=PACK, b=RUN)
 
-        def quantize(codes, plane, half, staged):
-            cols = slice(half * HALF, (half + 1) * HALF)
-            nc.vector.quantize_mx(out=codes[:, cols].bitcast(FP8X4), scales=plane[:, cols], in_=staged[:])
-
-        def cast_w2(pair):
-            staged = keep.tile([P, 2 * N], BF16, name="w2_staged%d" % pair, align_bytes=64)
-            nc.vector.tensor_copy(out=staged[:].rearrange("p (t a b j) -> p t a j b", t=2, b=RUN, j=PACK), in_=w2_cols[:, 2 * pair : 2 * pair + 2])
-            return staged
+        def cast_w2(staged, pair):
+            nc.vector.tensor_copy(out=staged[:, 0 : 2 * N].rearrange("p (t a b j) -> p t a j b", t=2, b=RUN, j=PACK), in_=w2_cols[:, 2 * pair : 2 * pair + 2])
 
         rows0 = keep.tile([P, PACK, HALF], BF16, name="h_rows0")
         rows1 = shared.tile([P, 4 * PACK, HALF], BF16, name="h_rows1", offset=ROWS_AT)
         first_layer(0, rows0)
         first_layer(1, rows1)
-        grouped0 = interleave(0, rows0, nc.vector.tensor_copy)
-        grouped1 = interleave(1, rows1, nc.scalar.copy)
-        staged0 = cast_w2(0)
-        quantize(h_codes, h_plane, 0, grouped0)
-        quantize(w2_codes, w2_plane, 0, staged0)
-        staged1 = cast_w2(1)
-        quantize(h_codes, h_plane, 1, grouped1)
-        quantize(w2_codes, w2_plane, 1, staged1)
+        grouped0 = keep.tile([P, HALF * PACK], BF16, name="h_grouped0", align_bytes=64)
+        grouped1 = keep.tile([P, HALF * PACK], BF16, name="h_grouped1", align_bytes=64)
+        staged0 = keep.tile([P, 2 * N], BF16, name="w2_staged0", align_bytes=64)
+        staged1 = keep.tile([P, 2 * N], BF16, name="w2_staged1", align_bytes=64)
+        interleave(grouped0, rows0, nc.vector.tensor_copy)
+        interleave(grouped1, rows1, nc.scalar.copy)
+        cast_w2(staged0, 0)
+        hidden = [quantize(grouped0, "h_codes0", new_plane("h_plane0"))]
+        weights = [quantize(staged0, "w2_codes0", new_plane("w2_plane0"))]
+        cast_w2(staged1, 1)
+        hidden.append(quantize(grouped1, "h_codes1", new_plane("h_plane1")))
+        weights.append(quantize(staged1, "w2_codes1", new_plane("w2_plane1")))
 
         picked_shf = [shared.tile([P, S], F32, name="picked_shf%d" % t, offset=ROWS_AT + t * 2 * KIB) for t in range(PACK)]
-        for t, half in ((0, 0), (1, 0), (0, 1), (1, 1), (2, 0), (2, 1), (3, 0)):
-            lo = half * HALF
+        for lo in range(0, PACK * S - HALF, HALF):
+            t, lo = divmod(lo, S)
             nc.scalar.activation(out=picked_shf[t][:, lo : lo + HALF], in_=shf_tables[t][:].indirect(entries(lo, HALF)), func=COPY)
 
         zs = [keep.tile([P, S], F32, name="z%d" % t) for t in range(PACK)]
@@ -161,17 +162,18 @@ def tile_picked_decode2_relu_p_kernel(tc, x_words, x_scales, w1, b1, w2, scl, sh
 
         def scale(t, half):
             span = slice(half * HALF, (half + 1) * HALF)
+            cols = slice(t % 2 * P, (t % 2 + 1) * P)
             acc = psum.tile([P, HALF], F32, name="acc", tag="bank%d" % (PACK * half + t))
             nc.tensor.matmul_mx(
                 out=acc[:],
-                lhsT=w2_codes[:, t * P : (t + 1) * P].bitcast(FP8X4),
-                lhsT_scale=w2_plane[:, t * P : (t + 1) * P],
-                rhs=h_codes[:, span].bitcast(FP8X4),
-                rhs_scale=h_plane[:, span],
+                lhsT=weights[t // 2][0][:, cols].bitcast(FP8X4),
+                lhsT_scale=weights[t // 2][1][:, cols],
+                rhs=hidden[half][0][:].bitcast(FP8X4),
+                rhs_scale=hidden[half][1][:],
                 start=True,
                 stop=True,
             )
-            nc.vector.tensor_tensor(zs[t][:, span], acc[:], picked_scl[t][:, span], MULT)
+            nc.vector.tensor_tensor(zs[t][:, span], acc[:], scl1_halves[half][:] if t == 1 else picked_scl[t][:, span], MULT)
 
         def add(t, lo, width, engine=nc.vector, fused=False):
             span = slice(lo, lo + width)
@@ -185,15 +187,16 @@ def tile_picked_decode2_relu_p_kernel(tc, x_words, x_scales, w1, b1, w2, scl, sh
             add(t, lo, width, engine, fused)
             store(t, lo, width)
 
-        for half in range(2):
-            for t in range(PACK):
-                scale(t, half)
+        for pair in range(2):
+            for half in range(2):
+                scale(2 * pair, half)
+                scale(2 * pair + 1, half)
         shift(0, 0, HALF, nc.gpsimd)
-        shift(1, 0, HALF, nc.gpsimd)
-        add(0, HALF, P, nc.gpsimd)
+        shift(0, HALF, HALF, nc.gpsimd)
+        add(1, 0, P, nc.gpsimd)
         shift(1, HALF, HALF)
-        add(0, HALF + P, P)
-        store(0, HALF, HALF)
+        add(1, P, P)
+        store(1, 0, HALF)
         shift(3, HALF, HALF, fused=True)
         shift(2, 0, HALF)
         shift(2, HALF, HALF)

@@ -70,7 +70,7 @@ def tile_picked_decode2_relu_p_kernel(tc, x_words, x_scales, w1, b1, w2, scl, sh
             nc.sync.dma_start(x_plane[:].bitcast(I32)[r:P:32, :], x_plane[:].bitcast(I32)[8 * r : P : 32, :])
         bias = shared.tile([P, PACK], F32, name="bias", offset=23 * KIB)
         nc.sync.dma_start(bias[:], b1.rearrange("(p t) o -> p (t o)", t=PACK))
-        scl_tables[3] = load_table(scl_rows[3], "scl3", 2 * KIB, 2 * U)
+        scl_tables[3] = load_table(scl_rows[3], "scl3", 2 * KIB)
         w2_raw = shared.tile([P, PACK, N], F32, name="w2_raw", offset=6 * KIB)
         nc.sync.dma_start(w2_raw[:], w2.rearrange("(p j) c -> p j c", j=PACK))
         for t in range(PACK):
@@ -103,7 +103,7 @@ def tile_picked_decode2_relu_p_kernel(tc, x_words, x_scales, w1, b1, w2, scl, sh
             x_codes.append(codes)
         nc.scalar.activation(out=picked_scl[2][:, 0:HALF], in_=scl_tables[2][:].indirect(entries(0, HALF)), func=COPY)
         nc.vector.tensor_copy(out=picked_scl[2][:, HALF:S], in_=scl_tables[2][:].indirect(entries(HALF, HALF)))
-        nc.vector.tensor_copy(out=picked_scl[3][:], in_=scl_tables[3][:].indirect(entries(0, S)))
+        nc.vector.tensor_copy(out=picked_scl[3][:, 0 : S - P], in_=scl_tables[3][:].indirect(entries(0, S - P)))
 
         def first_layer(half, h_rows):
             for t in range(PACK):
@@ -139,12 +139,14 @@ def tile_picked_decode2_relu_p_kernel(tc, x_words, x_scales, w1, b1, w2, scl, sh
         rows1 = shared.tile([P, 4 * PACK, HALF], BF16, name="h_rows1", offset=ROWS_AT)
         first_layer(0, rows0)
         first_layer(1, rows1)
+        scl3_last = shared.tile([P, P], F32, name="scl3_last", offset=60 * KIB + 4 * HALF)
         grouped0 = keep.tile([P, HALF * PACK], BF16, name="h_grouped0", align_bytes=64)
         grouped1 = keep.tile([P, HALF * PACK], BF16, name="h_grouped1", align_bytes=64)
         staged0 = keep.tile([P, 2 * N], BF16, name="w2_staged0", align_bytes=64)
         staged1 = keep.tile([P, 2 * N], BF16, name="w2_staged1", align_bytes=64)
         interleave(grouped0, rows0, nc.vector.tensor_copy)
         interleave(grouped1, rows1, nc.scalar.copy)
+        nc.scalar.activation(out=scl3_last[:], in_=scl_tables[3][:].indirect(entries(S - P, P)), func=COPY)
         cast_w2(staged0, 0)
         hidden = [quantize(grouped0, "h_codes0", new_plane("h_plane0"))]
         weights = [quantize(staged0, "w2_codes0", new_plane("w2_plane0"))]
@@ -173,7 +175,11 @@ def tile_picked_decode2_relu_p_kernel(tc, x_words, x_scales, w1, b1, w2, scl, sh
                 start=True,
                 stop=True,
             )
-            nc.vector.tensor_tensor(zs[t][:, span], acc[:], scl1_halves[half][:] if t == 1 else picked_scl[t][:, span], MULT)
+            if (t, half) == (PACK - 1, 1):
+                nc.vector.tensor_tensor(zs[t][:, HALF : S - P], acc[:, 0:P], picked_scl[t][:, HALF : S - P], MULT)
+                nc.vector.tensor_tensor(zs[t][:, S - P : S], acc[:, P:HALF], scl3_last[:], MULT)
+            else:
+                nc.vector.tensor_tensor(zs[t][:, span], acc[:], scl1_halves[half][:] if t == 1 else picked_scl[t][:, span], MULT)
 
         def add(t, lo, width, engine=nc.vector, fused=False):
             span = slice(lo, lo + width)

@@ -140,7 +140,7 @@ def tile_picked_decode2_relu_p_kernel(tc, x_words, x_scales, w1, b1, w2, scl, sh
         first_layer(0, rows0)
         first_layer(1, rows1)
         scl3_last = shared.tile([P, P], F32, name="scl3_last", offset=60 * KIB + 4 * HALF)
-        grouped0 = keep.tile([P, HALF * PACK], BF16, name="h_grouped0", align_bytes=64)
+        grouped0 = shared.tile([P, HALF * PACK], BF16, name="h_grouped0", align_bytes=64, offset=68 * KIB)
         grouped1 = keep.tile([P, HALF * PACK], BF16, name="h_grouped1", align_bytes=64)
         staged0 = keep.tile([P, 2 * N], BF16, name="w2_staged0", align_bytes=64)
         staged1 = keep.tile([P, 2 * N], BF16, name="w2_staged1", align_bytes=64)
@@ -154,10 +154,11 @@ def tile_picked_decode2_relu_p_kernel(tc, x_words, x_scales, w1, b1, w2, scl, sh
         hidden.append(quantize(grouped1, "h_codes1", new_plane("h_plane1")))
         weights.append(quantize(staged1, "w2_codes1", new_plane("w2_plane1")))
 
-        picked_shf = [shared.tile([P, S], F32, name="picked_shf%d" % t, offset=ROWS_AT + t * 2 * KIB) for t in range(PACK)]
-        for lo in range(0, PACK * S - HALF, HALF):
-            t, lo = divmod(lo, S)
-            nc.scalar.activation(out=picked_shf[t][:, lo : lo + HALF], in_=shf_tables[t][:].indirect(entries(lo, HALF)), func=COPY)
+        picked_shf = [shared.tile([P, S], F32, name="picked_shf%d" % t, offset=ROWS_AT + t * 2 * KIB if t else 68 * KIB) for t in range(PACK)]
+        for first in range(0, PACK * S, HALF):
+            t, lo = divmod(first, S)
+            width = min(HALF, PACK * S - P - first)
+            nc.scalar.activation(out=picked_shf[t][:, lo : lo + width], in_=shf_tables[t][:].indirect(entries(lo, width)), func=COPY)
 
         zs = [keep.tile([P, S], F32, name="z%d" % t) for t in range(PACK)]
         res = [keep.tile([P, S], F32, name="res%d" % t) for t in range(PACK)]
@@ -203,8 +204,8 @@ def tile_picked_decode2_relu_p_kernel(tc, x_words, x_scales, w1, b1, w2, scl, sh
         shift(1, HALF, HALF)
         add(1, P, P)
         store(1, 0, HALF)
-        shift(3, HALF, HALF, fused=True)
+        shift(3, S - P, P, fused=True)
         shift(2, 0, HALF)
         shift(2, HALF, HALF)
-        shift(3, 0, P)
-        shift(3, P, P)
+        shift(3, 0, HALF)
+        shift(3, HALF, P)

@@ -25,6 +25,8 @@ RUN = 4
 W1_VECTOR_EXTRA = 32
 KIB = 1024
 ROWS_AT = 40 * KIB
+Z_AT = 72 * KIB
+RES_AT = 80 * KIB
 
 
 def tile_picked_decode2_relu_p_kernel(tc, x_words, x_scales, w1, b1, w2, scl, shf, offs, rg, out):
@@ -120,48 +122,48 @@ def tile_picked_decode2_relu_p_kernel(tc, x_words, x_scales, w1, b1, w2, scl, sh
                 nc.scalar.activation(out=h_rows[:, t, :], in_=acc[:], func=RELU, bias=bias[:, t : t + 1])
 
         def interleave(grouped, h_rows, copy):
-            copy(out=grouped[:].rearrange("p (c i t) -> p c t i", i=4, t=PACK), in_=h_rows[:, 0:PACK, :].rearrange("p t (c i) -> p c t i", i=4))
+            copy(out=grouped.rearrange("p (c i t) -> p c t i", i=4, t=PACK), in_=h_rows.rearrange("p t (c i) -> p c t i", i=4))
 
-        def quantize(staged, name, plane):
-            codes = keep.tile([P, HALF], U32, name=name, align_bytes=64)
-            nc.vector.quantize_mx(out=codes[:].bitcast(FP8X4), scales=plane[:], in_=staged[:, 0 : HALF * PACK])
-            return codes, plane
+        def operand(name):
+            return keep.tile([P, HALF], U32, name=name + "_codes", align_bytes=64), keep.tile([P, HALF], U8, name=name + "_plane", align_bytes=64)
 
-        def new_plane(name):
-            return keep.tile([P, HALF], U8, name=name, align_bytes=64)
+        def quantize(staged, target, lo=0, width=HALF):
+            codes, plane = target
+            nc.vector.quantize_mx(out=codes[:, lo : lo + width].bitcast(FP8X4), scales=plane[:, lo : lo + width], in_=staged[:, PACK * lo : PACK * (lo + width)])
 
         w2_cols = w2_raw[:].rearrange("p j (a t b) -> p t a j b", t=PACK, b=RUN)
 
         def cast_w2(staged, pair):
-            nc.vector.tensor_copy(out=staged[:, 0 : 2 * N].rearrange("p (t a b j) -> p t a j b", t=2, b=RUN, j=PACK), in_=w2_cols[:, 2 * pair : 2 * pair + 2])
+            nc.vector.tensor_copy(out=staged[:].rearrange("p (t a b j) -> p t a j b", t=2, b=RUN, j=PACK), in_=w2_cols[:, 2 * pair : 2 * pair + 2])
 
         rows0 = keep.tile([P, PACK, HALF], BF16, name="h_rows0")
         rows1 = shared.tile([P, 4 * PACK, HALF], BF16, name="h_rows1", offset=ROWS_AT)
         first_layer(0, rows0)
         first_layer(1, rows1)
         scl3_last = shared.tile([P, P], F32, name="scl3_last", offset=60 * KIB + 4 * HALF)
-        grouped0 = shared.tile([P, HALF * PACK], BF16, name="h_grouped0", align_bytes=64, offset=68 * KIB)
-        grouped1 = keep.tile([P, HALF * PACK], BF16, name="h_grouped1", align_bytes=64)
-        staged0 = keep.tile([P, 2 * N], BF16, name="w2_staged0", align_bytes=64)
-        staged1 = keep.tile([P, 2 * N], BF16, name="w2_staged1", align_bytes=64)
-        interleave(grouped0, rows0, nc.vector.tensor_copy)
-        interleave(grouped1, rows1, nc.scalar.copy)
+        grouped = [keep.tile([P, HALF * PACK], BF16, name="h_grouped%d" % half, align_bytes=64) for half in range(2)]
+        staged = [keep.tile([P, 2 * N], BF16, name="w2_staged%d" % pair, align_bytes=64) for pair in range(2)]
+        hidden = [operand("h%d" % half) for half in range(2)]
+        weights = [operand("w2_%d" % pair) for pair in range(2)]
+        for lo in (0, P):
+            interleave(grouped[0][:, PACK * lo : PACK * (lo + P)], rows0[:, :, lo : lo + P], nc.vector.tensor_copy)
+        interleave(grouped[1][:], rows1[:, 0:PACK, :], nc.scalar.copy)
         nc.scalar.activation(out=scl3_last[:], in_=scl_tables[3][:].indirect(entries(S - P, P)), func=COPY)
-        cast_w2(staged0, 0)
-        hidden = [quantize(grouped0, "h_codes0", new_plane("h_plane0"))]
-        weights = [quantize(staged0, "w2_codes0", new_plane("w2_plane0"))]
-        cast_w2(staged1, 1)
-        hidden.append(quantize(grouped1, "h_codes1", new_plane("h_plane1")))
-        weights.append(quantize(staged1, "w2_codes1", new_plane("w2_plane1")))
+        for lo in (0, P):
+            quantize(grouped[0], hidden[0], lo, P)
+        cast_w2(staged[0], 0)
+        cast_w2(staged[1], 1)
+        quantize(staged[0], weights[0])
+        quantize(grouped[1], hidden[1])
+        quantize(staged[1], weights[1])
 
-        picked_shf = [shared.tile([P, S], F32, name="picked_shf%d" % t, offset=ROWS_AT + t * 2 * KIB if t else 68 * KIB) for t in range(PACK)]
-        for first in range(0, PACK * S, HALF):
-            t, lo = divmod(first, S)
-            width = min(HALF, PACK * S - P - first)
-            nc.scalar.activation(out=picked_shf[t][:, lo : lo + width], in_=shf_tables[t][:].indirect(entries(lo, width)), func=COPY)
+        pieces = [(t, half) for t in range(PACK) for half in range(2)]
+        picked_shf = {}
+        for n, (t, half) in enumerate(pieces):
+            picked_shf[t, half] = shared.tile([P, HALF], F32, name="picked_shf%d_%d" % (t, half), offset=ROWS_AT + n * KIB if n else 2 * KIB)
+            nc.scalar.activation(out=picked_shf[t, half][:], in_=shf_tables[t][:].indirect(entries(half * HALF, HALF)), func=COPY)
 
-        zs = [keep.tile([P, S], F32, name="z%d" % t) for t in range(PACK)]
-        res = [keep.tile([P, S], F32, name="res%d" % t) for t in range(PACK)]
+        zs = {}
 
         def scale(t, half):
             span = slice(half * HALF, (half + 1) * HALF)
@@ -176,36 +178,33 @@ def tile_picked_decode2_relu_p_kernel(tc, x_words, x_scales, w1, b1, w2, scl, sh
                 start=True,
                 stop=True,
             )
+            z = shared.tile([P, HALF], F32, name="z%d_%d" % (t, half), offset=Z_AT + (2 * t + half) * KIB)
+            zs[t, half] = z
             if (t, half) == (PACK - 1, 1):
-                nc.vector.tensor_tensor(zs[t][:, HALF : S - P], acc[:, 0:P], picked_scl[t][:, HALF : S - P], MULT)
-                nc.vector.tensor_tensor(zs[t][:, S - P : S], acc[:, P:HALF], scl3_last[:], MULT)
+                nc.vector.tensor_tensor(z[:, 0:P], acc[:, 0:P], picked_scl[t][:, HALF : S - P], MULT)
+                nc.vector.tensor_tensor(z[:, P:HALF], acc[:, P:HALF], scl3_last[:], MULT)
             else:
-                nc.vector.tensor_tensor(zs[t][:, span], acc[:], scl1_halves[half][:] if t == 1 else picked_scl[t][:, span], MULT)
+                nc.vector.tensor_tensor(z[:], acc[:], scl1_halves[half][:] if t == 1 else picked_scl[t][:, span], MULT)
 
-        def add(t, lo, width, engine=nc.vector, fused=False):
-            span = slice(lo, lo + width)
-            shifts = shf_tables[t][:].indirect(entries(lo, width)) if fused else picked_shf[t][:, span]
-            engine.tensor_tensor(res[t][:, span], shifts, zs[t][:, span], ADD)
+        def shift(t, half, engine=nc.vector, offset=None):
+            at = RES_AT + (2 * t + half) * KIB if offset is None else offset
+            res = shared.tile([P, HALF], F32, name="res%d_%d" % (t, half), offset=at)
+            engine.tensor_tensor(res[:], picked_shf[t, half][:], zs[t, half][:], ADD)
+            nc.sync.dma_start(out_rows[t][:, :, half * HALF : (half + 1) * HALF], res[:])
 
-        def store(t, lo, width):
-            nc.sync.dma_start(out_rows[t][:, :, lo : lo + width], res[t][:, lo : lo + width])
-
-        def shift(t, lo, width, engine=nc.vector, fused=False):
-            add(t, lo, width, engine, fused)
-            store(t, lo, width)
-
-        for pair in range(2):
-            for half in range(2):
-                scale(2 * pair, half)
-                scale(2 * pair + 1, half)
-        shift(0, 0, HALF, nc.gpsimd)
-        shift(0, HALF, HALF, nc.gpsimd)
-        add(1, 0, P, nc.gpsimd)
-        shift(1, HALF, HALF)
-        add(1, P, P)
-        store(1, 0, HALF)
-        shift(3, S - P, P, fused=True)
-        shift(2, 0, HALF)
-        shift(2, HALF, HALF)
-        shift(3, 0, HALF)
-        shift(3, HALF, P)
+        scale(0, 0)
+        scale(1, 0)
+        scale(0, 1)
+        scale(1, 1)
+        shift(0, 0, nc.gpsimd)
+        shift(0, 1)
+        shift(1, 0)
+        scale(2, 0)
+        scale(2, 1)
+        scale(3, 0)
+        shift(1, 1, nc.gpsimd, Z_AT + 2 * KIB)
+        shift(2, 0)
+        shift(2, 1)
+        scale(3, 1)
+        shift(3, 0)
+        shift(3, 1)

@@ -26,7 +26,6 @@ W1_VECTOR_EXTRA = 32
 KIB = 1024
 ROWS_AT = 40 * KIB
 Z_AT = 72 * KIB
-RES_AT = 80 * KIB
 
 
 def tile_picked_decode2_relu_p_kernel(tc, x_words, x_scales, w1, b1, w2, scl, shf, offs, rg, out):
@@ -54,37 +53,35 @@ def tile_picked_decode2_relu_p_kernel(tc, x_words, x_scales, w1, b1, w2, scl, sh
         offs_sb = lists.tile([P, S // GROUP], U16, name="offs_sb")
         rg_sb = lists.tile([P, S // GROUP], U16, name="rg_sb")
         scl_tables, shf_tables = {}, {}
-        scl_tables[1] = load_table(scl_rows[1], "scl1", 52 * KIB)
+        scl_tables[0] = load_table(scl_rows[0], "scl0", 52 * KIB, 2 * U)
         nc.sync.dma_start(rg_sb[:], rg)
         nc.sync.dma_start(offs_sb[:], offs)
-        scl_tables[0] = load_table(scl_rows[0], "scl0", 48 * KIB, 2 * U)
         nc.sync.dma_start(scale_table[:].bitcast(I32)[0:P:8, :], x_scales[0].bitcast(I32))
         w1_raw = shared.tile([P, PACK, H], F32, name="w1_raw", offset=28 * KIB)
         nc.sync.dma_start(w1_raw[:], w1.rearrange("(p j) c -> p j c", j=PACK))
         word_table = keep.tile([P, T], I32, name="word_table")
         nc.sync.dma_start(word_table[:], x_words[0].rearrange("p n t -> p (n t)").bitcast(I32))
-        scl_tables[2] = load_table(scl_rows[2], "scl2", 56 * KIB)
+        scl_tables[1] = load_table(scl_rows[1], "scl1", 56 * KIB)
 
         picked_scales = shared.tile([P, 24 * KIB], U8, name="picked_scales", align_bytes=64, offset=0)
         nc.vector.tensor_copy(out=picked_scales[:, 0:S], in_=scale_table[:].indirect(offs_sb[:]))
         nc.vector.tensor_copy(out=x_plane[:].bitcast(I32), in_=picked_scales[:, 0:S].bitcast(I32))
         for r in range(1, 4):
             nc.sync.dma_start(x_plane[:].bitcast(I32)[r:P:32, :], x_plane[:].bitcast(I32)[8 * r : P : 32, :])
-        bias = shared.tile([P, PACK], F32, name="bias", offset=23 * KIB)
+        bias = shared.tile([P, PACK], F32, name="bias", offset=1 * KIB)
         nc.sync.dma_start(bias[:], b1.rearrange("(p t) o -> p (t o)", t=PACK))
-        scl_tables[3] = load_table(scl_rows[3], "scl3", 2 * KIB)
-        w2_raw = shared.tile([P, PACK, N], F32, name="w2_raw", offset=6 * KIB)
+        scl_tables[2] = load_table(scl_rows[2], "scl2", 2 * KIB)
+        w2_raw = shared.tile([P, PACK, N], F32, name="w2_raw", offset=4 * KIB)
         nc.sync.dma_start(w2_raw[:], w2.rearrange("(p j) c -> p j c", j=PACK))
         for t in range(PACK):
-            shf_tables[t] = load_table(shf_rows[t], "shf%d" % t, (14 + 2 * t) * KIB)
+            if t == 2:
+                scl_tables[3] = load_table(scl_rows[3], "scl3", 20 * KIB)
+            shf_tables[t] = load_table(shf_rows[t], "shf%d" % t, (12 + 2 * t) * KIB)
 
         def entries(lo, width):
             return rg_sb[:, lo // GROUP : (lo + width) // GROUP]
 
-        picked_scl = {t: shared.tile([P, S], F32, name="picked_scl%d" % t, offset=(58 + 2 * t) * KIB) for t in (2, 3)}
-        scl1_halves = [keep.tile([P, HALF], F32, name="picked_scl1_0"), shared.tile([P, HALF], F32, name="picked_scl1_1", offset=22 * KIB)]
-        for half in range(2):
-            nc.vector.tensor_copy(out=scl1_halves[half][:], in_=scl_tables[1][:].indirect(entries(half * HALF, HALF)))
+        picked_scl = {t: shared.tile([P, S], F32, name="picked_scl%d" % t, offset=(60 + 2 * t) * KIB) for t in (1, 2)}
 
         w1_grouped = shared.tile([P, 6 * H], BF16, name="w1_grouped", align_bytes=64, offset=60 * KIB)
         dst = w1_grouped[:, 0 : PACK * H].rearrange("p (t m j) -> p m j t", t=PACK, j=PACK)
@@ -103,9 +100,9 @@ def tile_picked_decode2_relu_p_kernel(tc, x_words, x_scales, w1, b1, w2, scl, sh
             codes = shared.tile([P, HALF], U32, name="x_codes%d" % lo, align_bytes=64, offset=60 * KIB + 4 * lo)
             nc.vector.tensor_copy(out=codes[:], in_=word_table[:].bitcast(U32).indirect(offs_sb[:, lo // GROUP : (lo + HALF) // GROUP]))
             x_codes.append(codes)
-        nc.scalar.activation(out=picked_scl[2][:, 0:HALF], in_=scl_tables[2][:].indirect(entries(0, HALF)), func=COPY)
-        nc.vector.tensor_copy(out=picked_scl[2][:, HALF:S], in_=scl_tables[2][:].indirect(entries(HALF, HALF)))
-        nc.vector.tensor_copy(out=picked_scl[3][:, 0 : S - P], in_=scl_tables[3][:].indirect(entries(0, S - P)))
+        nc.scalar.activation(out=picked_scl[1][:, 0:HALF], in_=scl_tables[1][:].indirect(entries(0, HALF)), func=COPY)
+        nc.vector.tensor_copy(out=picked_scl[1][:, HALF:S], in_=scl_tables[1][:].indirect(entries(HALF, HALF)))
+        nc.vector.tensor_copy(out=picked_scl[2][:, 0 : S - P], in_=scl_tables[2][:].indirect(entries(0, S - P)))
 
         def first_layer(half, h_rows):
             for t in range(PACK):
@@ -133,14 +130,15 @@ def tile_picked_decode2_relu_p_kernel(tc, x_words, x_scales, w1, b1, w2, scl, sh
 
         w2_cols = w2_raw[:].rearrange("p j (a t b) -> p t a j b", t=PACK, b=RUN)
 
-        def cast_w2(staged, pair):
-            nc.vector.tensor_copy(out=staged[:].rearrange("p (t a b j) -> p t a j b", t=2, b=RUN, j=PACK), in_=w2_cols[:, 2 * pair : 2 * pair + 2])
+        def cast_w2(t):
+            place = staged[t // 2][:, t % 2 * N : (t % 2 + 1) * N]
+            nc.vector.tensor_copy(out=place.rearrange("p (a b j) -> p a j b", b=RUN, j=PACK), in_=w2_cols[:, t])
 
         rows0 = keep.tile([P, PACK, HALF], BF16, name="h_rows0")
-        rows1 = shared.tile([P, 4 * PACK, HALF], BF16, name="h_rows1", offset=ROWS_AT)
+        rows1 = shared.tile([P, 5 * PACK, HALF], BF16, name="h_rows1", offset=ROWS_AT)
         first_layer(0, rows0)
         first_layer(1, rows1)
-        scl3_last = shared.tile([P, P], F32, name="scl3_last", offset=60 * KIB + 4 * HALF)
+        scl2_last = shared.tile([P, P], F32, name="scl2_last", offset=60 * KIB + 4 * HALF)
         grouped = [keep.tile([P, HALF * PACK], BF16, name="h_grouped%d" % half, align_bytes=64) for half in range(2)]
         staged = [keep.tile([P, 2 * N], BF16, name="w2_staged%d" % pair, align_bytes=64) for pair in range(2)]
         hidden = [operand("h%d" % half) for half in range(2)]
@@ -148,20 +146,27 @@ def tile_picked_decode2_relu_p_kernel(tc, x_words, x_scales, w1, b1, w2, scl, sh
         for lo in (0, P):
             interleave(grouped[0][:, PACK * lo : PACK * (lo + P)], rows0[:, :, lo : lo + P], nc.vector.tensor_copy)
         interleave(grouped[1][:], rows1[:, 0:PACK, :], nc.scalar.copy)
-        nc.scalar.activation(out=scl3_last[:], in_=scl_tables[3][:].indirect(entries(S - P, P)), func=COPY)
+        nc.scalar.activation(out=scl2_last[:], in_=scl_tables[2][:].indirect(entries(S - P, P)), func=COPY)
         for lo in (0, P):
             quantize(grouped[0], hidden[0], lo, P)
-        cast_w2(staged[0], 0)
-        cast_w2(staged[1], 1)
+        for t in range(3):
+            cast_w2(t)
         quantize(staged[0], weights[0])
+        cast_w2(3)
         quantize(grouped[1], hidden[1])
         quantize(staged[1], weights[1])
 
-        pieces = [(t, half) for t in range(PACK) for half in range(2)]
-        picked_shf = {}
-        for n, (t, half) in enumerate(pieces):
-            picked_shf[t, half] = shared.tile([P, HALF], F32, name="picked_shf%d_%d" % (t, half), offset=ROWS_AT + n * KIB if n else 2 * KIB)
-            nc.scalar.activation(out=picked_shf[t, half][:], in_=shf_tables[t][:].indirect(entries(half * HALF, HALF)), func=COPY)
+        def late_gather(n, name, table, lo, width):
+            picked = shared.tile([P, width], F32, name=name, offset=ROWS_AT + n * KIB if n else 2 * KIB)
+            nc.scalar.activation(out=picked[:], in_=table[:].indirect(entries(lo, width)), func=COPY)
+            return picked
+
+        picked_shf, scl3_halves = {}, {}
+        for t, lo, width in ((0, 0, HALF), (0, HALF, HALF), (1, 0, HALF), (2, 0, HALF), (2, HALF, HALF), (3, 0, HALF), (3, HALF, P)):
+            if (t, lo) == (2, 0):
+                for half in range(2):
+                    scl3_halves[half] = late_gather(2 * PACK + half, "picked_scl3_%d" % half, scl_tables[3], half * HALF, HALF)
+            picked_shf[t, lo] = late_gather(2 * t + lo // HALF, "picked_shf%d_%d" % (t, lo), shf_tables[t], lo, width)
 
         zs = {}
 
@@ -180,31 +185,42 @@ def tile_picked_decode2_relu_p_kernel(tc, x_words, x_scales, w1, b1, w2, scl, sh
             )
             z = shared.tile([P, HALF], F32, name="z%d_%d" % (t, half), offset=Z_AT + (2 * t + half) * KIB)
             zs[t, half] = z
-            if (t, half) == (PACK - 1, 1):
+            if (t, half) == (2, 1):
                 nc.vector.tensor_tensor(z[:, 0:P], acc[:, 0:P], picked_scl[t][:, HALF : S - P], MULT)
-                nc.vector.tensor_tensor(z[:, P:HALF], acc[:, P:HALF], scl3_last[:], MULT)
+                nc.vector.tensor_tensor(z[:, P:HALF], acc[:, P:HALF], scl2_last[:], MULT)
             else:
-                nc.vector.tensor_tensor(z[:], acc[:], scl1_halves[half][:] if t == 1 else picked_scl[t][:, span], MULT)
+                nc.vector.tensor_tensor(z[:], acc[:], scl3_halves[half][:] if t == 3 else picked_scl[t][:, span], MULT)
 
-        def shift(t, half, engine=nc.vector, offset=None):
-            at = RES_AT + (2 * t + half) * KIB if offset is None else offset
-            res = shared.tile([P, HALF], F32, name="res%d_%d" % (t, half), offset=at)
-            engine.tensor_tensor(res[:], picked_shf[t, half][:], zs[t, half][:], ADD)
-            nc.sync.dma_start(out_rows[t][:, :, half * HALF : (half + 1) * HALF], res[:])
+        res = [keep.tile([P, S], F32, name="res%d" % t) for t in range(PACK)]
 
-        scale(0, 0)
-        scale(1, 0)
-        scale(0, 1)
-        scale(1, 1)
+        def add(t, lo, width, engine=nc.vector, fused=False):
+            half, span = lo // HALF, slice(lo % HALF, lo % HALF + width)
+            shifts = shf_tables[t][:].indirect(entries(lo, width)) if fused else picked_shf[t, half * HALF][:, span]
+            engine.tensor_tensor(res[t][:, lo : lo + width], shifts, zs[t, half][:, span], ADD)
+
+        def store(t, half):
+            span = slice(half * HALF, (half + 1) * HALF)
+            nc.sync.dma_start(out_rows[t][:, :, span], res[t][:, span])
+
+        def shift(t, half, engine=nc.vector, fused=False):
+            add(t, half * HALF, HALF, engine, fused)
+            store(t, half)
+
+        for half in range(2):
+            scale(0, half)
+            scale(1, half)
+        for t in (2, 3):
+            scale(t, 0)
+            scale(t, 1)
         shift(0, 0, nc.gpsimd)
-        shift(0, 1)
-        shift(1, 0)
-        scale(2, 0)
-        scale(2, 1)
-        scale(3, 0)
-        shift(1, 1, nc.gpsimd, Z_AT + 2 * KIB)
+        shift(0, 1, nc.gpsimd)
+        add(1, 0, P, nc.gpsimd)
+        add(1, P, P)
+        store(1, 0)
+        shift(1, 1, fused=True)
         shift(2, 0)
         shift(2, 1)
-        scale(3, 1)
         shift(3, 0)
-        shift(3, 1)
+        add(3, S - P, P, fused=True)
+        add(3, HALF, P)
+        store(3, 1)

@@ -209,18 +209,19 @@ def tile_picked_decode2_relu_p_kernel(tc, x_words, x_scales, w1, b1, w2, scl, sh
         for half in range(2):
             scale(0, half)
             scale(1, half)
-        for t in (2, 3):
-            scale(t, 0)
-            scale(t, 1)
+        scale(2, 0)
+        scale(2, 1)
+        scale(3, 0)
         shift(0, 0, nc.gpsimd)
         shift(0, 1, nc.gpsimd)
         add(1, 0, P, nc.gpsimd)
         add(1, P, P)
         store(1, 0)
         shift(1, 1, fused=True)
+        scale(3, 1)
         shift(2, 0)
         shift(2, 1)
-        shift(3, 0)
         add(3, S - P, P, fused=True)
+        shift(3, 0)
         add(3, HALF, P)
         store(3, 1)

@@ -198,13 +198,13 @@ def tile_picked_decode2_relu_p_kernel(tc, x_words, x_scales, w1, b1, w2, scl, sh
             shifts = shf_tables[t][:].indirect(entries(lo, width)) if fused else picked_shf[t, half * HALF][:, span]
             engine.tensor_tensor(res[t][:, lo : lo + width], shifts, zs[t, half][:, span], ADD)
 
-        def store(t, half):
-            span = slice(half * HALF, (half + 1) * HALF)
+        def store(t, lo, width):
+            span = slice(lo, lo + width)
             nc.sync.dma_start(out_rows[t][:, :, span], res[t][:, span])
 
         def shift(t, half, engine=nc.vector, fused=False):
             add(t, half * HALF, HALF, engine, fused)
-            store(t, half)
+            store(t, half * HALF, HALF)
 
         for half in range(2):
             scale(0, half)
@@ -212,16 +212,16 @@ def tile_picked_decode2_relu_p_kernel(tc, x_words, x_scales, w1, b1, w2, scl, sh
         scale(2, 0)
         scale(2, 1)
         scale(3, 0)
-        shift(0, 0, nc.gpsimd)
-        shift(0, 1, nc.gpsimd)
-        add(1, 0, P, nc.gpsimd)
-        add(1, P, P)
-        store(1, 0)
+        add(0, 0, HALF, nc.gpsimd)
+        add(0, HALF, HALF, nc.gpsimd)
+        store(0, 0, S)
+        shift(1, 0)
         shift(1, 1, fused=True)
         scale(3, 1)
         shift(2, 0)
         shift(2, 1)
         add(3, S - P, P, fused=True)
+        store(3, S - P, P)
         shift(3, 0)
         add(3, HALF, P)
-        store(3, 1)
+        store(3, HALF, P)

@@ -40,9 +40,9 @@ def tile_picked_decode2_relu_p_kernel(tc, x_words, x_scales, w1, b1, w2, scl, sh
         shf_rows = shf.rearrange("(a t b) u -> t a b u", t=PACK, b=RUN)
         out_rows = out.rearrange("(a t b) s -> t a b s", t=PACK, b=RUN)
 
-        scale_table = keep.tile([P, T], U8, name="scale_table", align_bytes=64)
+        scale_table = keep.tile([P, T], U8, name="scale_table", align_bytes=256)
         nc.vector.memset(scale_table[:].bitcast(I32), 0)
-        x_plane = keep.tile([P, S], U8, name="x_plane", align_bytes=64)
+        x_plane = keep.tile([P, S], U8, name="x_plane", align_bytes=256)
 
 
         def load_table(rows, name, offset, cols=U):
@@ -59,11 +59,11 @@ def tile_picked_decode2_relu_p_kernel(tc, x_words, x_scales, w1, b1, w2, scl, sh
         nc.sync.dma_start(scale_table[:].bitcast(I32)[0:P:8, :], x_scales[0].bitcast(I32))
         w1_raw = shared.tile([P, PACK, H], F32, name="w1_raw", offset=28 * KIB)
         nc.sync.dma_start(w1_raw[:], w1.rearrange("(p j) c -> p j c", j=PACK))
-        word_table = keep.tile([P, T], I32, name="word_table")
+        word_table = keep.tile([P, T], I32, name="word_table", align_bytes=256)
         nc.sync.dma_start(word_table[:], x_words[0].rearrange("p n t -> p (n t)").bitcast(I32))
         scl_tables[1] = load_table(scl_rows[1], "scl1", 56 * KIB)
 
-        picked_scales = shared.tile([P, 24 * KIB], U8, name="picked_scales", align_bytes=64, offset=0)
+        picked_scales = shared.tile([P, 24 * KIB], U8, name="picked_scales", align_bytes=256, offset=0)
         nc.vector.tensor_copy(out=picked_scales[:, 0:S], in_=scale_table[:].indirect(offs_sb[:]))
         nc.vector.tensor_copy(out=x_plane[:].bitcast(I32), in_=picked_scales[:, 0:S].bitcast(I32))
         for r in range(1, 4):
@@ -83,7 +83,7 @@ def tile_picked_decode2_relu_p_kernel(tc, x_words, x_scales, w1, b1, w2, scl, sh
 
         picked_scl = {t: shared.tile([P, S], F32, name="picked_scl%d" % t, offset=(60 + 2 * t) * KIB) for t in (1, 2)}
 
-        w1_grouped = shared.tile([P, 6 * H], BF16, name="w1_grouped", align_bytes=64, offset=60 * KIB)
+        w1_grouped = shared.tile([P, 6 * H], BF16, name="w1_grouped", align_bytes=256, offset=60 * KIB)
         dst = w1_grouped[:, 0 : PACK * H].rearrange("p (t m j) -> p m j t", t=PACK, j=PACK)
         src = w1_raw[:].rearrange("p j (m t) -> p m j t", t=PACK)
         nc.vector.tensor_copy(out=dst[:, :, :, 0:2], in_=src[:, :, :, 0:2])
@@ -91,13 +91,13 @@ def tile_picked_decode2_relu_p_kernel(tc, x_words, x_scales, w1, b1, w2, scl, sh
         nc.scalar.activation(out=dst[:, W1_VECTOR_EXTRA:P, :, 2:4], in_=src[:, W1_VECTOR_EXTRA:P, :, 2:4], func=COPY)
         picked_scl[0] = shared.tile([P, S], F32, name="picked_scl0", offset=28 * KIB)
         nc.scalar.activation(out=picked_scl[0][:], in_=scl_tables[0][:].indirect(entries(0, S)), func=COPY)
-        w1_codes = keep.tile([P, H], U32, name="w1_codes", align_bytes=64)
-        w1_plane = keep.tile([P, H], U8, name="w1_plane", align_bytes=64)
+        w1_codes = keep.tile([P, H], U32, name="w1_codes", align_bytes=256)
+        w1_plane = keep.tile([P, H], U8, name="w1_plane", align_bytes=256)
         nc.vector.quantize_mx(out=w1_codes[:].bitcast(FP8X4), scales=w1_plane[:], in_=w1_grouped[:, 0 : PACK * H])
 
         x_codes = []
         for lo in (0, HALF):
-            codes = shared.tile([P, HALF], U32, name="x_codes%d" % lo, align_bytes=64, offset=60 * KIB + 4 * lo)
+            codes = shared.tile([P, HALF], U32, name="x_codes%d" % lo, align_bytes=256, offset=60 * KIB + 4 * lo)
             nc.vector.tensor_copy(out=codes[:], in_=word_table[:].bitcast(U32).indirect(offs_sb[:, lo // GROUP : (lo + HALF) // GROUP]))
             x_codes.append(codes)
         nc.scalar.activation(out=picked_scl[1][:, 0:HALF], in_=scl_tables[1][:].indirect(entries(0, HALF)), func=COPY)
@@ -122,7 +122,7 @@ def tile_picked_decode2_relu_p_kernel(tc, x_words, x_scales, w1, b1, w2, scl, sh
             copy(out=grouped.rearrange("p (c i t) -> p c t i", i=4, t=PACK), in_=h_rows.rearrange("p t (c i) -> p c t i", i=4))
 
         def operand(name):
-            return keep.tile([P, HALF], U32, name=name + "_codes", align_bytes=64), keep.tile([P, HALF], U8, name=name + "_plane", align_bytes=64)
+            return keep.tile([P, HALF], U32, name=name + "_codes", align_bytes=256), keep.tile([P, HALF], U8, name=name + "_plane", align_bytes=256)
 
         def quantize(staged, target, lo=0, width=HALF):
             codes, plane = target
@@ -139,8 +139,8 @@ def tile_picked_decode2_relu_p_kernel(tc, x_words, x_scales, w1, b1, w2, scl, sh
         first_layer(0, rows0)
         first_layer(1, rows1)
         scl2_last = shared.tile([P, P], F32, name="scl2_last", offset=60 * KIB + 4 * HALF)
-        grouped = [keep.tile([P, HALF * PACK], BF16, name="h_grouped%d" % half, align_bytes=64) for half in range(2)]
-        staged = [keep.tile([P, 2 * N], BF16, name="w2_staged%d" % pair, align_bytes=64) for pair in range(2)]
+        grouped = [keep.tile([P, HALF * PACK], BF16, name="h_grouped%d" % half, align_bytes=256) for half in range(2)]
+        staged = [keep.tile([P, 2 * N], BF16, name="w2_staged%d" % pair, align_bytes=256) for pair in range(2)]
         hidden = [operand("h%d" % half) for half in range(2)]
         weights = [operand("w2_%d" % pair) for pair in range(2)]
         for lo in (0, P):
@@ -191,7 +191,7 @@ def tile_picked_decode2_relu_p_kernel(tc, x_words, x_scales, w1, b1, w2, scl, sh
             else:
                 nc.vector.tensor_tensor(z[:], acc[:], scl3_halves[half][:] if t == 3 else picked_scl[t][:, span], MULT)
 
-        res = [keep.tile([P, S], F32, name="res%d" % t) for t in range(PACK)]
+        res = [keep.tile([P, S], F32, name="res%d" % t, align_bytes=256) for t in range(PACK)]
 
         def add(t, lo, width, engine=nc.vector, fused=False):
             half, span = lo // HALF, slice(lo % HALF, lo % HALF + width)

from contextlib import ExitStack

import concourse.mybir as mybir

K, T, S, N, H, U = 512, 2048, 512, 512, 512, 512
FLOPS = 2 * K * H * S + 2 * H * N * S

F32 = mybir.dt.float32
BF16 = mybir.dt.bfloat16
I32 = mybir.dt.int32
U32 = mybir.dt.uint32
U16 = mybir.dt.uint16
U8 = mybir.dt.uint8
FP8X4 = mybir.dt.float8_e4m3fn_x4
MULT = mybir.AluOpType.mult
ADD = mybir.AluOpType.add
RELU = mybir.ActivationFunctionType.Relu
COPY = mybir.ActivationFunctionType.Copy

P = 128
PACK = 4
GROUP = 16
HALF = S // 2
RUN = 4
W1_VECTOR_EXTRA = 32
KIB = 1024
ROWS_AT = 40 * KIB
Z_AT = 72 * KIB


def tile_picked_decode2_relu_p_kernel(tc, x_words, x_scales, w1, b1, w2, scl, shf, offs, rg, out):
    nc = tc.nc
    with ExitStack() as ctx:
        lists = ctx.enter_context(tc.tile_pool(name="lists", bufs=1))
        shared = ctx.enter_context(tc.tile_pool(name="shared", bufs=1))
        keep = ctx.enter_context(tc.tile_pool(name="keep", bufs=1))
        psum = ctx.enter_context(tc.psum_pool(name="psum", bufs=1))

        scl_rows = scl.rearrange("(a t b) u -> t a b u", t=PACK, b=RUN)
        shf_rows = shf.rearrange("(a t b) u -> t a b u", t=PACK, b=RUN)
        out_rows = out.rearrange("(a t b) s -> t a b s", t=PACK, b=RUN)

        scale_table = keep.tile([P, T], U8, name="scale_table", align_bytes=256)
        nc.vector.memset(scale_table[:].bitcast(I32), 0)
        x_plane = keep.tile([P, S], U8, name="x_plane", align_bytes=256)


        def load_table(rows, name, offset, cols=U):
            table = shared.tile([P, cols], F32, name=name, offset=offset)
            nc.sync.dma_start(table[:, 0:U], rows)
            return table

        offs_sb = lists.tile([P, S // GROUP], U16, name="offs_sb")
        rg_sb = lists.tile([P, S // GROUP], U16, name="rg_sb")
        scl_tables, shf_tables = {}, {}
        scl_tables[0] = load_table(scl_rows[0], "scl0", 52 * KIB, 2 * U)
        nc.sync.dma_start(rg_sb[:], rg)
        nc.sync.dma_start(offs_sb[:], offs)
        nc.sync.dma_start(scale_table[:].bitcast(I32)[0:P:8, :], x_scales[0].bitcast(I32))
        w1_raw = shared.tile([P, PACK, H], F32, name="w1_raw", offset=28 * KIB)
        nc.sync.dma_start(w1_raw[:], w1.rearrange("(p j) c -> p j c", j=PACK))
        word_table = keep.tile([P, T], I32, name="word_table", align_bytes=256)
        nc.sync.dma_start(word_table[:], x_words[0].rearrange("p n t -> p (n t)").bitcast(I32))
        scl_tables[1] = load_table(scl_rows[1], "scl1", 56 * KIB)

        picked_scales = shared.tile([P, 24 * KIB], U8, name="picked_scales", align_bytes=256, offset=0)
        nc.vector.tensor_copy(out=picked_scales[:, 0:S], in_=scale_table[:].indirect(offs_sb[:]))
        nc.vector.tensor_copy(out=x_plane[:].bitcast(I32), in_=picked_scales[:, 0:S].bitcast(I32))
        for r in range(1, 4):
            nc.sync.dma_start(x_plane[:].bitcast(I32)[r:P:32, :], x_plane[:].bitcast(I32)[8 * r : P : 32, :])
        bias = shared.tile([P, PACK], F32, name="bias", offset=1 * KIB)
        nc.sync.dma_start(bias[:], b1.rearrange("(p t) o -> p (t o)", t=PACK))
        scl_tables[2] = load_table(scl_rows[2], "scl2", 2 * KIB)
        w2_raw = shared.tile([P, PACK, N], F32, name="w2_raw", offset=4 * KIB)
        nc.sync.dma_start(w2_raw[:], w2.rearrange("(p j) c -> p j c", j=PACK))
        for t in range(PACK):
            if t == 2:
                scl_tables[3] = load_table(scl_rows[3], "scl3", 20 * KIB)
            shf_tables[t] = load_table(shf_rows[t], "shf%d" % t, (12 + 2 * t) * KIB)

        def entries(lo, width):
            return rg_sb[:, lo // GROUP : (lo + width) // GROUP]

        picked_scl = {t: shared.tile([P, S], F32, name="picked_scl%d" % t, offset=(60 + 2 * t) * KIB) for t in (1, 2)}

        w1_grouped = shared.tile([P, 6 * H], BF16, name="w1_grouped", align_bytes=256, offset=60 * KIB)
        dst = w1_grouped[:, 0 : PACK * H].rearrange("p (t m j) -> p m j t", t=PACK, j=PACK)
        src = w1_raw[:].rearrange("p j (m t) -> p m j t", t=PACK)
        nc.vector.tensor_copy(out=dst[:, :, :, 0:2], in_=src[:, :, :, 0:2])
        nc.vector.tensor_copy(out=dst[:, 0:W1_VECTOR_EXTRA, :, 2:4], in_=src[:, 0:W1_VECTOR_EXTRA, :, 2:4])
        nc.scalar.activation(out=dst[:, W1_VECTOR_EXTRA:P, :, 2:4], in_=src[:, W1_VECTOR_EXTRA:P, :, 2:4], func=COPY)
        picked_scl[0] = shared.tile([P, S], F32, name="picked_scl0", offset=28 * KIB)
        nc.scalar.activation(out=picked_scl[0][:], in_=scl_tables[0][:].indirect(entries(0, S)), func=COPY)
        w1_codes = keep.tile([P, H], U32, name="w1_codes", align_bytes=256)
        w1_plane = keep.tile([P, H], U8, name="w1_plane", align_bytes=256)
        nc.vector.quantize_mx(out=w1_codes[:].bitcast(FP8X4), scales=w1_plane[:], in_=w1_grouped[:, 0 : PACK * H])

        x_codes = []
        for lo in (0, HALF):
            codes = shared.tile([P, HALF], U32, name="x_codes%d" % lo, align_bytes=256, offset=60 * KIB + 4 * lo)
            nc.vector.tensor_copy(out=codes[:], in_=word_table[:].bitcast(U32).indirect(offs_sb[:, lo // GROUP : (lo + HALF) // GROUP]))
            x_codes.append(codes)
        nc.scalar.activation(out=picked_scl[1][:, 0:HALF], in_=scl_tables[1][:].indirect(entries(0, HALF)), func=COPY)
        nc.vector.tensor_copy(out=picked_scl[1][:, HALF:S], in_=scl_tables[1][:].indirect(entries(HALF, HALF)))
        nc.vector.tensor_copy(out=picked_scl[2][:, 0 : S - P], in_=scl_tables[2][:].indirect(entries(0, S - P)))

        def first_layer(half, h_rows):
            for t in range(PACK):
                acc = psum.tile([P, HALF], F32, name="acc", tag="bank%d" % (PACK * half + t))
                nc.tensor.matmul_mx(
                    out=acc[:],
                    lhsT=w1_codes[:, t * P : (t + 1) * P].bitcast(FP8X4),
                    lhsT_scale=w1_plane[:, t * P : (t + 1) * P],
                    rhs=x_codes[half][:].bitcast(FP8X4),
                    rhs_scale=x_plane[:, half * HALF : (half + 1) * HALF],
                    start=True,
                    stop=True,
                )
                nc.scalar.activation(out=h_rows[:, t, :], in_=acc[:], func=RELU, bias=bias[:, t : t + 1])

        def interleave(grouped, h_rows, copy):
            copy(out=grouped.rearrange("p (c i t) -> p c t i", i=4, t=PACK), in_=h_rows.rearrange("p t (c i) -> p c t i", i=4))

        def operand(name):
            return keep.tile([P, HALF], U32, name=name + "_codes", align_bytes=256), keep.tile([P, HALF], U8, name=name + "_plane", align_bytes=256)

        def quantize(staged, target, lo=0, width=HALF):
            codes, plane = target
            nc.vector.quantize_mx(out=codes[:, lo : lo + width].bitcast(FP8X4), scales=plane[:, lo : lo + width], in_=staged[:, PACK * lo : PACK * (lo + width)])

        w2_cols = w2_raw[:].rearrange("p j (a t b) -> p t a j b", t=PACK, b=RUN)

        def cast_w2(t):
            place = staged[t // 2][:, t % 2 * N : (t % 2 + 1) * N]
            nc.vector.tensor_copy(out=place.rearrange("p (a b j) -> p a j b", b=RUN, j=PACK), in_=w2_cols[:, t])

        rows0 = keep.tile([P, PACK, HALF], BF16, name="h_rows0")
        rows1 = shared.tile([P, 5 * PACK, HALF], BF16, name="h_rows1", offset=ROWS_AT)
        first_layer(0, rows0)
        first_layer(1, rows1)
        scl2_last = shared.tile([P, P], F32, name="scl2_last", offset=60 * KIB + 4 * HALF)
        grouped = [keep.tile([P, HALF * PACK], BF16, name="h_grouped%d" % half, align_bytes=256) for half in range(2)]
        staged = [keep.tile([P, 2 * N], BF16, name="w2_staged%d" % pair, align_bytes=256) for pair in range(2)]
        hidden = [operand("h%d" % half) for half in range(2)]
        weights = [operand("w2_%d" % pair) for pair in range(2)]
        for lo in (0, P):
            interleave(grouped[0][:, PACK * lo : PACK * (lo + P)], rows0[:, :, lo : lo + P], nc.vector.tensor_copy)
        interleave(grouped[1][:], rows1[:, 0:PACK, :], nc.scalar.copy)
        nc.scalar.activation(out=scl2_last[:], in_=scl_tables[2][:].indirect(entries(S - P, P)), func=COPY)
        for lo in (0, P):
            quantize(grouped[0], hidden[0], lo, P)
        for t in range(3):
            cast_w2(t)
        quantize(staged[0], weights[0])
        cast_w2(3)
        quantize(grouped[1], hidden[1])
        quantize(staged[1], weights[1])

        def late_gather(n, name, table, lo, width):
            picked = shared.tile([P, width], F32, name=name, offset=ROWS_AT + n * KIB if n else 2 * KIB)
            nc.scalar.activation(out=picked[:], in_=table[:].indirect(entries(lo, width)), func=COPY)
            return picked

        picked_shf, scl3_halves = {}, {}
        for t, lo, width in ((0, 0, HALF), (0, HALF, HALF), (1, 0, HALF), (2, 0, HALF), (2, HALF, HALF), (3, 0, HALF), (3, HALF, P)):
            if (t, lo) == (2, 0):
                for half in range(2):
                    scl3_halves[half] = late_gather(2 * PACK + half, "picked_scl3_%d" % half, scl_tables[3], half * HALF, HALF)
            picked_shf[t, lo] = late_gather(2 * t + lo // HALF, "picked_shf%d_%d" % (t, lo), shf_tables[t], lo, width)

        zs = {}

        def scale(t, half):
            span = slice(half * HALF, (half + 1) * HALF)
            cols = slice(t % 2 * P, (t % 2 + 1) * P)
            acc = psum.tile([P, HALF], F32, name="acc", tag="bank%d" % (PACK * half + t))
            nc.tensor.matmul_mx(
                out=acc[:],
                lhsT=weights[t // 2][0][:, cols].bitcast(FP8X4),
                lhsT_scale=weights[t // 2][1][:, cols],
                rhs=hidden[half][0][:].bitcast(FP8X4),
                rhs_scale=hidden[half][1][:],
                start=True,
                stop=True,
            )
            z = shared.tile([P, HALF], F32, name="z%d_%d" % (t, half), offset=Z_AT + (2 * t + half) * KIB)
            zs[t, half] = z
            if (t, half) == (2, 1):
                nc.vector.tensor_tensor(z[:, 0:P], acc[:, 0:P], picked_scl[t][:, HALF : S - P], MULT)
                nc.vector.tensor_tensor(z[:, P:HALF], acc[:, P:HALF], scl2_last[:], MULT)
            else:
                nc.vector.tensor_tensor(z[:], acc[:], scl3_halves[half][:] if t == 3 else picked_scl[t][:, span], MULT)

        res = [keep.tile([P, S], F32, name="res%d" % t, align_bytes=256) for t in range(PACK)]

        def add(t, lo, width, engine=nc.vector, fused=False):
            half, span = lo // HALF, slice(lo % HALF, lo % HALF + width)
            shifts = shf_tables[t][:].indirect(entries(lo, width)) if fused else picked_shf[t, half * HALF][:, span]
            engine.tensor_tensor(res[t][:, lo : lo + width], shifts, zs[t, half][:, span], ADD)

        def store(t, lo, width):
            span = slice(lo, lo + width)
            nc.sync.dma_start(out_rows[t][:, :, span], res[t][:, span])

        def shift(t, half, engine=nc.vector, fused=False):
            add(t, half * HALF, HALF, engine, fused)
            store(t, half * HALF, HALF)

        for half in range(2):
            scale(0, half)
            scale(1, half)
        scale(2, 0)
        scale(2, 1)
        scale(3, 0)
        add(0, 0, HALF, nc.gpsimd)
        add(0, HALF, HALF, nc.gpsimd)
        store(0, 0, S)
        shift(1, 0)
        shift(1, 1, fused=True)
        scale(3, 1)
        shift(2, 0)
        shift(2, 1)
        add(3, S - P, P, fused=True)
        store(3, S - P, P)
        shift(3, 0)
        add(3, HALF, P)
        store(3, HALF, P)
